import numpy as np, ml_dtypes
CORES = [16,17,18,19,32,33,34,35]
N = 8
BF = ml_dtypes.bfloat16
Q, W, ND, T, S, SH, KS, WM, DM = 192, 4096, 1024, 3, 3, 4, 53, 16, 4
def pick(a, i):
    return np.take_along_axis(a, i.reshape(N, 8, 1, -1), 3).reshape((N, 8, 16) + i.shape[2:])
def bf(a):
    return np.ascontiguousarray(a).astype(np.float32).astype(BF)
def limits(rng, X, lo, hi):
    s = np.sort(np.add.reduce(np.abs(pick(X, rng.integers(0, W, (N, 8, 512))) - pick(X, rng.integers(0, W, (N, 8, 512)))), axis=2), axis=2)
    return np.concatenate([np.take_along_axis(s, rng.choice(np.array(v), (N, 8, 1)), 2) for v in (lo, hi)], axis=2)
def parts(rng):
    top = rng.choice(np.array([64, 128, 256]), (1, 8, 1, 1)) - 1
    X = rng.integers(0, 256, (N, 8, 16, W)) & top; z = rng.integers(0, 256, (N, 8, 16, Q)) & top
    DL = rng.integers(0, 256, (N, 8, 16, ND)); L = rng.integers(0, 256, (N, 8, 16, Q)); R = rng.integers(0, 256, (N, 8, 16, Q))
    n = rng.integers(1, 5, (N, 8, Q)); kp = rng.integers(0, 256, (N, 8, 16, 1)); w = rng.integers(0, 256, (N, 8, 16, 1))
    return X, DL, L, R, z, n, kp, w, limits(rng, X, [10, 26, 51, 77], [410, 450, 480])
def pack(X, DL, L, R, z, n, kp, w, lm):
    return {"stock": bf(X.reshape(N, 128, W)), "donor": bf(DL.reshape(N, 128, ND)), "lend": bf(L.reshape(N, 128, Q)), "rend": bf(R.reshape(N, 128, Q)), "zed": bf(z.reshape(N, 128, Q)),
            "cnt": n.astype(np.int32), "kap": kp.reshape(N, 128, 1).astype(np.int32), "wt": w.reshape(N, 128, 1).astype(np.int32), "lim": lm.astype(np.int32)}
def setup_inputs(rng):
    return pack(*parts(rng))
def setup_inputs_spread(rng):
    def col(m): return (np.exp2(8 * rng.random((N, 8, 1, m))) * rng.random((N, 8, 16, m))).astype(np.int64)
    def few(m): return np.exp2(8 * rng.random((N, 8, 16, m))).astype(np.int64) - rng.integers(0, 2, (N, 8, 16, m))
    X, z = col(W), col(Q)
    return pack(X, few(ND), few(Q), few(Q), z, rng.choice(np.array([1, 1, 1, 2, 3, 4]), (N, 8, Q)), few(1), few(1), limits(rng, X, [1, 10, 40, 120, 300], [200, 400, 460, 490, 508]))
def ends(rng, m):
    k = rng.integers(0, 3, (N, 8, 1, m))
    return np.where(k == 2, 255 * rng.integers(0, 2, (N, 8, 16, m)), 255 * k)
def setup_inputs_ends(rng):
    X, DL, L, R, z = ends(rng, W), ends(rng, ND), ends(rng, Q), ends(rng, Q), ends(rng, Q)
    n = 1 + 3 * rng.integers(0, 2, (N, 8, Q)); kp = 255 * rng.integers(0, 2, (N, 8, 16, 1)); w = 255 * rng.integers(0, 2, (N, 8, 16, 1))
    kp[:, :, 3] = 0; kp[:, :, 15] = 255; w[:, :, 2] = 0; w[:, :, 5] = 255; w[:, 4] = 255
    n[:, :, 0] = 4; n[:, :, 1] = 1; n[:, :, Q - 2] = 1; n[:, :, Q - 1] = 4
    for g in (0, 6):
        w[:, g, 14] = 1; w[:, g, 15] = 16
        for i in (0, 3, Q - 1): z[:, g, :, i] = 0; z[:, g, 14, i] = 15; z[:, g, 15, i] = 255
    for i in (2, 5, Q - 1): z[:, 7, :, i] = 0; z[:, 5, :, i] = 0
    X[:, 7, :, 0] = 255; X[:, 5, :, 0] = 0
    for i in (1, 4, Q - 1): z[:, 4, :, i] = 255
    lm = 4080 * rng.integers(0, 2, (N, 8, 2))
    lm[:, 2, 0] = 0; lm[:, 3, 0] = 4080; lm[:, 0, 1] = 0; lm[:, 1, 1] = 4080; lm[:, 7, 1] = 4080; lm[N - 1, :, 0] = 4080
    return pack(X, DL, L, R, z, n, kp, w, lm)
def far(d):
    return np.minimum(np.maximum(d - 255 * np.arange(16), 0), 255)
def setup_inputs_corners(rng):
    X, DL, L, R, z, n, kp, w, lm = parts(rng); o = KS * np.arange(16); k = np.arange(16)[:, None]
    for q in range(N):
        for g in range(8):
            j = (g // 2 + q) % 4
            if g % 2 == 1 and j == 3: continue
            w[q, g] = 0; DL[q, g, :, 0] = 0
            if g % 2 == 0:
                b = (2, 5, 15, 16)[j]; s = int(rng.integers(20, 100)); v = int(rng.integers(20, 100))
                y = np.full((16, 16), 100); y[0, b:] += s
            else:
                b = 7; s, v = ((4080, 4079), (2049, 2048), (1, 0))[j]
                y = np.zeros((16, 16), np.int64); y[:, b:] = far(s)[:, None]
            for e in range(3):
                X[q, g][:, o + e] = y + far((0, v, v + 1)[e])[:, None] * np.where(y >= 128, -1, 1)
            sb = s if q == 1 else s - 1
            lm[q, g, 0] = v; lm[q, g, 1] = sb
            m = n[q, g]; f = np.where((b > m) & (sb < s), b, 16)
            c = rng.integers(0, 6, Q); p = np.choose(c, [m - 1, m, f - 1, f, 15 + 0 * m, 16 + 0 * m])
            late = np.where((c == 0) | (c == 3), 2, rng.integers(1, 3, (16, Q)))
            R[q, g] = np.where(k == p, 1, np.where(k < p, 2, late))
    return pack(X, DL, L, R, z, n, kp, w, lm)
def setup_inputs_crowd(rng):
    X, DL, L, R, z, n, kp, w, lm = parts(rng); o = KS * np.arange(16)
    lm[:, :, 0] = 4080; lm[4:, :, 0] = rng.choice(np.array([0, 4080]), (N - 4, 8))
    s = (3 - S) % N
    for v in (DL, L, R): v[s] = np.minimum(v[s], 253)
    def plant(q, g, who):
        w[q, g] = 0; DL[q, g, :, 0] = 0; X[q, g][:, o] = 0; X[q, g][:, o + 1] = 255
        R[q, g] = np.where(who, 0, 1); lm[q, g, 0] = rng.choice(np.array([0, 4079])); lm[q, g, 1] = rng.choice(np.array([0, 4080]))
    i = np.arange(Q)
    plant(0, 7, i >= 0); plant(1, 0, i < Q - 1)
    for g in range(8):
        plant(2, g, i < 0); plant(3, g, (i == 0) & (g == 7))
    DL[3, :, :, 1] = 255 - (np.arange(16) & 1); lm[3, :, 0] = 0; lm[3, ::2, 1] = 0
    return pack(X, DL, L, R, z, n, kp, w, lm)
def setup_inputs_ties(rng):
    X, DL, L, R, z, n, kp, w, lm = parts(rng)
    pal = np.repeat(rng.integers(0, 256, (1, 8, 16, 5)), N, axis=0)
    X = pick(pal, rng.integers(0, 5, (N, 8, W))); z = pick(pal, rng.integers(0, 5, (N, 8, Q)))
    kp = rng.choice(np.array([0, 1, 7, 128, 255]), kp.shape); few = np.array([0, 1, 3, 100, 254, 255])
    DL[:, ::2] = rng.choice(few, (N, 4, 16, ND)); R[:, 1::2] = rng.choice(few, (N, 4, 16, Q))
    return pack(X, DL, L, R, z, n, kp, w, limits(rng, X, [10, 51, 150, 256], [150, 256, 400, 480]))
def check_inputs(d):
    bad = []
    for k, lo, hi in (("stock", 0, 255), ("donor", 0, 255), ("lend", 0, 255), ("rend", 0, 255), ("zed", 0, 255), ("cnt", 1, 4), ("kap", 0, 255), ("wt", 0, 255), ("lim", 0, 4080)):
        v = np.asarray(d[k]).astype(np.float64)
        if not np.all((v >= lo) & (v <= hi)): bad.append("range of " + k)
        elif not np.all(v == np.floor(v)): bad.append("whole numbers of " + k)
    return bad
def reference(stock, donor, lend, rend, zed, cnt, kap, wt, lim):
    def whole(a, m): return np.asarray(a).astype(np.float32).astype(np.int64).reshape(N, 8, 16, m)
    X, DL, L, R, z = whole(stock, W), whole(donor, ND), whole(lend, Q), whole(rend, Q), whole(zed, Q)
    n = cnt.astype(np.int64); kp, w = whole(kap, 1), whole(wt, 1)
    th = lim[:, :, 0].astype(np.int64)[:, :, None, None]; sb = lim[:, :, 1].astype(np.int64)[:, :, None, None]
    k = np.arange(16)[:, None]; lane = np.arange(Q); A = np.zeros((N, 1, 1, 1), np.int64)
    for t in range(T):
        if t > 0: L, R, z, n = [np.roll(v, S, axis=0) for v in (L, R, z, n)]
        u = np.add.reduce(w * z, axis=2) & 4095
        ub = u[:, :, None]; nb = n[:, :, None]
        c = ((ub * ub >> SH) + kp * ub + A) & (W - 1)
        m = np.argmin(np.add.reduce(np.abs(pick(X, c) - z[:, :, :, None]), axis=2), axis=2)
        c = np.take_along_axis(c, m[:, :, None], 2)[:, :, 0]
        xc = pick(X, c); D = pick(DL, c & (ND - 1))
        y = pick(X, ((D * ub >> SH) + D + KS * k) & (W - 1))
        h = pick(X, ((R * ub >> SH) + R + KS * k) & (W - 1))
        jump = np.add.reduce(np.abs(y[:, :, :, 1:] - y[:, :, :, :-1]), axis=2)
        f = np.min(np.where((jump > sb) & (k[1:] > nb), k[1:], 16), axis=2); fb = f[:, :, None]
        meet = (np.add.reduce(np.abs(y - h), axis=2) <= th) & (k >= nb) & (k < fb)
        a = np.min(np.where(meet, k, 16), axis=2); ab = a[:, :, None]
        found = a < 16; e = np.where(found, a, f - 1)
        ye = np.take_along_axis(y, e[:, :, None, None], 3)[:, :, :, 0]
        L = np.where((k >= nb) & (k < fb), D, L); L = np.where(k >= ab, R, L)
        done = found | (f == 16)
        R = np.where(done[:, :, None], L, R); n = np.where(done, 1 + (u & 3), f)
        z = (z + ye) >> 1
        ix = np.broadcast_to((WM * lane + (u & (WM - 1)))[:, :, None], (N, 8, 16, Q)); np.put_along_axis(X, ix, (xc + ye) >> 1, 3)
        ix = np.broadcast_to((DM * lane + (u & (DM - 1)))[:, :, None], (N, 8, 16, Q))
        np.put_along_axis(DL, ix, np.where(done[:, :, None], L, np.take_along_axis(DL, ix, 3)), 3)
        A = np.add.reduce(found.astype(np.int64).reshape(N, -1), axis=1).reshape(N, 1, 1, 1)
    return {"yl": bf(L.reshape(N, 128, Q)), "yr": bf(R.reshape(N, 128, Q)), "yd": bf(DL.reshape(N, 128, ND)), "yx": bf(X.reshape(N, 128, W)), "yz": bf(z.reshape(N, 128, Q)), "yn": n.astype(np.float32)}

@@ -1,0 +1,668 @@
+from concourse.mybir import dt, AluOpType, AxisListType, ActivationFunctionType
+
+A = AluOpType
+F = ActivationFunctionType
+NV, SHIFT, NC, CL = 3, 3, 2, 96
+YENG = ["vss", "vvv"]
+HENG = ["sss", "vss"]
+LPE = [True, True]
+MAGIC = 12582912.0
+XO, ZO, NO, RO, LO, ZI, NI, RI, LI, RW = 0, 96, 192, 208, 304, 400, 496, 512, 608, 704
+
+SCRATCH = {}
+
+
+def _buf(name, cols, dtype, where="sbuf"):
+    SCRATCH[name] = (where, [128] + (cols if isinstance(cols, list) else [cols]), dtype)
+
+
+for _n, _c, _d in (
+        ("X", 4096, "bfloat16"), ("DL", 1792, "bfloat16"), ("Z0", 192, "bfloat16"), ("L0", 192, "bfloat16"),
+        ("WI", 1, "int32"), ("KI", 1, "int32"), ("CNI", 192, "int32"), ("LMI", 2, "int32"),
+        ("CNF", 192, "float32"), ("LMF", 2, "float32"), ("TH", 2, "float32"),
+        ("PI", 8, "int32"), ("PF", 24, "float32"), ("IC", 144, "bfloat16"), ("IB", 128, "bfloat16"),
+        ("ICO", 544, "bfloat16"), ("INN", 544, "bfloat16"), ("IPA", 34, "bfloat16"), ("KC", 96, "bfloat16"),
+        ("IS", 48, "float32"), ("Z8", 144, "float32"), ("E8", 128, "float32"),
+        ("ID", 128, "bfloat16"), ("NID", 128, "bfloat16"), ("ZS", 144, "bfloat16"), ("WB", 128, "bfloat16"),
+        ("BLK", 128, "bfloat16"), ("ONE", 128, "bfloat16"), ("CT", 288, "bfloat16"), ("HI", 128, "bfloat16"), ("NM", 96, "bfloat16"),
+        ("RS", 96, "float32"), ("D2", 192, "bfloat16"), ("DG", 16, "bfloat16"), ("KF", 16, "float32"),
+        ("DS", 16, "float32"), ("DK", 96, "float32"), ("KX", 96, "float32"), ("OF", 56, "float32"),
+        ("OFU", 56, "uint16"), ("QI", 8, "int32"), ("TAB", 592, "bfloat16"), ("EB", 16, "float32"),
+        ("CAP", 48, "float32"), ("NF", 16, "bfloat16"), ("AC", 1, "float32"), ("YN", 192, "float32")):
+    _buf(_n, _c, _d)
+for _c in range(NC):
+    for _n, _w, _d in (
+            ("CB", 32, "float32"), ("B", 56, "float32"), ("DE", 24, "float32"), ("FA", 768, "float32"),
+            ("IA", 512, "int32"), ("UW", 16, "int32"), ("OU", 384, "uint16"), ("BA", 1280, "bfloat16"),
+            ("D1", 1536, "bfloat16"), ("H", 1536, "bfloat16"), ("Y", 1552, "bfloat16"),
+            ("AB", [6, 256], "bfloat16"), ("AM", [6, 256], "bfloat16"), ("AJ", [6, 256], "bfloat16")):
+        _buf(_n + str(_c), _w, _d)
+    for _t in range(NV):
+        _buf("ST%d%d" % (_t, _c), RW, "bfloat16")
+for _b in range(8):
+    _buf("PS%d" % _b, 512, "float32", "psum")
+
+NSEM = {"v": 44, "s": 30, "p": 30, "g": 12}
+SEMAPHORES = [e + str(i) for e in NSEM for i in range(NSEM[e])] + ["ld%d" % i for i in range(12)] \
+    + ["ar%d" % i for i in range(8)] + ["sent", "st"]
+CY = 1.0
+M = dict(pcy=0.5, hop=70.0, ga=1.56, sc=3.8, rl=2500.0, rb=30.0)
+MODELS = [dict(M), dict(pcy=0.45, hop=120.0, ga=1.15, sc=2.5, rl=3500.0, rb=20.0),
+          dict(pcy=0.7, hop=50.0, ga=2.0, sc=5.0, rl=2000.0, rb=40.0)]
+ROUNDS = [2500, 1]
+FB = [1.0]
+_PLAN = {}
+
+
+def build(g, T, send):
+    ops = []
+    Q = {"v": g.vector, "s": g.scalar, "p": g.tensor, "g": g, "y": g.sync}
+
+    def a(n, lo=None, hi=None, st=1, p=None):
+        w = SCRATCH[n][1][1]
+        lo = 0 if lo is None else lo
+        hi = w if hi is None else hi
+        ap = T[n][0:(p or 128), lo:hi:st] if st > 1 else T[n][0:(p or 128), lo:hi]
+        return (ap, ((n, lo, hi),), len(range(lo, hi, st)), SCRATCH[n][2], None)
+
+    def ind(win, off):
+        return (win[0].indirect(off[0]), win[1] + off[1], 16 * off[2], win[3], "ind")
+
+    def a3(n, ap, lo, hi, cnt):
+        return (ap, ((n, lo, hi),), cnt, SCRATCH[n][2], None)
+
+    def rec(e, fns, rd, wr, cost, **kw):
+        r, w = [], []
+        for x in rd:
+            if isinstance(x, tuple):
+                r += list(x[1])
+        for x in wr:
+            w += list(x[1])
+        ops.append(dict(e=e, fns=fns, r=r, w=w, cost=cost, **kw))
+        return len(ops) - 1
+
+    def u(x):
+        return x[0] if isinstance(x, tuple) else x
+
+    def vc(out, ins, two=False):
+        if ins[0][4] == "ind":
+            return (60 + M["ga"] * out[2]) * CY
+        if out[4] == "ind":
+            return (60 + M["sc"] * out[2]) * CY
+        half = all(x[3] in ("bfloat16", "uint16") for x in [out] + ins)
+        return max(64, out[2] * (0.5 if half else 1) * (2 if two else 1)) * CY
+
+    def ts(out, i, s1, o0, s2=None, o1=None):
+        if o1 is None:
+            f = lambda q: q.tensor_scalar(out[0], i[0], u(s1), None, o0)
+        else:
+            f = lambda q: q.tensor_scalar(out[0], i[0], u(s1), u(s2), o0, o1)
+        rec("v", [f], [i, s1, s2], [out], vc(out, [i]))
+
+    def tt(out, i0, i1, op):
+        sb = not (i0[1][0][0].startswith("PS") or i1[1][0][0].startswith("PS"))
+        rec("v", [lambda q: q.tensor_tensor(out[0], i0[0], i1[0], op)], [i0, i1], [out], vc(out, [i0, i1], sb))
+
+    def cp(out, i):
+        w = (out[0], out[1][:1]) if out[4] else out
+        rd = [i] + ([(0, out[1][1:])] if out[4] else [])
+        rec("v", [lambda q: q.tensor_copy(out[0], i[0])], rd, [w], vc(out, [i]))
+
+    def ms(out, val):
+        rec("v", [lambda q: q.memset(out[0], val)], [], [out], vc(out, [out]))
+
+    def scan(out, d0, d1, o0, o1):
+        rec("v", [lambda q: q.tensor_tensor_scan(out[0], d0[0], d1[0], 0.0, o0, o1)], [d0, d1], [out], vc(out, [d0, d1]))
+
+    def act(out, i, fn=F.Identity, scale=1.0, bias=0.0):
+        c = (78 + M["ga"] * out[2]) * CY if i[4] else max(64, out[2] + 30) * CY
+        rec("s", [lambda q: q.activation(out[0], i[0], fn, bias=u(bias), scale=scale)], [i, bias], [out], c)
+
+    def mm(out, pairs):
+        k = len(pairs)
+        fns = [(lambda q, j=j: q.matmul(out[0], pairs[j][0][0], pairs[j][1][0], j == 0, j == k - 1)) for j in range(k)]
+        c = sum(max(64, r[2]) * (4 if r[3] == "float32" else 1) for l, r in pairs) * M["pcy"] + 60
+        rec("p", fns, [x for pr in pairs for x in pr], [out], c)
+
+    def iota(out, pat, base=0, cm=0):
+        if out[3] == "int32":
+            f = lambda q: q.iota(out[0], pat, base, cm)
+        else:
+            f = lambda q: q.iota(out[0], pat, base, cm, allow_small_or_imprecise_dtypes=True)
+        rec("g", [f], [], [out], 130 + 2 * out[2] * CY)
+
+    nld = [0]
+
+    def load(e, out, src, ns):
+        rec(e, [lambda q: q.dma_start(out[0], src)], [], [out], 60, lat=ns, sem=("ld%d" % nld[0], 16), dma=1)
+        nld[0] += 1
+
+    def store(dst, i):
+        rec("y", [lambda q: q.dma_start(dst, i[0])], [i], [], 60 + 128 * 2 * i[2] / 150.0, lat=2000, store=1)
+
+    def gather(e, out, i, scale=0.5):
+        ts(out, i, scale, A.mult)
+        act(out, i, scale=scale)
+        os_, ov = ops.pop(), ops[-1]
+        ov["alt"] = {"v": (ov["fns"], ov["cost"]), "s": (os_["fns"], os_["cost"])}
+        put(ops, len(ops) - 1, e)
+
+    load("y", a("Z0"), T.zed[:], 2200)
+    load("s", a("WI"), T.wt[:], 2200)
+    load("s", a("KI"), T.kap[:], 2300)
+    load("y", a("X"), T.stock[:], 7500)
+    for c in range(NC):
+        load("s", a("ST0%d" % c, RI, RI + CL), T.rend[:, CL * c:CL * c + CL], 2500)
+    load("s", a("CNI", p=8), T.cnt[:], 2600)
+    load("s", a("LMI", p=8), T.lim[:], 2600)
+    load("y", a("DL", 384, 1408), T.donor[:], 9000)
+    load("y", a("L0"), T.lend[:], 9500)
+    iota(a("PI", 0, 1), [[0, 1]], 0, 1)
+    iota(a("IB"), [[16, 8], [0, 16]])
+    iota(a("KC"), [[0, 6], [1, 16]])
+    iota(a("IC"), [[1, 144]])
+    iota(a("IS", 0, 8), [[1, 8]])
+    iota(a("IS", 8, 14), [[4, 6]])
+    iota(a("IS", 16, 40), [[16, 6], [0, 4]])
+    iota(a("Z8", p=8), [[1, 144]], -15, -16)
+    iota(a("E8", p=8), [[16, 8], [0, 16]], 0, -16)
+    iota(a("ICO"), [[0, 16], [1, 34]])
+    iota(a("INN"), [[1, 16], [0, 34]])
+    iota(a("IPA"), [[0, 17], [1, 2]])
+    p0 = a("PI", 0, 1)
+    ts(a("PI", 1, 2), p0, 15, A.bitwise_and)
+    ts(a("PI", 2, 3), p0, 112, A.bitwise_and)
+    ts(a("PI", 3, 4), p0, 15, A.bitwise_and, 2, A.logical_shift_right)
+    ts(a("PI", 4, 5), p0, 3, A.bitwise_and)
+    ts(a("PI", 5, 6), p0, 7, A.bitwise_and)
+    cp(a("PF", 0, 6), a("PI", 0, 6))
+    col = lambda j: a("PF", j, j + 1)
+    PP, PB, G16, PQ, P3, P7, WF, KP, CU, CYY, P16, K53, K2, K1, K15, QB = [col(j) for j in range(16)]
+    ts(WF, a("WI"), 1.0 / 16, A.mult)
+    cp(KP, a("KI"))
+    ts(a("WB"), a("IB"), G16, A.is_equal, WF, A.mult)
+    ts(a("ID"), a("IC", 0, 128), PP, A.is_equal, 8192.0, A.mult)
+    ts(a("NM"), a("KC"), PB, A.not_equal, -16.0, A.mult)
+    ms(a("ONE"), 1.0)
+    ms(a("CT", 0, 96, p=64), -4.0)
+    rec("v", [lambda q: q.memset(T.CT[32:64, 0:96], 1.0 / 1024)], [], [a("CT", 0, 96)], 64 * CY)
+    ms(a("CT", 96, 192, p=64), 1.0 / 64)
+    ms(a("RS"), 1.0)
+    ms(a("RS", 0, 96, 16), 0.0)
+    ts(a("BLK"), a("IB"), G16, A.is_equal)
+    ts(a("DG"), a("KC", 0, 16), PB, A.is_equal, KP, A.mult)
+    mm(a("PS0", 0, 16), [(a("BLK"), a("DG"))])
+    cp(a("KF"), a("PS0", 0, 16))
+    ts(P7, P7, 5.0, A.min)
+    ts(CU, P7, 16.0, A.mult, 15.0, A.add)
+    ts(CYY, P7, 32.0, A.mult, 31.0, A.add)
+    ts(P16, PB, 16.0, A.mult)
+    ts(K53, PB, 53.0, A.mult, -15.0 / 32, A.add)
+    ts(K2, PB, 2.0, A.mult, 2.0, A.add)
+    ts(K1, PB, 2.0, A.mult, 1.0, A.add)
+    ms(a("CT", 192, 288, p=64), -1.0 / 256)
+    ts(a("HI"), a("ID"), 1.0 / 16384, A.mult)
+    ts(a("OF", 0, 6), a("IS", 0, 6), 0.0, A.mult, PB, A.add)
+    ts(a("IS", 40, 46), a("IS", 8, 14), PQ, A.add)
+    ts(a("QI", 0, 6), a("IS", 40, 46), -2.5, A.add, 1.0 / 6, A.mult)
+    ts(a("OF", 6, 12), a("QI", 0, 6), 4.0, A.mult, P3, A.add)
+    ts(a("OF", 12, 18), a("QI", 0, 6), -6.0, A.mult)
+    tt(a("OF", 12, 18), a("OF", 12, 18), a("IS", 40, 46), A.add)
+    ts(a("OF", 18, 42), a("IS", 16, 40), PB, A.add)
+    cp(a("OF", 42, 48), a("IS", 0, 6))
+    ts(a("OF", 48, 52), a("IS", 0, 4), 0.0, A.mult, CU, A.add)
+    ts(a("OF", 52, 56), a("IS", 0, 4), 0.0, A.mult, CYY, A.add)
+    cp(a("OFU"), a("OF"))
+    OPB, OK, OA, OZ, ON, OUU, OY = [a("OFU", x, y) for x, y in ((0, 6), (6, 12), (12, 18), (18, 42), (42, 48), (48, 51), (52, 55))]
+    act(a("KX"), ind(a("KF"), OK))
+    ms(a("DS", 0, 1), 33554432.0)
+    tt(a("DS", 1, 16), a("KF", 0, 15), a("KF", 1, 16), A.subtract)
+    ts(a("DS", 1, 16), a("DS", 1, 16), -256.0, A.add)
+    act(a("DK"), ind(a("DS"), OPB))
+    ts(K15, a("KF", 15, 16), 3840.0, A.add)
+    ts(a("ZS"), a("IC"), G16, A.subtract, 15.0, A.is_equal)
+    ts(a("NID"), a("ID"), -1.0, A.mult)
+    EB = a("EB", 0, 8)
+    ts(EB, a("IS", 0, 8), 256.0, A.mult, P16, A.add)
+    ts(a("EB", 8, 16), EB, 2.0, A.mult, 30.0, A.add)
+    for c in range(NC):
+        s = str(c)
+        cp(a("CB" + s, 0, 8), EB)
+        cp(a("CB" + s, 8, 16), EB)
+        ms(a("CB" + s, 16, 24), 1.0)
+        ts(a("CB" + s, 24, 32), EB, 0.25, A.mult, 384.0 if c == 0 else 0.0, A.add)
+        ts(a("B" + s, 32, 40), EB, 1.0 / 16, A.mult)
+        ms(a("B" + s, 48, 56), 575.0)
+        ms(a("DE" + s, 0, 8), 0.0)
+        ms(a("DE" + s, 8, 16), -384.0 if c == 0 else 640.0)
+        ms(a("DE" + s, 16, 24), float(RI - LO))
+        ms(a("Y" + s, 0, 16), 0.0)
+        ms(a("BA" + s, 0, 16), 0.0)
+        ms(a("ST0" + s, ZI, RI), 0.0)
+        for t in range(1, NV):
+            ms(a("ST%d%d" % (t, c), NI + 8, RI), 0.0)
+    ms(a("CAP"), 100.0)
+    ms(a("CAP", 8, 32), 0.0)
+    ms(a("D2"), -1.0)
+    ms(a("D2", 1, 192, 32), 1024.0)
+    ms(a("NF", 12, 13), -12.0)
+    ms(a("NF", 13, 14), 1.0 / 512)
+    ms(a("DL", 0, 384), 0.0)
+    ms(a("DL", 1408, 1792), 0.0)
+    ts(a("Z8", p=8), a("Z8", p=8), 0.0, A.is_equal)
+    ts(a("E8", p=8), a("E8", p=8), 0.0, A.is_equal)
+    cp(a("CNF", p=8), a("CNI", p=8))
+    cp(a("LMF", p=8), a("LMI", p=8))
+    mm(a("PS1", 0, 12), [(a("Z8", 15 - b, 143 - b, p=8), a("CNF", b, 192, 16, p=8)) for b in range(16)])
+    mm(a("PS2", 0, 2), [(a("E8", p=8), a("LMF", p=8))])
+    for c in range(NC):
+        act(a("ST0%d" % c, NI, NI + 6), a("PS1", 6 * c, 6 * c + 6))
+    act(a("TH"), a("PS2", 0, 2))
+    ts(a("TAB", 544, 578), a("ICO", 0, 34), K1, A.is_le)
+    tt(a("TAB", 544, 578), a("TAB", 544, 578), a("IPA"), A.mult)
+    ts(a("ICO"), a("ICO"), K2, A.is_ge)
+    ts(a("INN"), a("INN"), PB, A.is_le)
+    tt(a("TAB", 0, 544), a("ICO"), a("INN"), A.mult)
+    store(T.yx[:, 3072:4096], a("X", 3072, 4096))
+    rec("y", [lambda q: q.dma_start(T.yd[:, 768:1024], T.donor[:, 768:1024])], [a("L0")], [], 60, lat=2500, store=1)
+
+    XW, DW, TW = a("X"), a("DL", 384, 1408), a("TAB", 0, 578)
+    sel = [a("ZS", 15 - b, 143 - b) for b in range(16)]
+    ID, NID = a("ID"), a("NID")
+
+    def first(t, c):
+        s = str(c)
+        R = "ST%d%d" % (t, c)
+        z = a("Z0", CL * c, CL * c + CL) if t == 0 else a(R, ZI, ZI + CL)
+        PS, FA, IA, UW, OU, BA, B = "PS%d" % (6 + c), "FA" + s, "IA" + s, "UW" + s, "OU" + s, "BA" + s, "B" + s
+        one = a("ONE", p=64)
+        mm(a(PS, 192, 288), [(ID, a("NM")), (a("WB"), z)])
+        mm(a(PS, 0, 96), [(one, a("CT", 0, 96, p=64)), (a("WB"), z)])
+        mm(a(PS, 96, 192), [(one, a("CT", 96, 192, p=64)), (a("WB"), z)])
+        gather("s", a(BA, 128, 512), ind(z, OZ), 1.0)
+        scan(a(FA, 0, 96), a("RS"), a(PS, 192, 288), A.mult, A.max)
+        ts(a(IA, 0, 48), ind(a(FA, 0, 96), OUU), 16.0, A.mult)
+        uu, ba = a(UW, 0, 8), a(UW, 8, 16)
+        ts(uu, a(IA, 0, 8), 4095, A.bitwise_and)
+        tt(a(FA, 96, 104), uu, uu, A.mult)
+        tt(a(FA, 128, 224), ind(uu, OA), a("KX"), A.mult)
+        ts(ba, a(FA, 96, 104), 1.0 / 16, A.mult, -0.25 if t == 0 else a("AC"), A.add)
+        tt(a(IA, 64, 160), ind(ba, OA), a(FA, 128, 224), A.add)
+        ts(a(IA, 64, 160), a(IA, 64, 160), 4095, A.bitwise_and)
+        cp(a(OU, 0, 96), a(IA, 64, 160))
+        ts(a(FA, 224, 320), a(PS, 0, 96), 3221225472.0, A.add, 3221225472.0, A.subtract)
+        v = a(FA, 320, 416)
+        tt(v, a(PS, 96, 192), a(FA, 224, 320), A.subtract)
+        tt(a(FA, 224, 320), a(R, RI, RI + CL), v, A.mult)
+        ts(a(IA, 160, 256), a(FA, 224, 320), K53, A.add)
+        ts(a(IA, 160, 256), a(IA, 160, 256), 4095, A.bitwise_and)
+        cp(a(OU, 96, 192), a(IA, 160, 256))
+        for m in range(4):
+            d = a("D1" + s, 384 * m, 384 * m + 384)
+            tt(d, ind(XW, a(OU, 24 * m, 24 * m + 24)), a(BA, 128, 512), A.subtract)
+            act(a3("AB" + s, T["AB" + s][:, :, 64 * m:64 * m + 64], m, m + 1, 384), d, F.Abs, 4096.0)
+        for i in range(3):
+            gather(HENG[c][i], a("H" + s, 512 * i, 512 * i + 512), ind(XW, a(OU, 96 + 32 * i, 128 + 32 * i)))
+        mm(a(PS, 288, 384), [(sel[b], a3("AB" + s, T["AB" + s][:, :, b:256:16], 0, 4, 96)) for b in range(16)])
+        scan(a(FA, 0, 96), a("DK"), a(PS, 288, 384), A.add, A.min)
+        k = a(IA, 48, 54)
+        ts(k, a(FA, 15, 96, 16), K15, A.add)
+        ts(k, k, 255, A.bitwise_and)
+        tt(k, k, a(UW, 0, 6), A.mult)
+        tt(k, k, a(UW, 8, 14), A.add)
+        ts(a(IA, 256, 262), k, 1023, A.bitwise_and)
+        ts(a(IA, 262, 268), k, 4095, A.bitwise_and)
+        cp(a(OU, 288, 300), a(IA, 256, 268))
+        od, oc = a(OU, 288, 294), a(OU, 294, 300)
+        tt(a(FA, 128, 224), ind(DW, od), v, A.mult)
+        ts(a(IA, 64, 160), a(FA, 128, 224), K53, A.add)
+        ts(a(IA, 64, 160), a(IA, 64, 160), 4095, A.bitwise_and)
+        cp(a(OU, 192, 288), a(IA, 64, 160))
+        for i in range(3):
+            gather(YENG[c][i], a("Y" + s, 16 + 512 * i, 528 + 512 * i), ind(XW, a(OU, 192 + 32 * i, 224 + 32 * i)))
+        gather("s", a(BA, 512, 608), ind(DW, od), 1.0)
+        gather("s", a(BA, 1184, 1280), ind(XW, oc), 1.0)
+        ts(a(IA, 8, 16), a(IA, 8, 16), 15, A.bitwise_and)
+        ts(a(IA, 16, 40), a(IA, 16, 40), 3, A.bitwise_and)
+        tt(a(B, 0, 32), a(IA, 8, 40), a("CB" + s), A.add)
+        cp(a(OU, 336, 344), a(B, 0, 8))
+        ts(a(B, 40, 48), a(R, NI, NI + 8), 34.0, A.mult, 31.0, A.add)
+        tt(a(BA, 16, 112), ind(a(R, NI, NI + 8), ON), a("KC"), A.is_gt)
+        L = a("L0", CL * c, CL * c + CL) if t == 0 else a(R, LI, LI + CL)
+        tt(a(BA, 608, 704), a(BA, 512, 608), L, A.subtract)
+        tt(a(BA, 704, 800), a(R, RI, RI + CL), L, A.subtract)
+
+    def second(t, c):
+        s = str(c)
+        R = "ST%d%d" % (t, c)
+        PS, FA, IA, OU, BA, B, Y = "PS%d" % (6 + c), "FA" + s, "IA" + s, "OU" + s, "BA" + s, "B" + s, "Y" + s
+        L = a("L0", CL * c, CL * c + CL) if t == 0 else a(R, LI, LI + CL)
+        for i in range(3):
+            y = a(Y, 16 + 512 * i, 528 + 512 * i)
+            for j, (nm, o) in enumerate((("AJ" + s, a(Y, 15 + 512 * i, 527 + 512 * i)), ("AM" + s, a("H" + s, 512 * i, 512 * i + 512)))):
+                d = a("PS%d" % (3 * c + i))
+                mm(d, [(ID, y), (NID, o)])
+                act(a3(nm, T[nm][:, 2 * i:2 * i + 2, :], i, i + 1, 512), d, F.Abs, 1.0 / 4096)
+        for nm, lo, w, pen in (("AJ" + s, 0, NID, a(BA, 15, 111)), ("AM" + s, 96, ID, a(BA, 16, 112))):
+            mm(a(PS, lo, lo + 96), [(w, pen)] + [(sel[b], a3(nm, T[nm][:, :, 16 * b:16 * b + 16], 0, 3, 96)) for b in range(16)])
+        ts(a(BA, 800, 992, 2), a(PS, 0, 96), a("TH", 1, 2), A.is_le, 31.0, A.mult)
+        ts(a(BA, 801, 992, 2), a(PS, 96, 192), a("TH", 0, 1), A.is_gt, 31.0, A.mult)
+        sc = a(BA, 992, 1184)
+        scan(sc, a("D2"), a(BA, 800, 992), A.add, A.min)
+        e = a(IA, 272, 278)
+        tt(e, a(BA, 992 + 31, 1184, 32), a("EB", 8, 14), A.add)
+        ts(e, e, 1, A.arith_shift_right)
+        oe = a(OU, 344, 350)
+        cp(oe, e)
+        yw = a(Y, 16, 1552)
+        ye, pz, HI = a(BA, 320, 416), "PS%d" % (3 * c), a("HI")
+        z = a("Z0", CL * c, CL * c + CL) if t == 0 else a(R, ZI, ZI + CL)
+        gather("s", ye, ind(yw, oe), 2.0)
+        for lo, o in ((0, a(BA, 1184, 1280)), (96, z)):
+            mm(a(pz, lo, lo + 96), [(a("ONE", p=64), a("CT", 192, 288, p=64)), (HI, o), (HI, ye)])
+        ts(a(R, XO, ZO + CL), a(pz, 0, 192), MAGIC, A.add, MAGIC, A.subtract)
+        tt(a(IA, 288, 336), ind(sc, OY), a("CAP"), A.min)
+        ts(a(IA, 336, 368), a(IA, 288, 320), 1, A.bitwise_and)
+        tt(a("DE" + s, 0, 6), e, a(B, 8, 14), A.subtract)
+        tt(a(IA, 296, 320), a(IA, 344, 368), a("DE" + s), A.mult)
+        tt(a(FA, 704, 744), a(IA, 296, 336), a(B, 16, 56), A.add)
+        cp(a(OU, 352, 384), a(FA, 712, 744))
+        gather("s", a(R, NO, NO + 8), a(FA, 704, 712), 1.0)
+        if t < NV - 1:
+            cp(a("NF", 6 * c, 6 * c + 6), a(IA, 336, 342))
+            send(rec, a(R, ZO, NO + 8), a("ST%d%d" % (t + 1, c), ZI, NI + 8), 4 * t + 2 * c)
+            if c == NC - 1:
+                mm(a(PS, 496, 510), [(a("ONE"), a("NF", 0, 14))])
+                rec("v", [lambda q: q.tensor_reduce(T.AC[:], T[PS][:, 496:510], AxisListType.X, A.add, negate=True)],
+                    [a(PS, 496, 510)], [a("AC")], 64 * CY)
+        else:
+            store(T.yz[:, CL * c:CL * c + CL], a(R, ZO, ZO + CL))
+            nn = a(R, NO, NO + 6)
+            fns = [(lambda q, b=b: q.matmul(T[PS][0:8, 400 + b:496:16], T.ID[:, b:128:16], nn[0], True, True)) for b in range(16)]
+            rec("p", fns, [ID, nn], [a(PS, 400, 496)], 16 * 64 * M["pcy"], each=1)
+            act(a("YN", CL * c, CL * c + CL, p=8), a(PS, 400, 496, p=8), scale=1.0 / 8192)
+            if c == NC - 1:
+                store(T.yn[:], a("YN", p=8))
+        tt(a(BA, 128, 224), ind(TW, a(OU, 368, 374)), a(BA, 608, 704), A.mult)
+        tt(a(BA, 224, 320), ind(TW, a(OU, 376, 382)), a(BA, 704, 800), A.mult)
+        if LPE[c]:
+            pl = a("PS%d" % (3 * c + 1), 0, 96)
+            mm(pl, [(HI, L), (HI, a(BA, 128, 224)), (HI, a(BA, 224, 320))])
+            act(a(R, LO, LO + CL), pl, scale=2.0)
+        else:
+            tt(a(BA, 128, 224), a(BA, 128, 224), L, A.add)
+            tt(a(R, LO, LO + CL), a(BA, 128, 224), a(BA, 224, 320), A.add)
+        gather("s", a(R, RO, RO + CL), ind(a(R, LO, RI + CL), a(OU, 360, 366)), 1.0)
+        if t < NV - 1:
+            send(rec, a(R, RO, LO + CL), a("ST%d%d" % (t + 1, c), RI, LI + CL), 4 * t + 2 * c + 1)
+        else:
+            store(T.yl[:, CL * c:CL * c + CL], a(R, LO, LO + CL))
+            store(T.yr[:, CL * c:CL * c + CL], a(R, RO, RO + CL))
+
+    def writes(t, c):
+        s = str(c)
+        R = "ST%d%d" % (t, c)
+        xw = a("X", 1536 * c, 1536 * c + 1536)
+        cp(ind(xw, a("OU" + s, 336, 342)), a(R, XO, XO + CL))
+        dw = a("DL", 0, 768) if c == 0 else a("DL", 768, 1792)
+        cp(ind(dw, a("OU" + s, 352, 358)), a(R, LO, LO + CL))
+        if t == NV - 1:
+            store(T.yx[:, 1536 * c:1536 * c + 1536], xw)
+            store(T.yd[:, 384 * c:384 * c + 384], a("DL", 384 + 384 * c, 768 + 384 * c))
+
+    def part(f, t, c):
+        k = len(ops)
+        f(t, c)
+        for j in range(k, len(ops)):
+            ops[j]["key"] = (f is not first, c, j - k + (100 if f is writes else 0), t)
+
+    for t in range(NV):
+        for c in range(NC):
+            part(first, t, c)
+        for c in range(NC):
+            part(second, t, c)
+            part(writes, t, c)
+    return ops
+
+
+def depend(ops):
+    acc = {}
+    deps = []
+    for i, o in enumerate(ops):
+        d = set(o.get("after", ()))
+        for kind, lst in ((0, o["r"]), (1, o["w"])):
+            for n, lo, hi in lst:
+                for j, k2, l2, h2 in acc.get(n, ()):
+                    if j == i:
+                        continue
+                    if (kind or k2) and lo < h2 and l2 < hi:
+                        d.add(j)
+                    elif n.startswith("PS") and ops[j]["e"] != o["e"]:
+                        d.add(j)
+        for kind, lst in ((0, o["r"]), (1, o["w"])):
+            for n, lo, hi in lst:
+                acc.setdefault(n, []).append((i, kind, lo, hi))
+        deps.append(d)
+    anc = []
+    for i, d in enumerate(deps):
+        m, keep = 0, set()
+        for j in sorted(d, reverse=True):
+            if not m >> j & 1:
+                keep.add(j)
+                m |= anc[j]
+        anc.append(1 << i if ops[i]["e"] == "net" else m | 1 << i)
+        deps[i] = keep
+    return deps
+
+
+def place(ops, before, seq, hop, back):
+    busy = {}
+    end = [0.0] * len(ops)
+    st = [0.0] * len(ops)
+    for i in seq:
+        o = ops[i]
+        c, lat = o["cost"], o.get("lat", 0)
+        t = 0.0
+        for j in before[i]:
+            if end[j] + hop > t:
+                t = end[j] + hop
+        if back:
+            t += lat
+        if o["e"] != "net":
+            iv = busy.setdefault(o["e"], [])
+            lo, hi = 0, len(iv)
+            while lo < hi:
+                mid = (lo + hi) // 2
+                if iv[mid][1] <= t:
+                    lo = mid + 1
+                else:
+                    hi = mid
+            while lo < len(iv) and iv[lo][0] < t + c:
+                t = max(t, iv[lo][1])
+                lo += 1
+            iv.insert(lo, (t, t + c))
+        st[i] = t
+        end[i] = t + c + (0 if back else lat)
+    return st, end
+
+
+def in_order(before, users, key):
+    left = [len(b) for b in before]
+    ready = sorted(((key[i], i) for i in range(len(before)) if not left[i]), reverse=True)
+    seq = []
+    while ready:
+        i = ready.pop()[1]
+        seq.append(i)
+        new = False
+        for k in users[i]:
+            left[k] -= 1
+            if not left[k]:
+                ready.append((key[k], k))
+                new = True
+        if new:
+            ready.sort(reverse=True)
+    return seq
+
+
+def replay(ops, deps, order, hop):
+    free, fin = {}, [0.0] * len(ops)
+    for i in order:
+        o = ops[i]
+        t = free.get(o["e"], 0.0)
+        for j in deps[i]:
+            if fin[j] + hop > t:
+                t = fin[j] + hop
+        if o["e"] != "net":
+            free[o["e"]] = t + o["cost"]
+        fin[i] = t + o["cost"] + o.get("lat", 0)
+    return fin
+
+
+GUESS = {(0, 0): ((9, -3), (13, 0), (19, -2.5), (27, 0.5), (30, 0.6), (43, 3), (46, 6), (99, 8)),
+         (0, 1): ((19, 3.3), (27, 5), (30, 9.5), (43, 8), (46, 11), (99, 12)),
+         (1, 0): ((14, 7), (200, 10)), (1, 1): ((14, 12), (200, 16))}
+
+
+def guess(o, i):
+    if "key" not in o:
+        return -1e6 + i
+    ph, c, j, t = o["key"]
+    return 1000.0 * (22 * t + [v for lim, v in GUESS[(int(ph), c)] if j < lim][0]) + j
+
+
+def put(ops, i, e):
+    ops[i]["e"] = e
+    ops[i]["fns"], ops[i]["cost"] = ops[i]["alt"][e]
+
+
+def plan(all_ops, deps, rounds, seed, start=None):
+    ops, hop = all_ops[0]
+    n = len(ops)
+    users = [[] for _ in ops]
+    for i in range(n):
+        for j in deps[i]:
+            users[j].append(i)
+    flex = [i for i in range(n) if "alt" in ops[i]]
+    x = [seed]
+
+    def rnd():
+        x[0] = (x[0] * 1103515245 + 12345) % 2147483648
+        return x[0] / 2147483648.0
+
+    def forward(key):
+        key = [-1e9 + i if ops[i].get("dma") else key[i] for i in range(n)]
+        return place(ops, deps, in_order(deps, users, key), hop, False)
+
+    def score(st):
+        order = in_order(deps, users, st)
+        r = [max(replay(o, deps, order, h)) for o, h in all_ops]
+        return r[0] + sum(r), order, r, [ops[i]["e"] for i in flex], st
+
+    def flip(i):
+        e = "s" if ops[i]["e"] == "v" else "v"
+        for o, h in all_ops:
+            put(o, i, e)
+
+    st, end = forward(start or [float(i) for i in range(n)])
+    best = score(st)
+    cur, cs = st, best[0]
+    for r in range(rounds):
+        key = list(cur)
+        fl = []
+        if r:
+            a = rnd() * max(key)
+            w, amp = 2000 + 5000 * rnd(), 500 + 5000 * rnd() ** 2
+            key = [k + amp * (rnd() - 0.5) if a <= k <= a + w else k for k in key]
+            if rnd() < 0.3:
+                fl = [i for i in flex if a <= cur[i] <= a + w and rnd() < 0.25]
+        for i in fl:
+            flip(i)
+        st, end = forward(key)
+        for _ in range(1 if rnd() < FB[0] else 0):
+            bs, be = place(ops, users, in_order(users, deps, [-e for e in end]), hop, True)
+            st, end = forward([-e for e in be])
+        s = score(st)
+        if s[0] <= cs + 300:
+            cur, cs = st, s[0]
+        else:
+            for i in fl:
+                flip(i)
+        if s[0] < best[0]:
+            best = s
+    return deps, best[1], dict(zip(flex, best[3])), best[2], best[4]
+
+
+def rank_program(g, core, T, topo):
+    rank = T.rank_of(core)
+    if rank is None:
+        return
+    n = len(T.cores)
+    dst, src = T.cores[(rank + SHIFT) % n], T.cores[(rank - SHIFT) % n]
+    rid, pid = topo.addr(dst)[:2]
+    mask, n_out, n_in = topo.mask(core, dst), len(topo.engines(core, dst)), len(topo.engines(src, core))
+    sent = [0]
+
+    def send(rec, i, out, k):
+        sent[0] += n_out
+        j = rec("g", [lambda q: q.remote_dma(out[0], i[0], T.sem["ar%d" % k], T.sem.sent, pid, rid, mask)], [i], [], 300, remote=1)
+        rec("net", [], [], [out], 0, lat=M["rl"] + 128 * 2 * i[2] / M["rb"], after=[j], sem=("ar%d" % k, n_in))
+
+    ops = build(g, T, send)
+    if not _PLAN:
+        all_ops, mine = [], sent[0]
+        for m in MODELS:
+            M.update(m)
+            all_ops.append((build(g, T, send), m["hop"]))
+        sent[0] = mine
+        _PLAN["o"] = all_ops
+        _PLAN["p"] = plan(all_ops, depend(ops), ROUNDS[0], ROUNDS[1], [guess(o, i) for i, o in enumerate(ops)])
+    deps, order, eng = _PLAN["p"][:3]
+    for i in eng:
+        put(ops, i, eng[i])
+    Q = {"v": g.vector, "s": g.scalar, "p": g.tensor, "g": g, "y": g.sync}
+    pos = {i: k for k, i in enumerate(order)}
+    need = set()
+    for final in (False, True):
+        known = {e: 0 for e in Q}
+        clos, sig, last, cnt, val, waited = {}, {}, {}, {e: 0 for e in Q}, {}, {}
+        stores = 0
+        for i in order:
+            o = ops[i]
+            e = o["e"]
+            if e == "net":
+                clos[i], sig[i] = 1 << i, o["sem"]
+                val[o["sem"][0]] = o["sem"][1]
+                continue
+            want = sorted(deps[i], key=lambda j: -pos[j])
+            if "sem" in o:
+                sig[i] = o["sem"]
+            elif final and i in need:
+                s = e + str(cnt[e] % NSEM[e])
+                cnt[e] += 1
+                if s in last:
+                    want.append(last[s])
+                last[s] = i
+                sig[i] = (s, val.get(s, 0) + (len(o["fns"]) if o.get("each") else 1))
+            for j in want:
+                if not known[e] >> j & 1:
+                    need.add(j)
+                    known[e] |= clos[j]
+                    if final:
+                        Q[e].wait_ge(T.sem[sig[j][0]], sig[j][1])
+                        waited[sig[j][0]] = max(waited.get(sig[j][0], 0), sig[j][1])
+            clos[i] = known[e] | 1 << i
+            if i in sig:
+                val[sig[i][0]] = sig[i][1]
+            if final:
+                for k, f in enumerate(o["fns"]):
+                    ins = f(Q[e])
+                    if o.get("store"):
+                        ins.then_inc(T.sem.st, 16)
+                        stores += 16
+                    elif i in sig and (o.get("each") or k == len(o["fns"]) - 1):
+                        ins.then_inc(T.sem[sig[i][0]], 16 if o.get("dma") else 1)
+    for s in val:
+        if waited.get(s, 0) < val[s]:
+            g.wait_ge(T.sem[s], val[s])
+    g.wait_ge(T.sem.sent, sent[0])
+    g.sync.wait_ge(T.sem.st, stores)

@@ -3,9 +3,14 @@ from concourse.mybir import dt, AluOpType, AxisListType, ActivationFunctionType
 A = AluOpType
 F = ActivationFunctionType
 NV, SHIFT, NC, CL = 3, 3, 2, 96
-YENG = ["vss", "vvv"]
-HENG = ["sss", "vss"]
-LPE = [True, True]
+YENG = ["sss", "sss"]
+HENG = ["sss", "sss"]
+LPE = [False, False]
+ZPE = [False, False]
+SPLIT = [((0, 6),), ((0, 6),)]
+PPE = [True, True]
+DPE = [True, True]
+FUSE = [[0, 1, 1], [0, 1, 1]]
 MAGIC = 12582912.0
 XO, ZO, NO, RO, LO, ZI, NI, RI, LI, RW = 0, 96, 192, 208, 304, 400, 496, 512, 608, 704
 
@@ -33,7 +38,7 @@ for _n, _c, _d in (
 for _c in range(NC):
     for _n, _w, _d in (
             ("CB", 32, "float32"), ("B", 56, "float32"), ("DE", 24, "float32"), ("FA", 768, "float32"),
-            ("IA", 512, "int32"), ("UW", 16, "int32"), ("OU", 384, "uint16"), ("BA", 1280, "bfloat16"),
+            ("IA", 512, "int32"), ("UW", 16, "int32"), ("OU", 384, "uint16"), ("BA", 1376, "bfloat16"),
             ("D1", 1536, "bfloat16"), ("H", 1536, "bfloat16"), ("Y", 1552, "bfloat16"),
             ("AB", [6, 256], "bfloat16"), ("AM", [6, 256], "bfloat16"), ("AJ", [6, 256], "bfloat16")):
         _buf(_n + str(_c), _w, _d)
@@ -45,17 +50,17 @@ for _b in range(8):
 NSEM = {"v": 44, "s": 30, "p": 30, "g": 12}
 SEMAPHORES = [e + str(i) for e in NSEM for i in range(NSEM[e])] + ["ld%d" % i for i in range(12)] \
     + ["ar%d" % i for i in range(8)] + ["sent", "st"]
-CY = 1.0
-M = dict(pcy=0.5, hop=70.0, ga=1.56, sc=3.8, rl=2500.0, rb=30.0)
-MODELS = [dict(M), dict(pcy=0.45, hop=120.0, ga=1.15, sc=2.5, rl=3500.0, rb=20.0),
-          dict(pcy=0.7, hop=50.0, ga=2.0, sc=5.0, rl=2000.0, rb=40.0)]
-ROUNDS = [2500, 1]
+M = dict(cy=0.83, pcy=0.45, hop=(210.0, 210.0), ov=0.0, ga=1.56, sc=3.8, rl=2500.0, rb=30.0)
+MODELS = [dict(M), dict(cy=0.9, pcy=0.5, hop=(170.0, 170.0), ov=0.0, ga=1.25, sc=2.5, rl=3200.0, rb=22.0),
+          dict(cy=1.05, pcy=0.6, hop=(260.0, 260.0), ov=0.0, ga=1.85, sc=5.0, rl=2500.0, rb=30.0)]
+ROUNDS = [3600, 3]
 FB = [1.0]
 _PLAN = {}
 
 
 def build(g, T, send):
     ops = []
+    CY = M["cy"]
     Q = {"v": g.vector, "s": g.scalar, "p": g.tensor, "g": g, "y": g.sync}
 
     def a(n, lo=None, hi=None, st=1, p=None):
@@ -78,7 +83,7 @@ def build(g, T, send):
                 r += list(x[1])
         for x in wr:
             w += list(x[1])
-        ops.append(dict(e=e, fns=fns, r=r, w=w, cost=cost, **kw))
+        ops.append(dict(e=e, fns=fns, r=r, w=w, cost=cost + (M["ov"] if e in "vs" else 0), **kw))
         return len(ops) - 1
 
     def u(x):
@@ -109,6 +114,8 @@ def build(g, T, send):
         rec("v", [lambda q: q.tensor_copy(out[0], i[0])], rd, [w], vc(out, [i]))
 
     def ms(out, val):
+        if val == int(val) and abs(val) < 2048 and out[1][0][0] not in ("CT", "ONE", "RS"):
+            return iota(out, [[0, out[2]]], int(val), 0)
         rec("v", [lambda q: q.memset(out[0], val)], [], [out], vc(out, [out]))
 
     def scan(out, d0, d1, o0, o1):
@@ -140,10 +147,11 @@ def build(g, T, send):
     def store(dst, i):
         rec("y", [lambda q: q.dma_start(dst, i[0])], [i], [], 60 + 128 * 2 * i[2] / 150.0, lat=2000, store=1)
 
-    def gather(e, out, i, scale=0.5):
-        ts(out, i, scale, A.mult)
-        act(out, i, scale=scale)
+    def gather(e, out, i, scale, bias=0.0):
+        ts(out, i, scale, A.mult, bias, A.add)
+        act(out, i, scale=scale, bias=a("PF", 15, 16) if bias else 0.0)
         os_, ov = ops.pop(), ops[-1]
+        ov["r"] = os_["r"]
         ov["alt"] = {"v": (ov["fns"], ov["cost"]), "s": (os_["fns"], os_["cost"])}
         put(ops, len(ops) - 1, e)
 
@@ -200,7 +208,9 @@ def build(g, T, send):
     ts(K53, PB, 53.0, A.mult, -15.0 / 32, A.add)
     ts(K2, PB, 2.0, A.mult, 2.0, A.add)
     ts(K1, PB, 2.0, A.mult, 1.0, A.add)
-    ms(a("CT", 192, 288, p=64), -1.0 / 256)
+    ms(QB, -MAGIC)
+    if True in ZPE:
+        ms(a("CT", 192, 288, p=64), -1.0 / 256)
     ts(a("HI"), a("ID"), 1.0 / 16384, A.mult)
     ts(a("OF", 0, 6), a("IS", 0, 6), 0.0, A.mult, PB, A.add)
     ts(a("IS", 40, 46), a("IS", 8, 14), PQ, A.add)
@@ -239,8 +249,8 @@ def build(g, T, send):
         ms(a("Y" + s, 0, 16), 0.0)
         ms(a("BA" + s, 0, 16), 0.0)
         ms(a("ST0" + s, ZI, RI), 0.0)
-        for t in range(1, NV):
-            ms(a("ST%d%d" % (t, c), NI + 8, RI), 0.0)
+        for t in range(NV - 1):
+            ms(a("ST%d%d" % (t, c), NO + 8, RO), 0.0)
     ms(a("CAP"), 100.0)
     ms(a("CAP", 8, 32), 0.0)
     ms(a("D2"), -1.0)
@@ -302,7 +312,8 @@ def build(g, T, send):
             tt(d, ind(XW, a(OU, 24 * m, 24 * m + 24)), a(BA, 128, 512), A.subtract)
             act(a3("AB" + s, T["AB" + s][:, :, 64 * m:64 * m + 64], m, m + 1, 384), d, F.Abs, 4096.0)
         for i in range(3):
-            gather(HENG[c][i], a("H" + s, 512 * i, 512 * i + 512), ind(XW, a(OU, 96 + 32 * i, 128 + 32 * i)))
+            if not FUSE[c][i]:
+                gather(HENG[c][i], a("H" + s, 512 * i, 512 * i + 512), ind(XW, a(OU, 96 + 32 * i, 128 + 32 * i)), 1.0)
         mm(a(PS, 288, 384), [(sel[b], a3("AB" + s, T["AB" + s][:, :, b:256:16], 0, 4, 96)) for b in range(16)])
         scan(a(FA, 0, 96), a("DK"), a(PS, 288, 384), A.add, A.min)
         k = a(IA, 48, 54)
@@ -319,7 +330,11 @@ def build(g, T, send):
         ts(a(IA, 64, 160), a(IA, 64, 160), 4095, A.bitwise_and)
         cp(a(OU, 192, 288), a(IA, 64, 160))
         for i in range(3):
-            gather(YENG[c][i], a("Y" + s, 16 + 512 * i, 528 + 512 * i), ind(XW, a(OU, 192 + 32 * i, 224 + 32 * i)))
+            gather(YENG[c][i], a("Y" + s, 16 + 512 * i, 528 + 512 * i), ind(XW, a(OU, 192 + 32 * i, 224 + 32 * i)), 1.0)
+        for i in range(3):
+            if FUSE[c][i]:
+                tt(a("H" + s, 512 * i, 512 * i + 512), ind(XW, a(OU, 96 + 32 * i, 128 + 32 * i)),
+                   a("Y" + s, 16 + 512 * i, 528 + 512 * i), A.subtract)
         gather("s", a(BA, 512, 608), ind(DW, od), 1.0)
         gather("s", a(BA, 1184, 1280), ind(XW, oc), 1.0)
         ts(a(IA, 8, 16), a(IA, 8, 16), 15, A.bitwise_and)
@@ -327,10 +342,22 @@ def build(g, T, send):
         tt(a(B, 0, 32), a(IA, 8, 40), a("CB" + s), A.add)
         cp(a(OU, 336, 344), a(B, 0, 8))
         ts(a(B, 40, 48), a(R, NI, NI + 8), 34.0, A.mult, 31.0, A.add)
-        tt(a(BA, 16, 112), ind(a(R, NI, NI + 8), ON), a("KC"), A.is_gt)
         L = a("L0", CL * c, CL * c + CL) if t == 0 else a(R, LI, LI + CL)
-        tt(a(BA, 608, 704), a(BA, 512, 608), L, A.subtract)
-        tt(a(BA, 704, 800), a(R, RI, RI + CL), L, A.subtract)
+        if PPE[c]:
+            pn = a("PS%d" % (3 * c + 1), 0, 96)
+            gather("s", a(BA, 1280, 1376), ind(a(R, NI, NI + 8), ON), 1.0)
+            mm(pn, [(ID, a(BA, 1280, 1376)), (NID, a("KC"))])
+            act(a(BA, 16, 112), pn, F.Relu, 1.0 / 8192)
+        else:
+            tt(a(BA, 16, 112), ind(a(R, NI, NI + 8), ON), a("KC"), A.is_gt)
+        if DPE[c]:
+            pd = "PS%d" % (3 * c + 2)
+            mm(a(pd, 96, 192), [(ID, a(R, RI, RI + CL)), (NID, L)])
+            mm(a(pd, 0, 96), [(ID, a(BA, 512, 608)), (NID, L)])
+            act(a(BA, 608, 800), a(pd, 0, 192), scale=1.0 / 8192)
+        else:
+            tt(a(BA, 608, 704), a(BA, 512, 608), L, A.subtract)
+            tt(a(BA, 704, 800), a(R, RI, RI + CL), L, A.subtract)
 
     def second(t, c):
         s = str(c)
@@ -341,10 +368,15 @@ def build(g, T, send):
             y = a(Y, 16 + 512 * i, 528 + 512 * i)
             for j, (nm, o) in enumerate((("AJ" + s, a(Y, 15 + 512 * i, 527 + 512 * i)), ("AM" + s, a("H" + s, 512 * i, 512 * i + 512)))):
                 d = a("PS%d" % (3 * c + i))
+                if j and FUSE[c][i]:
+                    act(a3(nm, T[nm][:, 2 * i:2 * i + 2, :], i, i + 1, 512), o, F.Abs, 1.0)
+                    continue
                 mm(d, [(ID, y), (NID, o)])
-                act(a3(nm, T[nm][:, 2 * i:2 * i + 2, :], i, i + 1, 512), d, F.Abs, 1.0 / 4096)
-        for nm, lo, w, pen in (("AJ" + s, 0, NID, a(BA, 15, 111)), ("AM" + s, 96, ID, a(BA, 16, 112))):
-            mm(a(PS, lo, lo + 96), [(w, pen)] + [(sel[b], a3(nm, T[nm][:, :, 16 * b:16 * b + 16], 0, 3, 96)) for b in range(16)])
+                act(a3(nm, T[nm][:, 2 * i:2 * i + 2, :], i, i + 1, 512), d, F.Abs, 1.0 / 8192)
+        for a0, a1 in SPLIT[c]:
+            for nm, lo, w, pen in (("AJ" + s, 0, NID, 15), ("AM" + s, 96, ID, 16)):
+                mm(a(PS, lo + 16 * a0, lo + 16 * a1), [(w, a(BA, pen + 16 * a0, pen + 16 * a1))]
+                   + [(sel[b], a3(nm, T[nm][:, a0:a1, 16 * b:16 * b + 16], a0 // 2, a1 // 2, 16 * (a1 - a0))) for b in range(16)])
         ts(a(BA, 800, 992, 2), a(PS, 0, 96), a("TH", 1, 2), A.is_le, 31.0, A.mult)
         ts(a(BA, 801, 992, 2), a(PS, 96, 192), a("TH", 0, 1), A.is_gt, 31.0, A.mult)
         sc = a(BA, 992, 1184)
@@ -357,10 +389,16 @@ def build(g, T, send):
         yw = a(Y, 16, 1552)
         ye, pz, HI = a(BA, 320, 416), "PS%d" % (3 * c), a("HI")
         z = a("Z0", CL * c, CL * c + CL) if t == 0 else a(R, ZI, ZI + CL)
-        gather("s", ye, ind(yw, oe), 2.0)
-        for lo, o in ((0, a(BA, 1184, 1280)), (96, z)):
-            mm(a(pz, lo, lo + 96), [(a("ONE", p=64), a("CT", 192, 288, p=64)), (HI, o), (HI, ye)])
-        ts(a(R, XO, ZO + CL), a(pz, 0, 192), MAGIC, A.add, MAGIC, A.subtract)
+        if ZPE[c]:
+            gather("s", ye, ind(yw, oe), 1.0)
+            for lo, o in ((0, a(BA, 1184, 1280)), (96, z)):
+                mm(a(pz, lo, lo + 96), [(a("ONE", p=64), a("CT", 192, 288, p=64)), (HI, o), (HI, ye)])
+            ts(a(R, XO, ZO + CL), a(pz, 0, 192), MAGIC, A.add, MAGIC, A.subtract)
+        else:
+            for lo, o, to in ((416, z, ZO), (512, a(BA, 1184, 1280), XO)):
+                tt(a(FA, lo, lo + 96), ind(yw, oe), o, A.add)
+                ts(a(FA, lo, lo + 96), a(FA, lo, lo + 96), 0.5 - 1.0 / 4096, A.mult, MAGIC, A.add)
+                gather("v", a(R, to, to + CL), a(FA, lo, lo + 96), 1.0, -MAGIC)
         tt(a(IA, 288, 336), ind(sc, OY), a("CAP"), A.min)
         ts(a(IA, 336, 368), a(IA, 288, 320), 1, A.bitwise_and)
         tt(a("DE" + s, 0, 6), e, a(B, 8, 14), A.subtract)
@@ -370,7 +408,7 @@ def build(g, T, send):
         gather("s", a(R, NO, NO + 8), a(FA, 704, 712), 1.0)
         if t < NV - 1:
             cp(a("NF", 6 * c, 6 * c + 6), a(IA, 336, 342))
-            send(rec, a(R, ZO, NO + 8), a("ST%d%d" % (t + 1, c), ZI, NI + 8), 4 * t + 2 * c)
+            send(rec, a(R, ZO, NO), a("ST%d%d" % (t + 1, c), ZI, NI), 4 * t + 2 * c)
             if c == NC - 1:
                 mm(a(PS, 496, 510), [(a("ONE"), a("NF", 0, 14))])
                 rec("v", [lambda q: q.tensor_reduce(T.AC[:], T[PS][:, 496:510], AxisListType.X, A.add, negate=True)],
@@ -394,7 +432,7 @@ def build(g, T, send):
             tt(a(R, LO, LO + CL), a(BA, 128, 224), a(BA, 224, 320), A.add)
         gather("s", a(R, RO, RO + CL), ind(a(R, LO, RI + CL), a(OU, 360, 366)), 1.0)
         if t < NV - 1:
-            send(rec, a(R, RO, LO + CL), a("ST%d%d" % (t + 1, c), RI, LI + CL), 4 * t + 2 * c + 1)
+            send(rec, a(R, NO, LO + CL), a("ST%d%d" % (t + 1, c), NI, LI + CL), 4 * t + 2 * c + 1)
         else:
             store(T.yl[:, CL * c:CL * c + CL], a(R, LO, LO + CL))
             store(T.yr[:, CL * c:CL * c + CL], a(R, RO, RO + CL))
@@ -463,9 +501,11 @@ def place(ops, before, seq, hop, back):
         o = ops[i]
         c, lat = o["cost"], o.get("lat", 0)
         t = 0.0
+        e = o["e"]
         for j in before[i]:
-            if end[j] + hop > t:
-                t = end[j] + hop
+            x = end[j] + hop[ops[j]["e"] == e]
+            if x > t:
+                t = x
         if back:
             t += lat
         if o["e"] != "net":
@@ -508,19 +548,21 @@ def replay(ops, deps, order, hop):
     free, fin = {}, [0.0] * len(ops)
     for i in order:
         o = ops[i]
-        t = free.get(o["e"], 0.0)
+        e = o["e"]
+        t = free.get(e, 0.0)
         for j in deps[i]:
-            if fin[j] + hop > t:
-                t = fin[j] + hop
+            x = fin[j] + hop[ops[j]["e"] == e]
+            if x > t:
+                t = x
         if o["e"] != "net":
             free[o["e"]] = t + o["cost"]
         fin[i] = t + o["cost"] + o.get("lat", 0)
     return fin
 
 
-GUESS = {(0, 0): ((9, -3), (13, 0), (19, -2.5), (27, 0.5), (30, 0.6), (43, 3), (46, 6), (99, 8)),
-         (0, 1): ((19, 3.3), (27, 5), (30, 9.5), (43, 8), (46, 11), (99, 12)),
-         (1, 0): ((14, 7), (200, 10)), (1, 1): ((14, 12), (200, 16))}
+GUESS = {(0, 0): ((9, -3), (13, 0), (19, 2.5), (27, 0.5), (40, 3), (43, 6), (46, 7), (99, 8)),
+         (0, 1): ((19, 3.3), (27, 5), (40, 8), (43, 11), (46, 13), (99, 12)),
+         (1, 0): ((11, 7), (200, 10)), (1, 1): ((11, 12), (200, 16))}
 
 
 def guess(o, i):

@@ -2,17 +2,21 @@ from concourse.mybir import dt, AluOpType, AxisListType, ActivationFunctionType
 
 A = AluOpType
 F = ActivationFunctionType
-NV, SHIFT, NC, CL = 3, 3, 2, 96
-YENG = ["sss", "sss"]
-HENG = ["sss", "sss"]
-LPE = [False, False]
-ZPE = [False, False]
-SPLIT = [((0, 6),), ((0, 6),)]
+NV, SHIFT, NC = 3, 3, 2
+CLS = [96, 96]
+PA = [3, 3]
+FUSE = [[1, 1, 1, 1], [1, 1, 1, 1]]
+LPE = [True, True]
 PPE = [True, True]
-DPE = [True, True]
-FUSE = [[0, 1, 1], [0, 1, 1]]
-MAGIC = 12582912.0
-XO, ZO, NO, RO, LO, ZI, NI, RI, LI, RW = 0, 96, 192, 208, 304, 400, 496, 512, 608, 704
+L0S = [0, CLS[0]]
+EXT = 16 * CLS[0]
+BIG = 8192.0
+EV = 130
+
+
+def region(cl):
+    return 0, cl, 2 * cl, 2 * cl + 16, 3 * cl + 16, 4 * cl + 16, 4 * cl + 32, 5 * cl + 32, 6 * cl + 32
+
 
 SCRATCH = {}
 
@@ -22,59 +26,72 @@ def _buf(name, cols, dtype, where="sbuf"):
 
 
 for _n, _c, _d in (
-        ("X", 4096, "bfloat16"), ("DL", 1792, "bfloat16"), ("Z0", 192, "bfloat16"), ("L0", 192, "bfloat16"),
+        ("X", 4096 + EXT, "bfloat16"), ("DL", 1024 + 4 * sum(CLS), "bfloat16"), ("Z0", 192, "bfloat16"), ("L0", 192, "bfloat16"),
         ("WI", 1, "int32"), ("KI", 1, "int32"), ("CNI", 192, "int32"), ("LMI", 2, "int32"),
-        ("CNF", 192, "float32"), ("LMF", 2, "float32"), ("TH", 2, "float32"),
-        ("PI", 8, "int32"), ("PF", 24, "float32"), ("IC", 144, "bfloat16"), ("IB", 128, "bfloat16"),
-        ("ICO", 544, "bfloat16"), ("INN", 544, "bfloat16"), ("IPA", 34, "bfloat16"), ("KC", 96, "bfloat16"),
-        ("IS", 48, "float32"), ("Z8", 144, "float32"), ("E8", 128, "float32"),
-        ("ID", 128, "bfloat16"), ("NID", 128, "bfloat16"), ("ZS", 144, "bfloat16"), ("WB", 128, "bfloat16"),
-        ("BLK", 128, "bfloat16"), ("ONE", 128, "bfloat16"), ("CT", 288, "bfloat16"), ("HI", 128, "bfloat16"), ("NM", 96, "bfloat16"),
-        ("RS", 96, "float32"), ("D2", 192, "bfloat16"), ("DG", 16, "bfloat16"), ("KF", 16, "float32"),
-        ("DS", 16, "float32"), ("DK", 96, "float32"), ("KX", 96, "float32"), ("OF", 56, "float32"),
-        ("OFU", 56, "uint16"), ("QI", 8, "int32"), ("TAB", 592, "bfloat16"), ("EB", 16, "float32"),
-        ("CAP", 48, "float32"), ("NF", 16, "bfloat16"), ("AC", 1, "float32"), ("YN", 192, "float32")):
+        ("CNF", 192, "float32"), ("LMF", 2, "float32"), ("TH", 4, "float32"),
+        ("PI", 8, "int32"), ("PF", 32, "float32"), ("IC", 144, "bfloat16"), ("IB", 128, "bfloat16"),
+        ("ICO", 512, "bfloat16"), ("INN", 512, "bfloat16"), ("IPA", 512, "bfloat16"), ("KC", 128, "bfloat16"),
+        ("IS", 16, "float32"), ("Z8", 144, "float32"), ("E8", 128, "float32"), ("E", 1024, "bfloat16"),
+        ("ID", 128, "bfloat16"), ("NID", 128, "bfloat16"), ("IDB", 128, "bfloat16"), ("ZS", 144, "bfloat16"), ("NZS", 144, "bfloat16"),
+        ("WZ", 144, "float16"), ("WB", 128, "float16"), ("NH", 128, "float16"), ("IDH", 128, "float16"),
+        ("DGM", 128, "float16"), ("DGJ", 128, "float16"), ("CH", 512, "float16"),
+        ("BLK", 128, "bfloat16"), ("ONE", 128, "bfloat16"), ("CT", 256, "bfloat16"),
+        ("DG", 32, "bfloat16"), ("KF", 16, "float32"), ("DS", 16, "float32"), ("DK", 128, "float32"), ("OF", 24, "float32"),
+        ("OFU", 24, "uint16"), ("TAB", 1024, "bfloat16"), ("LN", 8, "float32"),
+        ("NF", 16, "bfloat16"), ("AC", 2, "float32"), ("YN", 192, "float32")):
     _buf(_n, _c, _d)
 for _c in range(NC):
+    _na, _w16 = CLS[_c] // 16, 16 * CLS[_c]
     for _n, _w, _d in (
-            ("CB", 32, "float32"), ("B", 56, "float32"), ("DE", 24, "float32"), ("FA", 768, "float32"),
-            ("IA", 512, "int32"), ("UW", 16, "int32"), ("OU", 384, "uint16"), ("BA", 1376, "bfloat16"),
-            ("D1", 1536, "bfloat16"), ("H", 1536, "bfloat16"), ("Y", 1552, "bfloat16"),
-            ("AB", [6, 256], "bfloat16"), ("AM", [6, 256], "bfloat16"), ("AJ", [6, 256], "bfloat16")):
+            ("CB", 32, "float32"), ("B", 48, "float32"), ("DE", 24, "float32"), ("NB", 32, "float32"), ("EB", 16, "float32"),
+            ("FA", 1024, "float32"), ("OFF", 256, "float32"), ("SC", 256, "float32"),
+            ("IA", 160, "int32"), ("IH", [_na, 16], "int32"), ("IY", [_na, 16], "int32"), ("OU", 448, "uint16"), ("BA", 1040, "bfloat16"),
+            ("ZT", 128, "bfloat16"), ("X2", 128, "float16"),
+            ("XC", _w16, "bfloat16"), ("H", _w16, "bfloat16"), ("Y", _w16 + 16, "bfloat16"),
+            ("AB", [2 * _na, 128], "bfloat16"), ("AM", [2 * _na, 128], "bfloat16"), ("AJ", [2 * _na, 128], "bfloat16")):
         _buf(_n + str(_c), _w, _d)
     for _t in range(NV):
-        _buf("ST%d%d" % (_t, _c), RW, "bfloat16")
-for _b in range(8):
-    _buf("PS%d" % _b, 512, "float32", "psum")
+        _buf("ST%d%d" % (_t, _c), region(CLS[_c])[8], "bfloat16")
+        _buf("ZI%d%d" % (_t, _c), [_na, 16], "float16")
+        _buf("ZN%d%d" % (_t, _c), CLS[_c], "float16")
+for _b in ("D0", "D1", "D2", "D3", "K0", "K1", "U0", "U1"):
+    _buf("PS" + _b, 512, "float32", "psum")
 
-NSEM = {"v": 44, "s": 30, "p": 30, "g": 12}
-SEMAPHORES = [e + str(i) for e in NSEM for i in range(NSEM[e])] + ["ld%d" % i for i in range(12)] \
+NSEM = {"v": 44, "s": 30, "p": 30, "g": 11}
+SEMAPHORES = [e + str(i) for e in NSEM for i in range(NSEM[e])] + ["ld%d" % i for i in range(13)] \
     + ["ar%d" % i for i in range(8)] + ["sent", "st"]
-M = dict(cy=0.83, pcy=0.45, hop=(210.0, 210.0), ov=0.0, ga=1.56, sc=3.8, rl=2500.0, rb=30.0)
-MODELS = [dict(M), dict(cy=0.9, pcy=0.5, hop=(170.0, 170.0), ov=0.0, ga=1.25, sc=2.5, rl=3200.0, rb=22.0),
-          dict(cy=1.05, pcy=0.6, hop=(260.0, 260.0), ov=0.0, ga=1.85, sc=5.0, rl=2500.0, rb=30.0)]
-ROUNDS = [3600, 3]
-FB = [1.0]
+M = dict(cy=0.83, pcy=0.45, hop=210.0, ov=0.0, ga=1.56, sc=3.8, rl=2500.0, rb=30.0)
+MODELS = [dict(M), dict(cy=0.9, pcy=0.5, hop=170.0, ov=0.0, ga=1.25, sc=2.5, rl=3200.0, rb=22.0),
+          dict(cy=1.05, pcy=0.6, hop=260.0, ov=0.0, ga=1.85, sc=5.0, rl=2500.0, rb=30.0)]
+ROUNDS = [2500, 3]
 _PLAN = {}
 
 
 def build(g, T, send):
     ops = []
     CY = M["cy"]
-    Q = {"v": g.vector, "s": g.scalar, "p": g.tensor, "g": g, "y": g.sync}
 
-    def a(n, lo=None, hi=None, st=1, p=None):
+    def a(n, lo=None, hi=None, st=1, p=None, p0=0):
         w = SCRATCH[n][1][1]
         lo = 0 if lo is None else lo
         hi = w if hi is None else hi
-        ap = T[n][0:(p or 128), lo:hi:st] if st > 1 else T[n][0:(p or 128), lo:hi]
+        ps = slice(p0, p0 + (p or 128))
+        ap = T[n][ps, lo:hi:st] if st > 1 else T[n][ps, lo:hi]
         return (ap, ((n, lo, hi),), len(range(lo, hi, st)), SCRATCH[n][2], None)
+
+    def rev(n, lo, hi):
+        ap = T[n][:, hi - 1:lo - 1:-1] if lo else T[n][:, hi - 1::-1]
+        return (ap, ((n, lo, hi),), hi - lo, SCRATCH[n][2], None)
+
+    def a3(n, r0=0, r1=None, c0=0, c1=None):
+        rows, w = SCRATCH[n][1][1:]
+        r1 = rows if r1 is None else r1
+        c1 = w if c1 is None else c1
+        rng = ((n, r0 * w, r1 * w),) if (c0, c1) == (0, w) else tuple((n, r * w + c0, r * w + c1) for r in range(r0, r1))
+        return (T[n][:, r0:r1, c0:c1], rng, (r1 - r0) * (c1 - c0), SCRATCH[n][2], None)
 
     def ind(win, off):
         return (win[0].indirect(off[0]), win[1] + off[1], 16 * off[2], win[3], "ind")
-
-    def a3(n, ap, lo, hi, cnt):
-        return (ap, ((n, lo, hi),), cnt, SCRATCH[n][2], None)
 
     def rec(e, fns, rd, wr, cost, **kw):
         r, w = [], []
@@ -94,7 +111,7 @@ def build(g, T, send):
             return (60 + M["ga"] * out[2]) * CY
         if out[4] == "ind":
             return (60 + M["sc"] * out[2]) * CY
-        half = all(x[3] in ("bfloat16", "uint16") for x in [out] + ins)
+        half = all(x[3] in ("bfloat16", "uint16", "float16") for x in [out] + ins)
         return max(64, out[2] * (0.5 if half else 1) * (2 if two else 1)) * CY
 
     def ts(out, i, s1, o0, s2=None, o1=None):
@@ -113,8 +130,8 @@ def build(g, T, send):
         rd = [i] + ([(0, out[1][1:])] if out[4] else [])
         rec("v", [lambda q: q.tensor_copy(out[0], i[0])], rd, [w], vc(out, [i]))
 
-    def ms(out, val):
-        if val == int(val) and abs(val) < 2048 and out[1][0][0] not in ("CT", "ONE", "RS"):
+    def ms(out, val, v=False):
+        if not v and val == int(val) and abs(val) <= 256 and out[3] in ("float32", "bfloat16"):
             return iota(out, [[0, out[2]]], int(val), 0)
         rec("v", [lambda q: q.memset(out[0], val)], [], [out], vc(out, [out]))
 
@@ -125,11 +142,16 @@ def build(g, T, send):
         c = (78 + M["ga"] * out[2]) * CY if i[4] else max(64, out[2] + 30) * CY
         rec("s", [lambda q: q.activation(out[0], i[0], fn, bias=u(bias), scale=scale)], [i, bias], [out], c)
 
-    def mm(out, pairs):
+    groups = {None: 0}
+
+    def mm(out, pairs, first=True, last=True):
         k = len(pairs)
-        fns = [(lambda q, j=j: q.matmul(out[0], pairs[j][0][0], pairs[j][1][0], j == 0, j == k - 1)) for j in range(k)]
-        c = sum(max(64, r[2]) * (4 if r[3] == "float32" else 1) for l, r in pairs) * M["pcy"] + 60
-        rec("p", fns, [x for pr in pairs for x in pr], [out], c)
+        if first:
+            groups[None] += 1
+            groups[out[1][0]] = groups[None]
+        fns = [(lambda q, j=j: q.matmul(out[0], pairs[j][0][0], pairs[j][1][0], first and j == 0, last and j == k - 1)) for j in range(k)]
+        c = sum(max(64, r[2]) * (4 if r[3] == "float32" else 1) for l, r in pairs) * M["pcy"] + 30
+        rec("p", fns, [x for pr in pairs for x in pr], [out], c, grp=groups[out[1][0]])
 
     def iota(out, pat, base=0, cm=0):
         if out[3] == "int32":
@@ -147,312 +169,353 @@ def build(g, T, send):
     def store(dst, i):
         rec("y", [lambda q: q.dma_start(dst, i[0])], [i], [], 60 + 128 * 2 * i[2] / 150.0, lat=2000, store=1)
 
-    def gather(e, out, i, scale, bias=0.0):
+    def either(e, out, i, scale=1.0, bias=0.0, bcol=0.0):
         ts(out, i, scale, A.mult, bias, A.add)
-        act(out, i, scale=scale, bias=a("PF", 15, 16) if bias else 0.0)
+        act(out, i, scale=scale, bias=bcol)
         os_, ov = ops.pop(), ops[-1]
         ov["r"] = os_["r"]
         ov["alt"] = {"v": (ov["fns"], ov["cost"]), "s": (os_["fns"], os_["cost"])}
         put(ops, len(ops) - 1, e)
 
+    D0 = 4 * CLS[0]
     load("y", a("Z0"), T.zed[:], 2200)
     load("s", a("WI"), T.wt[:], 2200)
     load("s", a("KI"), T.kap[:], 2300)
-    load("y", a("X"), T.stock[:], 7500)
+    load("y", a("X", 0, 4096), T.stock[:], 7000)
     for c in range(NC):
-        load("s", a("ST0%d" % c, RI, RI + CL), T.rend[:, CL * c:CL * c + CL], 2500)
+        RI = region(CLS[c])[6]
+        load("s", a("ST0%d" % c, RI, RI + CLS[c]), T.rend[:, L0S[c]:L0S[c] + CLS[c]], 2500)
     load("s", a("CNI", p=8), T.cnt[:], 2600)
     load("s", a("LMI", p=8), T.lim[:], 2600)
-    load("y", a("DL", 384, 1408), T.donor[:], 9000)
-    load("y", a("L0"), T.lend[:], 9500)
+    load("y", a("DL", D0, D0 + 1024), T.donor[:], 8500)
+    load("y", a("L0"), T.lend[:], 9000)
+    load("y", a("X", 4096, 4096 + EXT), T.stock[:, 0:EXT], 11000)
     iota(a("PI", 0, 1), [[0, 1]], 0, 1)
     iota(a("IB"), [[16, 8], [0, 16]])
-    iota(a("KC"), [[0, 6], [1, 16]])
     iota(a("IC"), [[1, 144]])
     iota(a("IS", 0, 8), [[1, 8]])
-    iota(a("IS", 8, 14), [[4, 6]])
-    iota(a("IS", 16, 40), [[16, 6], [0, 4]])
+    iota(a("E", 0, 512), [[16, 4], [1, 8], [0, 16]])
+    iota(a("KC"), [[0, 8], [1, 16]])
     iota(a("Z8", p=8), [[1, 144]], -15, -16)
     iota(a("E8", p=8), [[16, 8], [0, 16]], 0, -16)
-    iota(a("ICO"), [[0, 16], [1, 34]])
-    iota(a("INN"), [[1, 16], [0, 34]])
-    iota(a("IPA"), [[0, 17], [1, 2]])
+    iota(a("ICO"), [[0, 16], [1, 32]])
+    iota(a("INN"), [[1, 16], [0, 32]])
+    iota(a("IPA"), [[0, 256], [-1, 2]], 1)
     p0 = a("PI", 0, 1)
-    ts(a("PI", 1, 2), p0, 15, A.bitwise_and)
-    ts(a("PI", 2, 3), p0, 112, A.bitwise_and)
-    ts(a("PI", 3, 4), p0, 15, A.bitwise_and, 2, A.logical_shift_right)
-    ts(a("PI", 4, 5), p0, 3, A.bitwise_and)
-    ts(a("PI", 5, 6), p0, 7, A.bitwise_and)
+    for j, m in ((1, 15), (2, 112), (3, 63), (4, 7), (5, 8)):
+        ts(a("PI", j, j + 1), p0, m, A.bitwise_and)
     cp(a("PF", 0, 6), a("PI", 0, 6))
     col = lambda j: a("PF", j, j + 1)
-    PP, PB, G16, PQ, P3, P7, WF, KP, CU, CYY, P16, K53, K2, K1, K15, QB = [col(j) for j in range(16)]
-    ts(WF, a("WI"), 1.0 / 16, A.mult)
+    PP, PB, G16, P64, P7, P8, W32, W2, KP, K4, KQ, K53, K1, K2, K15, CW, C1024, C2047 = [col(j) for j in range(18)]
+    ts(W32, a("WI"), 1.0 / 32, A.mult)
+    ts(W2, a("WI"), 0.5, A.mult)
     cp(KP, a("KI"))
-    ts(a("WB"), a("IB"), G16, A.is_equal, WF, A.mult)
-    ts(a("ID"), a("IC", 0, 128), PP, A.is_equal, 8192.0, A.mult)
-    ts(a("NM"), a("KC"), PB, A.not_equal, -16.0, A.mult)
+    ts(K4, a("KI"), 2.0, A.mult, -4.0, A.add)
+    ts(KQ, KP, KP, A.mult, -4.0, A.mult)
+    ts(KQ, KQ, -0.25, A.add)
+    ts(a("WB"), a("IB"), G16, A.is_equal, W32, A.mult)
+    ts(a("ID"), a("IC", 0, 128), PP, A.is_equal)
+    ts(a("NH"), a("ID"), -0.5, A.mult)
+    ts(a("ZS"), a("IC"), G16, A.subtract, 15.0, A.is_equal)
+    ts(a("WZ"), a("ZS"), W2, A.mult)
+    ts(a("E", 512, 1024), a("E", 0, 512), 8.0, A.add, P64, A.is_equal)
+    ts(a("E", 0, 512), a("E", 0, 512), P64, A.is_equal)
     ms(a("ONE"), 1.0)
-    ms(a("CT", 0, 96, p=64), -4.0)
-    rec("v", [lambda q: q.memset(T.CT[32:64, 0:96], 1.0 / 1024)], [], [a("CT", 0, 96)], 64 * CY)
-    ms(a("CT", 96, 192, p=64), 1.0 / 64)
-    ms(a("RS"), 1.0)
-    ms(a("RS", 0, 96, 16), 0.0)
+    ms(a("CT", 0, 128, p=32), -4.0)
+    ms(a("CT", 0, 128, p=32, p0=32), 1.0 / 1024)
+    ms(a("CT", 128, 256, p=64), 1.0 / 64)
+    NEG, RB, CM, CJ = [lambda n, k=k: a("CH", 128 * k, 128 * k + n) for k in range(4)]
+    ms(NEG(128), -2048.0)
+    ms(RB(128), BIG)
+    ms(CM(128), -2040.0)
+    ms(CJ(128), 2041.0)
+    ms(a("CH", 384, 512, 16), -60000.0)
+    ms(C1024, 1024.0)
+    ms(C2047, 2047.5)
     ts(a("BLK"), a("IB"), G16, A.is_equal)
-    ts(a("DG"), a("KC", 0, 16), PB, A.is_equal, KP, A.mult)
-    mm(a("PS0", 0, 16), [(a("BLK"), a("DG"))])
-    cp(a("KF"), a("PS0", 0, 16))
-    ts(P7, P7, 5.0, A.min)
-    ts(CU, P7, 16.0, A.mult, 15.0, A.add)
-    ts(CYY, P7, 32.0, A.mult, 31.0, A.add)
-    ts(P16, PB, 16.0, A.mult)
+    ts(a("DG", 0, 16), a("KC", 0, 16), PB, A.is_equal, KP, A.mult)
+    cp(a("DG", 16, 17), a("WI"))
+    mm(a("PSD2", 0, 17), [(a("BLK"), a("DG", 0, 17))])
+    cp(a("KF"), a("PSD2", 0, 16))
+    ts(CW, a("PSD2", 16, 17), -1024.0, A.mult)
     ts(K53, PB, 53.0, A.mult, -15.0 / 32, A.add)
-    ts(K2, PB, 2.0, A.mult, 2.0, A.add)
     ts(K1, PB, 2.0, A.mult, 1.0, A.add)
-    ms(QB, -MAGIC)
-    if True in ZPE:
-        ms(a("CT", 192, 288, p=64), -1.0 / 256)
-    ts(a("HI"), a("ID"), 1.0 / 16384, A.mult)
-    ts(a("OF", 0, 6), a("IS", 0, 6), 0.0, A.mult, PB, A.add)
-    ts(a("IS", 40, 46), a("IS", 8, 14), PQ, A.add)
-    ts(a("QI", 0, 6), a("IS", 40, 46), -2.5, A.add, 1.0 / 6, A.mult)
-    ts(a("OF", 6, 12), a("QI", 0, 6), 4.0, A.mult, P3, A.add)
-    ts(a("OF", 12, 18), a("QI", 0, 6), -6.0, A.mult)
-    tt(a("OF", 12, 18), a("OF", 12, 18), a("IS", 40, 46), A.add)
-    ts(a("OF", 18, 42), a("IS", 16, 40), PB, A.add)
-    cp(a("OF", 42, 48), a("IS", 0, 6))
-    ts(a("OF", 48, 52), a("IS", 0, 4), 0.0, A.mult, CU, A.add)
-    ts(a("OF", 52, 56), a("IS", 0, 4), 0.0, A.mult, CYY, A.add)
+    ts(K2, PB, 2.0, A.mult)
+    ts(a("OF", 0, 8), a("IS", 0, 8), 0.0, A.mult, PB, A.add)
+    for c in range(NC):
+        lo = 8 + 4 * c
+        ts(a("OF", lo, lo + 2), a("IS", 0, 2), 0.0, A.mult, P7, A.add)
+        ts(a("OF", lo, lo + 2), a("OF", lo, lo + 2), CLS[c] // 16 - 1.0, A.min)
+        ts(a("OF", lo + 2, lo + 4), a("OF", lo, lo + 2), 32.0, A.mult)
+    cp(a("OF", 16, 24), a("IS", 0, 8))
     cp(a("OFU"), a("OF"))
-    OPB, OK, OA, OZ, ON, OUU, OY = [a("OFU", x, y) for x, y in ((0, 6), (6, 12), (12, 18), (18, 42), (42, 48), (48, 51), (52, 55))]
-    act(a("KX"), ind(a("KF"), OK))
     ms(a("DS", 0, 1), 33554432.0)
     tt(a("DS", 1, 16), a("KF", 0, 15), a("KF", 1, 16), A.subtract)
     ts(a("DS", 1, 16), a("DS", 1, 16), -256.0, A.add)
-    act(a("DK"), ind(a("DS"), OPB))
+    act(a("DK"), ind(a("DS"), a("OFU", 0, 8)))
     ts(K15, a("KF", 15, 16), 3840.0, A.add)
-    ts(a("ZS"), a("IC"), G16, A.subtract, 15.0, A.is_equal)
     ts(a("NID"), a("ID"), -1.0, A.mult)
-    EB = a("EB", 0, 8)
-    ts(EB, a("IS", 0, 8), 256.0, A.mult, P16, A.add)
-    ts(a("EB", 8, 16), EB, 2.0, A.mult, 30.0, A.add)
+    ts(a("IDB"), a("ID"), 134217728.0, A.mult)
+    ts(a("IDH"), a("ID"), BIG, A.mult)
+    ts(a("NZS"), a("ZS"), -1.0, A.mult)
+    LN = a("LN")
+    ts(LN, a("IS", 0, 8), 16.0, A.mult, PB, A.add)
     for c in range(NC):
-        s = str(c)
-        cp(a("CB" + s, 0, 8), EB)
-        cp(a("CB" + s, 8, 16), EB)
-        ms(a("CB" + s, 16, 24), 1.0)
-        ts(a("CB" + s, 24, 32), EB, 0.25, A.mult, 384.0 if c == 0 else 0.0, A.add)
-        ts(a("B" + s, 32, 40), EB, 1.0 / 16, A.mult)
-        ms(a("B" + s, 48, 56), 575.0)
-        ms(a("DE" + s, 0, 8), 0.0)
-        ms(a("DE" + s, 8, 16), -384.0 if c == 0 else 640.0)
-        ms(a("DE" + s, 16, 24), float(RI - LO))
+        s, na, cl = str(c), CLS[c] // 16, CLS[c]
+        XO, ZO, NO, RO, LO, NI, RI, LI, RW = region(cl)
+        EB, T0, T1, OFF = a("EB" + s, 0, 8), col(20 + 2 * c), col(21 + 2 * c), "OFF" + s
+        ts(T0, P8, 16.0 * na, A.mult)
+        ts(T1, P7, 16.0, A.mult, T0, A.add)
+        ts(EB, a("IS", 0, 8), 128.0, A.mult, T1, A.add)
+        ts(a("EB" + s, 8, 16), EB, -2.0, A.mult)
+        ts(T0, T1, 2.0, A.mult)
+        iota(a(OFF, 0, 32 * na), [[256, na], [2, 16], [0, 2]])
+        ts(a(OFF, 0, 32 * na), a(OFF, 0, 32 * na), T0, A.add)
+        ts(a(OFF, 1, 32 * na, 2), a(OFF, 1, 32 * na, 2), 0.75, A.add)
+        ts(a(OFF, 31, 32 * na, 32), a(OFF, 31, 32 * na, 32), -0.125, A.add)
+        ms(a("CB" + s, 0, 8), 1.0)
+        ts(a("CB" + s, 8, 16), LN, 4.0, A.mult, float(D0) if c == 0 else 0.0, A.add)
+        cp(a("CB" + s, 16, 24), EB)
+        ts(a("CB" + s, 24, 32), LN, 16.0, A.mult)
+        ms(a("B" + s, 0, 8), 0.0)
+        cp(a("B" + s, 8, 16), LN)
+        ms(a("DE" + s, 0, 8), float(RI - LO))
+        ms(a("DE" + s, 8, 16), 0.0)
+        ms(a("DE" + s, 16, 24), -float(D0) if c == 0 else 1024.0 - D0)
+        ms(a("NB" + s, 0, 8), 0.0)
+        ms(a("NB" + s, 8, 32), -0.2)
+        ms(a("IA" + s, 0, 8), 0)
         ms(a("Y" + s, 0, 16), 0.0)
         ms(a("BA" + s, 0, 16), 0.0)
-        ms(a("ST0" + s, ZI, RI), 0.0)
+        ms(a("ST0" + s, NI, RI), 0.0)
+        ms(a("PSK" + s, EV + 32 * na - 1, EV + 32 * na), -1e6)
+        ms(a("PSD%d" % (2 * c + 1), 0, 128), 0.0, True)
         for t in range(NV - 1):
             ms(a("ST%d%d" % (t, c), NO + 8, RO), 0.0)
-    ms(a("CAP"), 100.0)
-    ms(a("CAP", 8, 32), 0.0)
-    ms(a("D2"), -1.0)
-    ms(a("D2", 1, 192, 32), 1024.0)
-    ms(a("NF", 12, 13), -12.0)
-    ms(a("NF", 13, 14), 1.0 / 512)
-    ms(a("DL", 0, 384), 0.0)
-    ms(a("DL", 1408, 1792), 0.0)
+        ts(a3("ZI0" + s), a("Z0", L0S[c], L0S[c] + cl), 2.0, A.mult, 2048.0, A.add)
+    ms(a("DL", 0, D0), 0.0)
+    ms(a("DL", D0 + 1024), 0.0)
     ts(a("Z8", p=8), a("Z8", p=8), 0.0, A.is_equal)
     ts(a("E8", p=8), a("E8", p=8), 0.0, A.is_equal)
     cp(a("CNF", p=8), a("CNI", p=8))
     cp(a("LMF", p=8), a("LMI", p=8))
-    mm(a("PS1", 0, 12), [(a("Z8", 15 - b, 143 - b, p=8), a("CNF", b, 192, 16, p=8)) for b in range(16)])
-    mm(a("PS2", 0, 2), [(a("E8", p=8), a("LMF", p=8))])
+    mm(a("PSD2", 32, 44), [(a("Z8", 15 - b, 143 - b, p=8), a("CNF", b, 192, 16, p=8)) for b in range(16)])
+    mm(a("PSD2", 48, 50), [(a("E8", p=8), a("LMF", p=8))])
     for c in range(NC):
-        act(a("ST0%d" % c, NI, NI + 6), a("PS1", 6 * c, 6 * c + 6))
-    act(a("TH"), a("PS2", 0, 2))
-    ts(a("TAB", 544, 578), a("ICO", 0, 34), K1, A.is_le)
-    tt(a("TAB", 544, 578), a("TAB", 544, 578), a("IPA"), A.mult)
-    ts(a("ICO"), a("ICO"), K2, A.is_ge)
+        NI = region(CLS[c])[5]
+        act(a("ST0%d" % c, NI, NI + CLS[c] // 16), a("PSD2", 32 + L0S[c] // 16, 32 + (L0S[c] + CLS[c]) // 16))
+    act(a("TH", 0, 2), a("PSD2", 48, 50))
+    ts(a("TH", 2, 3), a("TH", 0, 1), -1.0, A.mult, 2040.0, A.add)
+    ts(a("TH", 3, 4), a("TH", 1, 2), -2040.0, A.add)
+    ts(a("DGM"), a("ID"), a("TH", 2, 3), A.mult)
+    ts(a("DGJ"), a("ID"), a("TH", 3, 4), A.mult)
+    ts(a("TAB", 512, 1024), a("ICO"), K2, A.is_le)
+    tt(a("TAB", 512, 1024), a("TAB", 512, 1024), a("IPA"), A.mult)
+    ts(a("ICO"), a("ICO"), K1, A.is_ge)
     ts(a("INN"), a("INN"), PB, A.is_le)
-    tt(a("TAB", 0, 544), a("ICO"), a("INN"), A.mult)
+    tt(a("TAB", 0, 512), a("ICO"), a("INN"), A.mult)
     store(T.yx[:, 3072:4096], a("X", 3072, 4096))
     rec("y", [lambda q: q.dma_start(T.yd[:, 768:1024], T.donor[:, 768:1024])], [a("L0")], [], 60, lat=2500, store=1)
 
-    XW, DW, TW = a("X"), a("DL", 384, 1408), a("TAB", 0, 578)
+    XW, DW = a("X", 0, 4096), a("DL", D0, D0 + 1024)
     sel = [a("ZS", 15 - b, 143 - b) for b in range(16)]
+    nsel = [a("NZS", 15 - b, 143 - b) for b in range(16)]
     ID, NID = a("ID"), a("NID")
+    APS = a("PSD0", 511, 512)
+
+    def pieces(c):
+        w = 8 * PA[c]
+        return [(w * i, w) for i in range(CLS[c] // w)]
+
+    def listing(c, I, lo, add):
+        na = CLS[c] // 16
+        ts(a3(I), a3(I), 4095, A.bitwise_and)
+        for h in range(2):
+            o = a("OU%d" % c, lo + 8 * na * h, lo + 8 * na * (h + 1))
+            if add is None:
+                cp(o, a3(I, 0, na, 8 * h, 8 * h + 8))
+            else:
+                ts(o, a3(I, 0, na, 8 * h, 8 * h + 8), add, A.add)
+
+    def sums(c, out, head, w, nm):
+        na = CLS[c] // 16
+        if head:
+            mm(out, head, True, False)
+        for h in range(2):
+            mm(out, [(w[8 * h + b], a3(nm, h * na, h * na + na, 16 * b, 16 * b + 16)) for b in range(8)], not head and h == 0, h == 1)
 
     def first(t, c):
-        s = str(c)
-        R = "ST%d%d" % (t, c)
-        z = a("Z0", CL * c, CL * c + CL) if t == 0 else a(R, ZI, ZI + CL)
-        PS, FA, IA, UW, OU, BA, B = "PS%d" % (6 + c), "FA" + s, "IA" + s, "UW" + s, "OU" + s, "BA" + s, "B" + s
-        one = a("ONE", p=64)
-        mm(a(PS, 192, 288), [(ID, a("NM")), (a("WB"), z)])
-        mm(a(PS, 0, 96), [(one, a("CT", 0, 96, p=64)), (a("WB"), z)])
-        mm(a(PS, 96, 192), [(one, a("CT", 96, 192, p=64)), (a("WB"), z)])
-        gather("s", a(BA, 128, 512), ind(z, OZ), 1.0)
-        scan(a(FA, 0, 96), a("RS"), a(PS, 192, 288), A.mult, A.max)
-        ts(a(IA, 0, 48), ind(a(FA, 0, 96), OUU), 16.0, A.mult)
-        uu, ba = a(UW, 0, 8), a(UW, 8, 16)
-        ts(uu, a(IA, 0, 8), 4095, A.bitwise_and)
-        tt(a(FA, 96, 104), uu, uu, A.mult)
-        tt(a(FA, 128, 224), ind(uu, OA), a("KX"), A.mult)
-        ts(ba, a(FA, 96, 104), 1.0 / 16, A.mult, -0.25 if t == 0 else a("AC"), A.add)
-        tt(a(IA, 64, 160), ind(ba, OA), a(FA, 128, 224), A.add)
-        ts(a(IA, 64, 160), a(IA, 64, 160), 4095, A.bitwise_and)
-        cp(a(OU, 0, 96), a(IA, 64, 160))
-        ts(a(FA, 224, 320), a(PS, 0, 96), 3221225472.0, A.add, 3221225472.0, A.subtract)
-        v = a(FA, 320, 416)
-        tt(v, a(PS, 96, 192), a(FA, 224, 320), A.subtract)
-        tt(a(FA, 224, 320), a(R, RI, RI + CL), v, A.mult)
-        ts(a(IA, 160, 256), a(FA, 224, 320), K53, A.add)
-        ts(a(IA, 160, 256), a(IA, 160, 256), 4095, A.bitwise_and)
-        cp(a(OU, 96, 192), a(IA, 160, 256))
-        for m in range(4):
-            d = a("D1" + s, 384 * m, 384 * m + 384)
-            tt(d, ind(XW, a(OU, 24 * m, 24 * m + 24)), a(BA, 128, 512), A.subtract)
-            act(a3("AB" + s, T["AB" + s][:, :, 64 * m:64 * m + 64], m, m + 1, 384), d, F.Abs, 4096.0)
-        for i in range(3):
+        s, cl, na, pa = str(c), CLS[c], CLS[c] // 16, PA[c]
+        XO, ZO, NO, RO, LO, NI, RI, LI, RW = region(cl)
+        R, Z = "ST%d%d" % (t, c), "ZI%d%d" % (t, c)
+        PU, PK, FA, IA, OU, BA, B = "PSU" + s, "PSK" + s, "FA" + s, "IA" + s, "OU" + s, "BA" + s, "B" + s
+        PD = ["PSD%d" % (2 * c), "PSD%d" % (2 * c + 1)]
+        fa = lambda k: a(FA, 128 * k, 128 * k + cl)
+        one, z2 = a("ONE", p=64), a3(Z)
+        for k in range(2):
+            mm(a(PU, 128 * k, 128 * k + cl), [(a("WB"), NEG(cl)), (one, a("CT", 128 * k, 128 * k + cl, p=64))], True, False)
+            mm(a(PU, 128 * k, 128 * k + cl), [(a("WB"), z2)], False, True)
+        v = fa(1)
+        ts(fa(0), a(PU, 0, cl), 3221225472.0, A.add, 3221225472.0, A.subtract)
+        tt(v, a(PU, 128, 128 + cl), fa(0), A.subtract)
+        act(fa(2), v, F.Square, 4.0, K4)
+        ts(a3("IY" + s), fa(2), KQ, A.add)
+        listing(c, "IY" + s, 0, None if t == 0 else APS if c == 0 else a("AC", 0, 1))
+        if t and c == 0:
+            ts(a("AC", 0, 1), APS, 0.0, A.add)
+            ts(a("AC", 1, 2), APS, -0.25, A.add)
+        for r in range(na // pa):
+            mm(a(PD[1], 0, 128, p=16 * pa, p0=64 * r), [(a3(Z, r * pa, r * pa + pa), a("NH"))])
+        act(a("ZT" + s), a(PD[1], 0, 128), bias=C1024)
+        mm(a(PK, 400, 400 + na), [(a("WZ", 15 - b, 143 - b), a3(Z, 0, na, b, b + 1)) for b in range(16)])
+        ts(a(IA, 0, na), a(PK, 400, 400 + na), CW, A.add)
+        uu, ba = a(IA, 8, 8 + na), a(IA, 16, 16 + na)
+        ts(uu, a(IA, 0, na), 4095, A.bitwise_and)
+        tt(a(FA, 896, 896 + na), uu, uu, A.mult)
+        ts(ba, a(FA, 896, 896 + na), 1.0 / 16, A.mult, -0.25 if t == 0 else a("AC", 1, 2), A.add)
+        tt(fa(0), a(R, RI, RI + cl), v, A.mult)
+        ts(a3("IH" + s), fa(0), K53, A.add)
+        listing(c, "IH" + s, 128, None)
+        xw = XW if t == 0 else a("X")
+        for i, (lo, w) in enumerate(pieces(c)):
+            xc, d = a("XC" + s, 16 * lo, 16 * (lo + w)), a(PD[i % 2], 0, 16 * w)
+            either("sv"[i % 2], xc, ind(xw, a(OU, lo, lo + w)))
+            h, r = divmod(i, na // pa)
+            mm(d, [(ID, xc), (a("ZT" + s, p=2 * w, p0=64 * r), a("E", 512 * h, 512 * h + 16 * w, p=2 * w, p0=64 * r))])
+            act(a3("AB" + s, lo // 8, (lo + w) // 8), d, F.Abs, 4096.0)
+        for i, (lo, w) in enumerate(pieces(c)):
             if not FUSE[c][i]:
-                gather(HENG[c][i], a("H" + s, 512 * i, 512 * i + 512), ind(XW, a(OU, 96 + 32 * i, 128 + 32 * i)), 1.0)
-        mm(a(PS, 288, 384), [(sel[b], a3("AB" + s, T["AB" + s][:, :, b:256:16], 0, 4, 96)) for b in range(16)])
-        scan(a(FA, 0, 96), a("DK"), a(PS, 288, 384), A.add, A.min)
-        k = a(IA, 48, 54)
-        ts(k, a(FA, 15, 96, 16), K15, A.add)
+                either("s", a("H" + s, 16 * lo, 16 * (lo + w)), ind(XW, a(OU, 128 + lo, 128 + lo + w)))
+        sums(c, a(PK, 0, cl), [], sel, "AB" + s)
+        scan(fa(2), a("DK", 0, cl), a(PK, 0, cl), A.add, A.min)
+        k = a(IA, 24, 24 + na)
+        ts(k, a(FA, 256 + 15, 256 + cl, 16), K15, A.add)
         ts(k, k, 255, A.bitwise_and)
-        tt(k, k, a(UW, 0, 6), A.mult)
-        tt(k, k, a(UW, 8, 14), A.add)
-        ts(a(IA, 256, 262), k, 1023, A.bitwise_and)
-        ts(a(IA, 262, 268), k, 4095, A.bitwise_and)
-        cp(a(OU, 288, 300), a(IA, 256, 268))
-        od, oc = a(OU, 288, 294), a(OU, 294, 300)
-        tt(a(FA, 128, 224), ind(DW, od), v, A.mult)
-        ts(a(IA, 64, 160), a(FA, 128, 224), K53, A.add)
-        ts(a(IA, 64, 160), a(IA, 64, 160), 4095, A.bitwise_and)
-        cp(a(OU, 192, 288), a(IA, 64, 160))
-        for i in range(3):
-            gather(YENG[c][i], a("Y" + s, 16 + 512 * i, 528 + 512 * i), ind(XW, a(OU, 192 + 32 * i, 224 + 32 * i)), 1.0)
-        for i in range(3):
+        tt(k, k, uu, A.mult)
+        tt(k, k, ba, A.add)
+        ts(a(IA, 32, 32 + na), k, 1023, A.bitwise_and)
+        od, oc = a(OU, 384, 384 + na), a(OU, 392, 392 + na)
+        cp(od, a(IA, 32, 32 + na))
+        tt(fa(5), ind(DW, od), v, A.mult)
+        ts(a3("IY" + s), fa(5), K53, A.add)
+        listing(c, "IY" + s, 256, None)
+        for i, (lo, w) in enumerate(pieces(c)):
+            y = a("Y" + s, 16 + 16 * lo, 16 + 16 * (lo + w))
+            either("s", y, ind(XW, a(OU, 256 + lo, 256 + lo + w)))
             if FUSE[c][i]:
-                tt(a("H" + s, 512 * i, 512 * i + 512), ind(XW, a(OU, 96 + 32 * i, 128 + 32 * i)),
-                   a("Y" + s, 16 + 512 * i, 528 + 512 * i), A.subtract)
-        gather("s", a(BA, 512, 608), ind(DW, od), 1.0)
-        gather("s", a(BA, 1184, 1280), ind(XW, oc), 1.0)
-        ts(a(IA, 8, 16), a(IA, 8, 16), 15, A.bitwise_and)
-        ts(a(IA, 16, 40), a(IA, 16, 40), 3, A.bitwise_and)
-        tt(a(B, 0, 32), a(IA, 8, 40), a("CB" + s), A.add)
-        cp(a(OU, 336, 344), a(B, 0, 8))
-        ts(a(B, 40, 48), a(R, NI, NI + 8), 34.0, A.mult, 31.0, A.add)
-        L = a("L0", CL * c, CL * c + CL) if t == 0 else a(R, LI, LI + CL)
+                tt(a("H" + s, 16 * lo, 16 * (lo + w)), ind(XW, a(OU, 128 + lo, 128 + lo + w)), y, A.subtract)
+        ts(a(IA, 40, 40 + na), k, 4095, A.bitwise_and)
+        cp(oc, a(IA, 40, 40 + na))
+        either("s", a(BA, 144, 144 + cl), ind(DW, od))
+        either("s", fa(3), ind(XW, oc), 1.0, 2047.5, C2047)
+        ts(fa(4), z2, 0.5, A.mult, 1023.5, A.add)
+        ts(a(IA, 48, 80), ind(a(IA, 0, 8), a("OFU", 8 + 4 * c, 10 + 4 * c)), 1.0, A.mult)
+        ts(a(IA, 48, 72), a(IA, 48, 72), 3, A.bitwise_and)
+        ts(a(IA, 72, 80), a(IA, 72, 80), 15, A.bitwise_and)
+        tt(a(B, 16, 48), a(IA, 48, 80), a("CB" + s), A.add)
+        cp(a(OU, 400, 408), a(B, 40, 48))
+        ts(a("NB" + s, 0, na), a(R, NI, NI + na), 32.0, A.mult)
+        tt(a("NB" + s, 0, na), a("NB" + s, 0, na), a("EB" + s, 8, 8 + na), A.add)
+        L = a("L0", L0S[c], L0S[c] + cl) if t == 0 else a(R, LI, LI + cl)
+        nw, on = a(R, NI, NI + 16), a("OFU", 16, 16 + na)
         if PPE[c]:
-            pn = a("PS%d" % (3 * c + 1), 0, 96)
-            gather("s", a(BA, 1280, 1376), ind(a(R, NI, NI + 8), ON), 1.0)
-            mm(pn, [(ID, a(BA, 1280, 1376)), (NID, a("KC"))])
-            act(a(BA, 16, 112), pn, F.Relu, 1.0 / 8192)
+            pn = a(PU, 256, 256 + cl)
+            either("s", a(BA, 272, 272 + cl), ind(nw, on))
+            mm(pn, [(ID, a(BA, 272, 272 + cl)), (NID, a("KC", 0, cl))])
+            act(a(BA, 16, 16 + cl), pn, F.Relu)
         else:
-            tt(a(BA, 16, 112), ind(a(R, NI, NI + 8), ON), a("KC"), A.is_gt)
-        if DPE[c]:
-            pd = "PS%d" % (3 * c + 2)
-            mm(a(pd, 96, 192), [(ID, a(R, RI, RI + CL)), (NID, L)])
-            mm(a(pd, 0, 96), [(ID, a(BA, 512, 608)), (NID, L)])
-            act(a(BA, 608, 800), a(pd, 0, 192), scale=1.0 / 8192)
-        else:
-            tt(a(BA, 608, 704), a(BA, 512, 608), L, A.subtract)
-            tt(a(BA, 704, 800), a(R, RI, RI + CL), L, A.subtract)
+            tt(a(BA, 16, 16 + cl), ind(nw, on), a("KC", 0, cl), A.is_gt)
+        mm(a(PU, cl, 2 * cl), [(ID, a(R, RI, RI + cl)), (NID, L)])
+        mm(a(PU, 0, cl), [(ID, a(BA, 144, 144 + cl)), (NID, L)])
+        act(a(BA, 400, 400 + 2 * cl), a(PU, 0, 2 * cl))
 
     def second(t, c):
-        s = str(c)
+        s, cl, na = str(c), CLS[c], CLS[c] // 16
+        XO, ZO, NO, RO, LO, NI, RI, LI, RW = region(cl)
         R = "ST%d%d" % (t, c)
-        PS, FA, IA, OU, BA, B, Y = "PS%d" % (6 + c), "FA" + s, "IA" + s, "OU" + s, "BA" + s, "B" + s, "Y" + s
-        L = a("L0", CL * c, CL * c + CL) if t == 0 else a(R, LI, LI + CL)
-        for i in range(3):
-            y = a(Y, 16 + 512 * i, 528 + 512 * i)
-            for j, (nm, o) in enumerate((("AJ" + s, a(Y, 15 + 512 * i, 527 + 512 * i)), ("AM" + s, a("H" + s, 512 * i, 512 * i + 512)))):
-                d = a("PS%d" % (3 * c + i))
+        PU, PK, FA, IA, OU, BA, B, Y, SC = "PSU" + s, "PSK" + s, "FA" + s, "IA" + s, "OU" + s, "BA" + s, "B" + s, "Y" + s, "SC" + s
+        fa = lambda k: a(FA, 128 * k, 128 * k + cl)
+        L = a("L0", L0S[c], L0S[c] + cl) if t == 0 else a(R, LI, LI + cl)
+        k = 0
+        for i, (lo, w) in enumerate(pieces(c)):
+            y = a(Y, 16 + 16 * lo, 16 + 16 * (lo + w))
+            for j, (nm, o) in enumerate((("AJ" + s, a(Y, 15 + 16 * lo, 15 + 16 * (lo + w))), ("AM" + s, a("H" + s, 16 * lo, 16 * (lo + w))))):
+                out = a3(nm, lo // 8, (lo + w) // 8)
                 if j and FUSE[c][i]:
-                    act(a3(nm, T[nm][:, 2 * i:2 * i + 2, :], i, i + 1, 512), o, F.Abs, 1.0)
+                    act(out, o, F.Abs, BIG)
                     continue
+                d = a("PSD%d" % (2 * c + k % 2), 0, 16 * w)
+                k += 1
                 mm(d, [(ID, y), (NID, o)])
-                act(a3(nm, T[nm][:, 2 * i:2 * i + 2, :], i, i + 1, 512), d, F.Abs, 1.0 / 8192)
-        for a0, a1 in SPLIT[c]:
-            for nm, lo, w, pen in (("AJ" + s, 0, NID, 15), ("AM" + s, 96, ID, 16)):
-                mm(a(PS, lo + 16 * a0, lo + 16 * a1), [(w, a(BA, pen + 16 * a0, pen + 16 * a1))]
-                   + [(sel[b], a3(nm, T[nm][:, a0:a1, 16 * b:16 * b + 16], a0 // 2, a1 // 2, 16 * (a1 - a0))) for b in range(16)])
-        ts(a(BA, 800, 992, 2), a(PS, 0, 96), a("TH", 1, 2), A.is_le, 31.0, A.mult)
-        ts(a(BA, 801, 992, 2), a(PS, 96, 192), a("TH", 0, 1), A.is_gt, 31.0, A.mult)
-        sc = a(BA, 992, 1184)
-        scan(sc, a("D2"), a(BA, 800, 992), A.add, A.min)
-        e = a(IA, 272, 278)
-        tt(e, a(BA, 992 + 31, 1184, 32), a("EB", 8, 14), A.add)
-        ts(e, e, 1, A.arith_shift_right)
-        oe = a(OU, 344, 350)
-        cp(oe, e)
-        yw = a(Y, 16, 1552)
-        ye, pz, HI = a(BA, 320, 416), "PS%d" % (3 * c), a("HI")
-        z = a("Z0", CL * c, CL * c + CL) if t == 0 else a(R, ZI, ZI + CL)
-        if ZPE[c]:
-            gather("s", ye, ind(yw, oe), 1.0)
-            for lo, o in ((0, a(BA, 1184, 1280)), (96, z)):
-                mm(a(pz, lo, lo + 96), [(a("ONE", p=64), a("CT", 192, 288, p=64)), (HI, o), (HI, ye)])
-            ts(a(R, XO, ZO + CL), a(pz, 0, 192), MAGIC, A.add, MAGIC, A.subtract)
-        else:
-            for lo, o, to in ((416, z, ZO), (512, a(BA, 1184, 1280), XO)):
-                tt(a(FA, lo, lo + 96), ind(yw, oe), o, A.add)
-                ts(a(FA, lo, lo + 96), a(FA, lo, lo + 96), 0.5 - 1.0 / 4096, A.mult, MAGIC, A.add)
-                gather("v", a(R, to, to + CL), a(FA, lo, lo + 96), 1.0, -MAGIC)
-        tt(a(IA, 288, 336), ind(sc, OY), a("CAP"), A.min)
-        ts(a(IA, 336, 368), a(IA, 288, 320), 1, A.bitwise_and)
-        tt(a("DE" + s, 0, 6), e, a(B, 8, 14), A.subtract)
-        tt(a(IA, 296, 320), a(IA, 344, 368), a("DE" + s), A.mult)
-        tt(a(FA, 704, 744), a(IA, 296, 336), a(B, 16, 56), A.add)
-        cp(a(OU, 352, 384), a(FA, 712, 744))
-        gather("s", a(R, NO, NO + 8), a(FA, 704, 712), 1.0)
+                act(out, d, F.Abs, BIG)
+        for nm, lo, w, pen, dg, cc in (("AJ" + s, EV - 1, nsel, 15, "DGJ", CJ), ("AM" + s, EV, sel, 16, "DGM", CM)):
+            sums(c, a(PK, lo, lo + 32 * na, 2), [(a("IDH"), cc(cl)), (a(dg), RB(cl)), (a("IDB"), a(BA, pen, pen + cl))], w, nm)
+        scan(rev(SC, 0, 32 * na), rev(PK, EV, EV + 32 * na), rev("OFF" + s, 0, 32 * na), A.min, A.max)
+        sc, oe = a(SC, 0, 32 * na, 32), a(OU, 408, 408 + na)
+        ts(oe, sc, 0.5, A.mult)
+        yw, zn = a(Y, 16), a("ZN%d%d" % (t, c))
+        tt(zn, ind(yw, oe), fa(4), A.add)
         if t < NV - 1:
-            cp(a("NF", 6 * c, 6 * c + 6), a(IA, 336, 342))
-            send(rec, a(R, ZO, NO), a("ST%d%d" % (t + 1, c), ZI, NI), 4 * t + 2 * c)
-            if c == NC - 1:
-                mm(a(PS, 496, 510), [(a("ONE"), a("NF", 0, 14))])
-                rec("v", [lambda q: q.tensor_reduce(T.AC[:], T[PS][:, 496:510], AxisListType.X, A.add, negate=True)],
-                    [a(PS, 496, 510)], [a("AC")], 64 * CY)
-        else:
-            store(T.yz[:, CL * c:CL * c + CL], a(R, ZO, ZO + CL))
-            nn = a(R, NO, NO + 6)
-            fns = [(lambda q, b=b: q.matmul(T[PS][0:8, 400 + b:496:16], T.ID[:, b:128:16], nn[0], True, True)) for b in range(16)]
-            rec("p", fns, [ID, nn], [a(PS, 400, 496)], 16 * 64 * M["pcy"], each=1)
-            act(a("YN", CL * c, CL * c + CL, p=8), a(PS, 400, 496, p=8), scale=1.0 / 8192)
+            send(rec, zn, a3("ZI%d%d" % (t + 1, c)), 4 * t + 2 * c)
+        tt(a("X2" + s, 0, cl), ind(yw, oe), fa(3), A.add)
+        ts(a(R, XO, XO + cl), a("X2" + s, 0, cl), 0.5, A.mult, -1024.0, A.add)
+        tt(a(IA, 80, 112), ind(a(SC, 0, 32 * na), a("OFU", 10 + 4 * c, 12 + 4 * c)), a("NB" + s), A.add)
+        if t < NV - 1:
+            tt(a("NF", 8 * c, 8 * c + na), sc, a(IA, 88, 88 + na), A.is_equal)
+            mm(APS, [(a("ONE"), a("NF", 8 * c + j, 8 * c + j + 1)) for j in range(na)], c == 0, c == NC - 1)
+        ts(a(IA, 136, 136 + na), sc, 0.5, A.mult)
+        ts(a(IA, 112, 136), a(IA, 88, 112), 1, A.bitwise_and)
+        tt(a("DE" + s, 8, 8 + na), a(IA, 136, 136 + na), a(B, 32, 32 + na), A.subtract)
+        tt(a(IA, 88, 112), a(IA, 112, 136), a("DE" + s), A.mult)
+        tt(a(FA, 912, 944), a(IA, 80, 112), a(B, 0, 32), A.add)
+        cp(a(OU, 416, 448), a(FA, 912, 944))
+        either("s", a(R, NO, NO + 8), a(FA, 928, 936))
+        if t == NV - 1:
+            ts(a(R, ZO, ZO + cl), zn, 0.5, A.mult, -1024.0, A.add)
+            store(T.yz[:, L0S[c]:L0S[c] + cl], a(R, ZO, ZO + cl))
+            nn = a(R, NO, NO + na)
+            fns = [(lambda q, b=b: q.matmul(T[PU][0:8, 384 + b:384 + cl:16], T.ID[:, b:128:16], nn[0], True, True)) for b in range(16)]
+            rec("p", fns, [ID, nn], [a(PU, 384, 384 + cl)], 16 * 64 * M["pcy"], each=1, grp=-1 - c)
+            act(a("YN", L0S[c], L0S[c] + cl, p=8), a(PU, 384, 384 + cl, p=8))
             if c == NC - 1:
                 store(T.yn[:], a("YN", p=8))
-        tt(a(BA, 128, 224), ind(TW, a(OU, 368, 374)), a(BA, 608, 704), A.mult)
-        tt(a(BA, 224, 320), ind(TW, a(OU, 376, 382)), a(BA, 704, 800), A.mult)
+        oi = a(OU, 416, 416 + na)
+        m1, m2 = a(BA, 656, 656 + cl), a(BA, 784, 784 + cl)
+        tt(m1, ind(a("TAB", 0, 512), oi), a(BA, 400, 400 + cl), A.mult)
+        tt(m2, ind(a("TAB", 512, 1024), oi), a(BA, 400 + cl, 400 + 2 * cl), A.mult)
         if LPE[c]:
-            pl = a("PS%d" % (3 * c + 1), 0, 96)
-            mm(pl, [(HI, L), (HI, a(BA, 128, 224)), (HI, a(BA, 224, 320))])
-            act(a(R, LO, LO + CL), pl, scale=2.0)
+            pl = a(PU, 0, cl)
+            mm(pl, [(ID, L), (ID, m1), (ID, m2)])
+            act(a(R, LO, LO + cl), pl)
         else:
-            tt(a(BA, 128, 224), a(BA, 128, 224), L, A.add)
-            tt(a(R, LO, LO + CL), a(BA, 128, 224), a(BA, 224, 320), A.add)
-        gather("s", a(R, RO, RO + CL), ind(a(R, LO, RI + CL), a(OU, 360, 366)), 1.0)
+            tt(m1, m1, L, A.add)
+            tt(a(R, LO, LO + cl), m1, m2, A.add)
+        either("s", a(R, RO, RO + cl), ind(a(R, LO, RI + cl), a(OU, 424, 424 + na)))
         if t < NV - 1:
-            send(rec, a(R, NO, LO + CL), a("ST%d%d" % (t + 1, c), NI, LI + CL), 4 * t + 2 * c + 1)
+            send(rec, a(R, NO, LO + cl), a("ST%d%d" % (t + 1, c), NI, LI + cl), 4 * t + 2 * c + 1)
         else:
-            store(T.yl[:, CL * c:CL * c + CL], a(R, LO, LO + CL))
-            store(T.yr[:, CL * c:CL * c + CL], a(R, RO, RO + CL))
+            store(T.yl[:, L0S[c]:L0S[c] + cl], a(R, LO, LO + cl))
+            store(T.yr[:, L0S[c]:L0S[c] + cl], a(R, RO, RO + cl))
 
     def writes(t, c):
-        s = str(c)
+        s, cl, na = str(c), CLS[c], CLS[c] // 16
+        XO, ZO, NO, RO, LO, NI, RI, LI, RW = region(cl)
         R = "ST%d%d" % (t, c)
-        xw = a("X", 1536 * c, 1536 * c + 1536)
-        cp(ind(xw, a("OU" + s, 336, 342)), a(R, XO, XO + CL))
-        dw = a("DL", 0, 768) if c == 0 else a("DL", 768, 1792)
-        cp(ind(dw, a("OU" + s, 352, 358)), a(R, LO, LO + CL))
+        xw, ox = a("X", 16 * L0S[c], 16 * (L0S[c] + cl)), a("OU" + s, 400, 400 + na)
+        cp(ind(xw, ox), a(R, XO, XO + cl))
+        if c == 0 and t < NV - 1:
+            cp(ind(a("X", 4096), ox), a(R, XO, XO + cl))
+        dw = a("DL", 0, 2 * D0) if c == 0 else a("DL", 2 * D0)
+        cp(ind(dw, a("OU" + s, 440, 440 + na)), a(R, LO, LO + cl))
         if t == NV - 1:
-            store(T.yx[:, 1536 * c:1536 * c + 1536], xw)
-            store(T.yd[:, 384 * c:384 * c + 384], a("DL", 384 + 384 * c, 768 + 384 * c))
+            store(T.yx[:, 16 * L0S[c]:16 * (L0S[c] + cl)], xw)
+            store(T.yd[:, 4 * L0S[c]:4 * (L0S[c] + cl)], a("DL", D0 + 4 * L0S[c], D0 + 4 * (L0S[c] + cl)))
 
     def part(f, t, c):
         k = len(ops)
         f(t, c)
         for j in range(k, len(ops)):
-            ops[j]["key"] = (f is not first, c, j - k + (100 if f is writes else 0), t)
+            ops[j]["key"] = ((first, second, writes).index(f), c, (j - k) / (len(ops) - k), t)
 
     for t in range(NV):
         for c in range(NC):
@@ -475,20 +538,23 @@ def depend(ops):
                         continue
                     if (kind or k2) and lo < h2 and l2 < hi:
                         d.add(j)
-                    elif n.startswith("PS") and ops[j]["e"] != o["e"]:
+                    elif n.startswith("PS") and (ops[j]["e"] != o["e"] or o["e"] == "p"):
                         d.add(j)
         for kind, lst in ((0, o["r"]), (1, o["w"])):
             for n, lo, hi in lst:
                 acc.setdefault(n, []).append((i, kind, lo, hi))
         deps.append(d)
-    anc = []
+    done, issued = [], []
     for i, d in enumerate(deps):
-        m, keep = 0, set()
+        m, q, keep = 0, 0, set()
         for j in sorted(d, reverse=True):
-            if not m >> j & 1:
+            soft = ops[i]["e"] == "p" == ops[j]["e"]
+            if not (m | q if soft else m) >> j & 1:
                 keep.add(j)
-                m |= anc[j]
-        anc.append(1 << i if ops[i]["e"] == "net" else m | 1 << i)
+                m |= done[j] & ~(1 << j) if soft and ops[i]["grp"] != ops[j]["grp"] else done[j]
+                q |= issued[j] if soft else 0
+        done.append(1 << i if ops[i]["e"] == "net" else m | 1 << i)
+        issued.append(q | 1 << i)
         deps[i] = keep
     return deps
 
@@ -503,7 +569,7 @@ def place(ops, before, seq, hop, back):
         t = 0.0
         e = o["e"]
         for j in before[i]:
-            x = end[j] + hop[ops[j]["e"] == e]
+            x = end[j] if e == "p" == ops[j]["e"] else end[j] + hop
             if x > t:
                 t = x
         if back:
@@ -551,7 +617,7 @@ def replay(ops, deps, order, hop):
         e = o["e"]
         t = free.get(e, 0.0)
         for j in deps[i]:
-            x = fin[j] + hop[ops[j]["e"] == e]
+            x = fin[j] if e == "p" == ops[j]["e"] else fin[j] + hop
             if x > t:
                 t = x
         if o["e"] != "net":
@@ -560,16 +626,11 @@ def replay(ops, deps, order, hop):
     return fin
 
 
-GUESS = {(0, 0): ((9, -3), (13, 0), (19, 2.5), (27, 0.5), (40, 3), (43, 6), (46, 7), (99, 8)),
-         (0, 1): ((19, 3.3), (27, 5), (40, 8), (43, 11), (46, 13), (99, 12)),
-         (1, 0): ((11, 7), (200, 10)), (1, 1): ((11, 12), (200, 16))}
-
-
 def guess(o, i):
     if "key" not in o:
         return -1e6 + i
-    ph, c, j, t = o["key"]
-    return 1000.0 * (22 * t + [v for lim, v in GUESS[(int(ph), c)] if j < lim][0]) + j
+    ph, c, x, t = o["key"]
+    return 1000.0 * (18 * t + 4 * c + (-3 + 11 * x, 8 + 5 * x, 13)[ph])
 
 
 def put(ops, i, e):
@@ -577,7 +638,7 @@ def put(ops, i, e):
     ops[i]["fns"], ops[i]["cost"] = ops[i]["alt"][e]
 
 
-def plan(all_ops, deps, rounds, seed, start=None):
+def plan(all_ops, deps, rounds, seed, start):
     ops, hop = all_ops[0]
     n = len(ops)
     users = [[] for _ in ops]
@@ -605,7 +666,7 @@ def plan(all_ops, deps, rounds, seed, start=None):
         for o, h in all_ops:
             put(o, i, e)
 
-    st, end = forward(start or [float(i) for i in range(n)])
+    st, end = forward(start)
     best = score(st)
     cur, cs = st, best[0]
     for r in range(rounds):
@@ -615,14 +676,13 @@ def plan(all_ops, deps, rounds, seed, start=None):
             a = rnd() * max(key)
             w, amp = 2000 + 5000 * rnd(), 500 + 5000 * rnd() ** 2
             key = [k + amp * (rnd() - 0.5) if a <= k <= a + w else k for k in key]
-            if rnd() < 0.3:
+            if rnd() < 0.4:
                 fl = [i for i in flex if a <= cur[i] <= a + w and rnd() < 0.25]
         for i in fl:
             flip(i)
         st, end = forward(key)
-        for _ in range(1 if rnd() < FB[0] else 0):
-            bs, be = place(ops, users, in_order(users, deps, [-e for e in end]), hop, True)
-            st, end = forward([-e for e in be])
+        bs, be = place(ops, users, in_order(users, deps, [-e for e in end]), hop, True)
+        st, end = forward([-e for e in be])
         s = score(st)
         if s[0] <= cs + 300:
             cur, cs = st, s[0]
@@ -666,7 +726,7 @@ def rank_program(g, core, T, topo):
     need = set()
     for final in (False, True):
         known = {e: 0 for e in Q}
-        clos, sig, last, cnt, val, waited = {}, {}, {}, {e: 0 for e in Q}, {}, {}
+        clos, sig, last, cnt, val, waited, group = {}, {}, {}, {e: 0 for e in Q}, {}, {}, {}
         stores = 0
         for i in order:
             o = ops[i]
@@ -675,7 +735,7 @@ def rank_program(g, core, T, topo):
                 clos[i], sig[i] = 1 << i, o["sem"]
                 val[o["sem"][0]] = o["sem"][1]
                 continue
-            want = sorted(deps[i], key=lambda j: -pos[j])
+            want = sorted((j for j in deps[i] if not e == "p" == ops[j]["e"]), key=lambda j: -pos[j])
             if "sem" in o:
                 sig[i] = o["sem"]
             elif final and i in need:
@@ -693,6 +753,9 @@ def rank_program(g, core, T, topo):
                         Q[e].wait_ge(T.sem[sig[j][0]], sig[j][1])
                         waited[sig[j][0]] = max(waited.get(sig[j][0], 0), sig[j][1])
             clos[i] = known[e] | 1 << i
+            if e == "p":
+                group[o["grp"]] = group.get(o["grp"], 0) | 1 << i
+                clos[i] |= group[o["grp"]]
             if i in sig:
                 val[sig[i][0]] = sig[i][1]
             if final:

@@ -34,7 +34,7 @@ for _n, _c, _d in (
         ("IS", 16, "float32"), ("Z8", 144, "float32"), ("E8", 128, "float32"), ("E", 1024, "bfloat16"),
         ("ID", 128, "bfloat16"), ("NID", 128, "bfloat16"), ("IDB", 128, "bfloat16"), ("ZS", 144, "bfloat16"), ("NZS", 144, "bfloat16"),
         ("WZ", 144, "float16"), ("WB", 128, "float16"), ("NH", 128, "float16"), ("IDH", 128, "float16"),
-        ("DGM", 128, "float16"), ("DGJ", 128, "float16"), ("CH", 512, "float16"),
+        ("DGM", 128, "float16"), ("DGJ", 128, "float16"), ("CH", 640, "float16"), ("XO", EXT, "bfloat16"),
         ("BLK", 128, "bfloat16"), ("ONE", 128, "bfloat16"), ("CT", 256, "bfloat16"),
         ("DG", 32, "bfloat16"), ("KF", 16, "float32"), ("DS", 16, "float32"), ("DK", 128, "float32"), ("OF", 24, "float32"),
         ("OFU", 24, "uint16"), ("TAB", 1024, "bfloat16"), ("LN", 8, "float32"),
@@ -45,7 +45,7 @@ for _c in range(NC):
     for _n, _w, _d in (
             ("CB", 32, "float32"), ("B", 48, "float32"), ("DE", 24, "float32"), ("NB", 32, "float32"), ("EB", 16, "float32"),
             ("FA", 1024, "float32"), ("OFF", 256, "float32"), ("SC", 256, "float32"),
-            ("IA", 160, "int32"), ("IH", [_na, 16], "int32"), ("IY", [_na, 16], "int32"), ("OU", 448, "uint16"), ("BA", 1040, "bfloat16"),
+            ("IA", 416, "int32"), ("IH", [_na, 16], "int32"), ("IY", [_na, 16], "int32"), ("OU", 448, "uint16"), ("BA", 1040, "bfloat16"),
             ("ZT", 128, "bfloat16"), ("X2", 128, "float16"),
             ("XC", _w16, "bfloat16"), ("H", _w16, "bfloat16"), ("Y", _w16 + 16, "bfloat16"),
             ("AB", [2 * _na, 128], "bfloat16"), ("AM", [2 * _na, 128], "bfloat16"), ("AJ", [2 * _na, 128], "bfloat16")):
@@ -60,10 +60,11 @@ for _b in ("D0", "D1", "D2", "D3", "K0", "K1", "U0", "U1"):
 NSEM = {"v": 44, "s": 30, "p": 30, "g": 11}
 SEMAPHORES = [e + str(i) for e in NSEM for i in range(NSEM[e])] + ["ld%d" % i for i in range(13)] \
     + ["ar%d" % i for i in range(8)] + ["sent", "st"]
-M = dict(cy=0.83, pcy=0.45, hop=210.0, ov=0.0, ga=1.56, sc=3.8, rl=2500.0, rb=30.0)
-MODELS = [dict(M), dict(cy=0.9, pcy=0.5, hop=170.0, ov=0.0, ga=1.25, sc=2.5, rl=3200.0, rb=22.0),
-          dict(cy=1.05, pcy=0.6, hop=260.0, ov=0.0, ga=1.85, sc=5.0, rl=2500.0, rb=30.0)]
-ROUNDS = [2500, 3]
+M = dict(cy=0.83, pcy=0.43, hop=202.0, ov=0.0, ga=1.56, sc=3.8, rl=1200.0, rb=17.0, r1=2600.0, ld=1840.0, lb=256.0)
+MODELS = [dict(M), dict(cy=0.9, pcy=0.5, hop=170.0, ov=0.0, ga=1.25, sc=2.5, rl=2000.0, rb=30.0, r1=3500.0, ld=1600.0, lb=200.0),
+          dict(cy=1.05, pcy=0.6, hop=260.0, ov=0.0, ga=1.85, sc=5.0, rl=1800.0, rb=22.0, r1=2000.0, ld=2000.0, lb=230.0)]
+ROUNDS = [600, 3, 60000]
+HEAT = [2500.0]
 _PLAN = {}
 
 
@@ -120,6 +121,17 @@ def build(g, T, send):
         else:
             f = lambda q: q.tensor_scalar(out[0], i[0], u(s1), u(s2), o0, o1)
         rec("v", [f], [i, s1, s2], [out], vc(out, [i]))
+        if plain(out, i, s1, s2) and (o0, o1) in ((A.mult, None), (A.add, None), (A.mult, A.add)):
+            act(out, i, scale=s1 if o0 == A.mult else 1.0, bias=s1 if o0 == A.add else s2 if o1 else 0.0)
+            also()
+
+    def plain(*xs):
+        return all(x[3] in ("float32", "bfloat16") and not x[1][0][0].startswith("PS") for x in xs if isinstance(x, tuple))
+
+    def also(e=None):
+        o2, o1 = ops.pop(), ops[-1]
+        o1["alt"] = {o1["e"]: (o1["fns"], o1["cost"]), o2["e"]: (o2["fns"], o2["cost"])}
+        put(ops, len(ops) - 1, e or o1["e"])
 
     def tt(out, i0, i1, op):
         sb = not (i0[1][0][0].startswith("PS") or i1[1][0][0].startswith("PS"))
@@ -129,29 +141,34 @@ def build(g, T, send):
         w = (out[0], out[1][:1]) if out[4] else out
         rd = [i] + ([(0, out[1][1:])] if out[4] else [])
         rec("v", [lambda q: q.tensor_copy(out[0], i[0])], rd, [w], vc(out, [i]))
+        if plain(out, i) and not out[4]:
+            act(out, i)
+            also()
 
-    def ms(out, val, v=False):
-        if not v and val == int(val) and abs(val) <= 256 and out[3] in ("float32", "bfloat16"):
-            return iota(out, [[0, out[2]]], int(val), 0)
+    def ms(out, val):
         rec("v", [lambda q: q.memset(out[0], val)], [], [out], vc(out, [out]))
+        if val == int(val) and abs(val) <= 256 and plain(out):
+            iota(out, [[0, out[2]]], int(val), 0)
+            also()
 
     def scan(out, d0, d1, o0, o1):
         rec("v", [lambda q: q.tensor_tensor_scan(out[0], d0[0], d1[0], 0.0, o0, o1)], [d0, d1], [out], vc(out, [d0, d1]))
 
     def act(out, i, fn=F.Identity, scale=1.0, bias=0.0):
-        c = (78 + M["ga"] * out[2]) * CY if i[4] else max(64, out[2] + 30) * CY
-        rec("s", [lambda q: q.activation(out[0], i[0], fn, bias=u(bias), scale=scale)], [i, bias], [out], c)
+        c = (78 + M["ga"] * out[2]) * CY if i[4] else max(64, out[2] + 8) * CY
+        rec("s", [lambda q: q.activation(out[0], i[0], fn, bias=u(bias), scale=u(scale))], [i, bias, scale], [out], c)
 
     groups = {None: 0}
 
-    def mm(out, pairs, first=True, last=True):
+    def mm(out, pairs, first=True, last=True, whole=None):
         k = len(pairs)
+        key = (whole or out)[1][0]
         if first:
             groups[None] += 1
-            groups[out[1][0]] = groups[None]
+            groups[key] = groups[None]
         fns = [(lambda q, j=j: q.matmul(out[0], pairs[j][0][0], pairs[j][1][0], first and j == 0, last and j == k - 1)) for j in range(k)]
         c = sum(max(64, r[2]) * (4 if r[3] == "float32" else 1) for l, r in pairs) * M["pcy"] + 30
-        rec("p", fns, [x for pr in pairs for x in pr], [out], c, grp=groups[out[1][0]])
+        rec("p", fns, [x for pr in pairs for x in pr], [out], c, grp=groups[key])
 
     def iota(out, pat, base=0, cm=0):
         if out[3] == "int32":
@@ -163,18 +180,17 @@ def build(g, T, send):
     nld = [0]
 
     def load(e, out, src, ns):
-        rec(e, [lambda q: q.dma_start(out[0], src)], [], [out], 60, lat=ns, sem=("ld%d" % nld[0], 16), dma=1)
+        rec(e, [lambda q: q.dma_start(out[0], src)], [], [out], 60, lat=ns, sem=("ld%d" % nld[0], 16), dma=1, dq=local(out[2]))
         nld[0] += 1
 
-    def store(dst, i):
-        rec("y", [lambda q: q.dma_start(dst, i[0])], [i], [], 60 + 128 * 2 * i[2] / 150.0, lat=2000, store=1)
+    def local(cols):
+        return M["ld"], 160 + 128 * 2 * cols / M["lb"]
 
-    def either(e, out, i, scale=1.0, bias=0.0, bcol=0.0):
+    def store(dst, i):
+        rec("y", [lambda q: q.dma_start(dst, i[0])], [i], [], 60, lat=sum(local(i[2])), store=1, dq=local(i[2]))
+
+    def either(e, out, i, scale=1.0, bias=0.0):
         ts(out, i, scale, A.mult, bias, A.add)
-        act(out, i, scale=scale, bias=bcol)
-        os_, ov = ops.pop(), ops[-1]
-        ov["r"] = os_["r"]
-        ov["alt"] = {"v": (ov["fns"], ov["cost"]), "s": (os_["fns"], os_["cost"])}
         put(ops, len(ops) - 1, e)
 
     D0 = 4 * CLS[0]
@@ -188,8 +204,8 @@ def build(g, T, send):
     load("s", a("CNI", p=8), T.cnt[:], 2600)
     load("s", a("LMI", p=8), T.lim[:], 2600)
     load("y", a("DL", D0, D0 + 1024), T.donor[:], 8500)
-    load("y", a("L0"), T.lend[:], 9000)
-    load("y", a("X", 4096, 4096 + EXT), T.stock[:, 0:EXT], 11000)
+    load("y", a("X", 4096, 4096 + EXT), T.stock[:, 0:EXT], 10500)
+    load("y", a("L0"), T.lend[:], 11000)
     iota(a("PI", 0, 1), [[0, 1]], 0, 1)
     iota(a("IB"), [[16, 8], [0, 16]])
     iota(a("IC"), [[1, 144]])
@@ -207,13 +223,12 @@ def build(g, T, send):
     cp(a("PF", 0, 6), a("PI", 0, 6))
     col = lambda j: a("PF", j, j + 1)
     PP, PB, G16, P64, P7, P8, W32, W2, KP, K4, KQ, K53, K1, K2, K15, CW, C1024, C2047 = [col(j) for j in range(18)]
-    ts(W32, a("WI"), 1.0 / 32, A.mult)
     ts(W2, a("WI"), 0.5, A.mult)
     cp(KP, a("KI"))
     ts(K4, a("KI"), 2.0, A.mult, -4.0, A.add)
     ts(KQ, KP, KP, A.mult, -4.0, A.mult)
     ts(KQ, KQ, -0.25, A.add)
-    ts(a("WB"), a("IB"), G16, A.is_equal, W32, A.mult)
+    ts(a("WB"), a("IB"), G16, A.is_equal, W2, A.mult)
     ts(a("ID"), a("IC", 0, 128), PP, A.is_equal)
     ts(a("NH"), a("ID"), -0.5, A.mult)
     ts(a("ZS"), a("IC"), G16, A.subtract, 15.0, A.is_equal)
@@ -221,15 +236,14 @@ def build(g, T, send):
     ts(a("E", 512, 1024), a("E", 0, 512), 8.0, A.add, P64, A.is_equal)
     ts(a("E", 0, 512), a("E", 0, 512), P64, A.is_equal)
     ms(a("ONE"), 1.0)
-    ms(a("CT", 0, 128, p=32), -4.0)
-    ms(a("CT", 0, 128, p=32, p0=32), 1.0 / 1024)
-    ms(a("CT", 128, 256, p=64), 1.0 / 64)
-    NEG, RB, CM, CJ = [lambda n, k=k: a("CH", 128 * k, 128 * k + n) for k in range(4)]
-    ms(NEG(128), -2048.0)
-    ms(RB(128), BIG)
-    ms(CM(128), -2040.0)
-    ms(CJ(128), 2041.0)
-    ms(a("CH", 384, 512, 16), -60000.0)
+    ms(a("CT", 0, 128, p=32), -64.0)
+    ms(a("CT", 0, 128, p=32, p0=32), 1.0 / 64)
+    ms(a("CT", 128, 256, p=64), 0.25)
+    ms(a("CH", 0, 256), -2048.0)
+    ms(a("CH", 256, 384), BIG)
+    ms(a("CH", 384, 640, 2), 2041.0)
+    ms(a("CH", 385, 640, 2), -2040.0)
+    ms(a("CH", 384, 640, 32), -60000.0)
     ms(C1024, 1024.0)
     ms(C2047, 2047.5)
     ts(a("BLK"), a("IB"), G16, A.is_equal)
@@ -238,7 +252,7 @@ def build(g, T, send):
     mm(a("PSD2", 0, 17), [(a("BLK"), a("DG", 0, 17))])
     cp(a("KF"), a("PSD2", 0, 16))
     ts(CW, a("PSD2", 16, 17), -1024.0, A.mult)
-    ts(K53, PB, 53.0, A.mult, -15.0 / 32, A.add)
+    ts(K53, PB, 53.0, A.mult)
     ts(K1, PB, 2.0, A.mult, 1.0, A.add)
     ts(K2, PB, 2.0, A.mult)
     ts(a("OF", 0, 8), a("IS", 0, 8), 0.0, A.mult, PB, A.add)
@@ -267,7 +281,7 @@ def build(g, T, send):
         ts(T0, P8, 16.0 * na, A.mult)
         ts(T1, P7, 16.0, A.mult, T0, A.add)
         ts(EB, a("IS", 0, 8), 128.0, A.mult, T1, A.add)
-        ts(a("EB" + s, 8, 16), EB, -2.0, A.mult)
+        ts(a("B" + s, 0, 8), EB, -2.0, A.mult)
         ts(T0, T1, 2.0, A.mult)
         iota(a(OFF, 0, 32 * na), [[256, na], [2, 16], [0, 2]])
         ts(a(OFF, 0, 32 * na), a(OFF, 0, 32 * na), T0, A.add)
@@ -277,7 +291,6 @@ def build(g, T, send):
         ts(a("CB" + s, 8, 16), LN, 4.0, A.mult, float(D0) if c == 0 else 0.0, A.add)
         cp(a("CB" + s, 16, 24), EB)
         ts(a("CB" + s, 24, 32), LN, 16.0, A.mult)
-        ms(a("B" + s, 0, 8), 0.0)
         cp(a("B" + s, 8, 16), LN)
         ms(a("DE" + s, 0, 8), float(RI - LO))
         ms(a("DE" + s, 8, 16), 0.0)
@@ -289,7 +302,7 @@ def build(g, T, send):
         ms(a("BA" + s, 0, 16), 0.0)
         ms(a("ST0" + s, NI, RI), 0.0)
         ms(a("PSK" + s, EV + 32 * na - 1, EV + 32 * na), -1e6)
-        ms(a("PSD%d" % (2 * c + 1), 0, 128), 0.0, True)
+        ms(a("PSD%d" % (2 * c + 1), 0, 128), 0.0)
         for t in range(NV - 1):
             ms(a("ST%d%d" % (t, c), NO + 8, RO), 0.0)
         ts(a3("ZI0" + s), a("Z0", L0S[c], L0S[c] + cl), 2.0, A.mult, 2048.0, A.add)
@@ -315,9 +328,9 @@ def build(g, T, send):
     ts(a("INN"), a("INN"), PB, A.is_le)
     tt(a("TAB", 0, 512), a("ICO"), a("INN"), A.mult)
     store(T.yx[:, 3072:4096], a("X", 3072, 4096))
-    rec("y", [lambda q: q.dma_start(T.yd[:, 768:1024], T.donor[:, 768:1024])], [a("L0")], [], 60, lat=2500, store=1)
+    rec("y", [lambda q: q.dma_start(T.yd[:, 768:1024], T.donor[:, 768:1024])], [a("L0")], [], 60, lat=2500, store=1, dq=local(256))
 
-    XW, DW = a("X", 0, 4096), a("DL", D0, D0 + 1024)
+    XW, XE, DW = a("X", 0, 4096), a("X"), a("DL", D0, D0 + 1024)
     sel = [a("ZS", 15 - b, 143 - b) for b in range(16)]
     nsel = [a("NZS", 15 - b, 143 - b) for b in range(16)]
     ID, NID = a("ID"), a("NID")
@@ -329,7 +342,6 @@ def build(g, T, send):
 
     def listing(c, I, lo, add):
         na = CLS[c] // 16
-        ts(a3(I), a3(I), 4095, A.bitwise_and)
         for h in range(2):
             o = a("OU%d" % c, lo + 8 * na * h, lo + 8 * na * (h + 1))
             if add is None:
@@ -337,12 +349,9 @@ def build(g, T, send):
             else:
                 ts(o, a3(I, 0, na, 8 * h, 8 * h + 8), add, A.add)
 
-    def sums(c, out, head, w, nm):
+    def sums(c, out, w, nm, h, first, last, whole=None):
         na = CLS[c] // 16
-        if head:
-            mm(out, head, True, False)
-        for h in range(2):
-            mm(out, [(w[8 * h + b], a3(nm, h * na, h * na + na, 16 * b, 16 * b + 16)) for b in range(8)], not head and h == 0, h == 1)
+        mm(out, [(w[8 * h + b], a3(nm, h * na, h * na + na, 16 * b, 16 * b + 16)) for b in range(8)], first, last, whole)
 
     def first(t, c):
         s, cl, na, pa = str(c), CLS[c], CLS[c] // 16, PA[c]
@@ -352,14 +361,16 @@ def build(g, T, send):
         PD = ["PSD%d" % (2 * c), "PSD%d" % (2 * c + 1)]
         fa = lambda k: a(FA, 128 * k, 128 * k + cl)
         one, z2 = a("ONE", p=64), a3(Z)
+        pu = a(PU, 0, 256)
+        mm(pu, [(a("WB"), a("CH", 0, 256)), (one, a("CT", p=64))], True, False)
         for k in range(2):
-            mm(a(PU, 128 * k, 128 * k + cl), [(a("WB"), NEG(cl)), (one, a("CT", 128 * k, 128 * k + cl, p=64))], True, False)
-            mm(a(PU, 128 * k, 128 * k + cl), [(a("WB"), z2)], False, True)
+            mm(a(PU, 128 * k, 128 * k + cl), [(a("WB"), z2)], False, k == 1, pu)
         v = fa(1)
-        ts(fa(0), a(PU, 0, cl), 3221225472.0, A.add, 3221225472.0, A.subtract)
+        ts(fa(0), a(PU, 0, cl), 51539607552.0, A.add, 51539607552.0, A.subtract)
         tt(v, a(PU, 128, 128 + cl), fa(0), A.subtract)
-        act(fa(2), v, F.Square, 4.0, K4)
+        act(fa(2), v, F.Square, 0.25, K4)
         ts(a3("IY" + s), fa(2), KQ, A.add)
+        ts(a3("IY" + s), a3("IY" + s), 4095, A.bitwise_and)
         listing(c, "IY" + s, 0, None if t == 0 else APS if c == 0 else a("AC", 0, 1))
         if t and c == 0:
             ts(a("AC", 0, 1), APS, 0.0, A.add)
@@ -373,20 +384,20 @@ def build(g, T, send):
         ts(uu, a(IA, 0, na), 4095, A.bitwise_and)
         tt(a(FA, 896, 896 + na), uu, uu, A.mult)
         ts(ba, a(FA, 896, 896 + na), 1.0 / 16, A.mult, -0.25 if t == 0 else a("AC", 1, 2), A.add)
-        tt(fa(0), a(R, RI, RI + cl), v, A.mult)
-        ts(a3("IH" + s), fa(0), K53, A.add)
-        listing(c, "IH" + s, 128, None)
-        xw = XW if t == 0 else a("X")
+        tt(a(IA, 160, 160 + cl), a(R, RI, RI + cl), v, A.mult)
+        ts(a3("IH" + s), a(IA, 160, 160 + cl), 4, A.logical_shift_right, 4095, A.bitwise_and)
+        listing(c, "IH" + s, 128, K53)
         for i, (lo, w) in enumerate(pieces(c)):
-            xc, d = a("XC" + s, 16 * lo, 16 * (lo + w)), a(PD[i % 2], 0, 16 * w)
-            either("sv"[i % 2], xc, ind(xw, a(OU, lo, lo + w)))
+            xc, d = a("XC" + s, 16 * lo, 16 * (lo + w)), a((PD[0], PD[1], PU, PD[0])[i], 0, 16 * w)
+            either("sv"[i % 2], xc, ind(XW if t == 0 else XE, a(OU, lo, lo + w)))
             h, r = divmod(i, na // pa)
             mm(d, [(ID, xc), (a("ZT" + s, p=2 * w, p0=64 * r), a("E", 512 * h, 512 * h + 16 * w, p=2 * w, p0=64 * r))])
             act(a3("AB" + s, lo // 8, (lo + w) // 8), d, F.Abs, 4096.0)
         for i, (lo, w) in enumerate(pieces(c)):
             if not FUSE[c][i]:
-                either("s", a("H" + s, 16 * lo, 16 * (lo + w)), ind(XW, a(OU, 128 + lo, 128 + lo + w)))
-        sums(c, a(PK, 0, cl), [], sel, "AB" + s)
+                either("s", a("H" + s, 16 * lo, 16 * (lo + w)), ind(XE, a(OU, 128 + lo, 128 + lo + w)))
+        for h in range(2):
+            sums(c, a(PK, 0, cl), sel, "AB" + s, h, h == 0, h == 1)
         scan(fa(2), a("DK", 0, cl), a(PK, 0, cl), A.add, A.min)
         k = a(IA, 24, 24 + na)
         ts(k, a(FA, 256 + 15, 256 + cl, 16), K15, A.add)
@@ -396,26 +407,25 @@ def build(g, T, send):
         ts(a(IA, 32, 32 + na), k, 1023, A.bitwise_and)
         od, oc = a(OU, 384, 384 + na), a(OU, 392, 392 + na)
         cp(od, a(IA, 32, 32 + na))
-        tt(fa(5), ind(DW, od), v, A.mult)
-        ts(a3("IY" + s), fa(5), K53, A.add)
-        listing(c, "IY" + s, 256, None)
+        tt(a(IA, 288, 288 + cl), ind(DW, od), v, A.mult)
+        ts(a3("IY" + s), a(IA, 288, 288 + cl), 4, A.logical_shift_right, 4095, A.bitwise_and)
+        listing(c, "IY" + s, 256, K53)
         for i, (lo, w) in enumerate(pieces(c)):
             y = a("Y" + s, 16 + 16 * lo, 16 + 16 * (lo + w))
-            either("s", y, ind(XW, a(OU, 256 + lo, 256 + lo + w)))
+            either("s", y, ind(XE, a(OU, 256 + lo, 256 + lo + w)))
             if FUSE[c][i]:
-                tt(a("H" + s, 16 * lo, 16 * (lo + w)), ind(XW, a(OU, 128 + lo, 128 + lo + w)), y, A.subtract)
+                tt(a("H" + s, 16 * lo, 16 * (lo + w)), ind(XE, a(OU, 128 + lo, 128 + lo + w)), y, A.subtract)
         ts(a(IA, 40, 40 + na), k, 4095, A.bitwise_and)
         cp(oc, a(IA, 40, 40 + na))
         either("s", a(BA, 144, 144 + cl), ind(DW, od))
-        either("s", fa(3), ind(XW, oc), 1.0, 2047.5, C2047)
+        either("s", fa(3), ind(XW, oc), 1.0, C2047)
         ts(fa(4), z2, 0.5, A.mult, 1023.5, A.add)
         ts(a(IA, 48, 80), ind(a(IA, 0, 8), a("OFU", 8 + 4 * c, 10 + 4 * c)), 1.0, A.mult)
         ts(a(IA, 48, 72), a(IA, 48, 72), 3, A.bitwise_and)
         ts(a(IA, 72, 80), a(IA, 72, 80), 15, A.bitwise_and)
         tt(a(B, 16, 48), a(IA, 48, 80), a("CB" + s), A.add)
         cp(a(OU, 400, 408), a(B, 40, 48))
-        ts(a("NB" + s, 0, na), a(R, NI, NI + na), 32.0, A.mult)
-        tt(a("NB" + s, 0, na), a("NB" + s, 0, na), a("EB" + s, 8, 8 + na), A.add)
+        either("s", a("NB" + s, 0, na), a(R, NI, NI + na), 32.0)
         L = a("L0", L0S[c], L0S[c] + cl) if t == 0 else a(R, LI, LI + cl)
         nw, on = a(R, NI, NI + 16), a("OFU", 16, 16 + na)
         if PPE[c]:
@@ -448,8 +458,13 @@ def build(g, T, send):
                 k += 1
                 mm(d, [(ID, y), (NID, o)])
                 act(out, d, F.Abs, BIG)
-        for nm, lo, w, pen, dg, cc in (("AJ" + s, EV - 1, nsel, 15, "DGJ", CJ), ("AM" + s, EV, sel, 16, "DGM", CM)):
-            sums(c, a(PK, lo, lo + 32 * na, 2), [(a("IDH"), cc(cl)), (a(dg), RB(cl)), (a("IDB"), a(BA, pen, pen + cl))], w, nm)
+        ev, pj, pm = a(PK, EV - 1, EV - 1 + 32 * na), a(PK, EV - 1, EV - 1 + 32 * na, 2), a(PK, EV, EV + 32 * na, 2)
+        mm(ev, [(a("IDH"), a("CH", 384, 384 + 2 * cl))], True, False)
+        for out, dg, pen in ((pj, "DGJ", 15), (pm, "DGM", 16)):
+            mm(out, [(a(dg), a("CH", 256, 256 + cl)), (a("IDB"), a(BA, pen, pen + cl))], False, False, ev)
+        for h in range(2):
+            sums(c, pj, nsel, "AJ" + s, h, False, False, ev)
+            sums(c, pm, sel, "AM" + s, h, False, h == 1, ev)
         scan(rev(SC, 0, 32 * na), rev(PK, EV, EV + 32 * na), rev("OFF" + s, 0, 32 * na), A.min, A.max)
         sc, oe = a(SC, 0, 32 * na, 32), a(OU, 408, 408 + na)
         ts(oe, sc, 0.5, A.mult)
@@ -484,7 +499,7 @@ def build(g, T, send):
         tt(m1, ind(a("TAB", 0, 512), oi), a(BA, 400, 400 + cl), A.mult)
         tt(m2, ind(a("TAB", 512, 1024), oi), a(BA, 400 + cl, 400 + 2 * cl), A.mult)
         if LPE[c]:
-            pl = a(PU, 0, cl)
+            pl = a(PK, 0, cl)
             mm(pl, [(ID, L), (ID, m1), (ID, m2)])
             act(a(R, LO, LO + cl), pl)
         else:
@@ -502,6 +517,10 @@ def build(g, T, send):
         XO, ZO, NO, RO, LO, NI, RI, LI, RW = region(cl)
         R = "ST%d%d" % (t, c)
         xw, ox = a("X", 16 * L0S[c], 16 * (L0S[c] + cl)), a("OU" + s, 400, 400 + na)
+        if c == 0 and t == NV - 1:
+            rec("y", [lambda q, x=xw: q.dma_start(T.XO[:], x[0])], [xw, a("ST%d1" % t, region(CLS[1])[5])], [a("XO")], 60,
+                lat=3500, sem=("ld%d" % nld[0], 16), dma=1, late=1, dq=local(EXT))
+            xw = a("XO")
         cp(ind(xw, ox), a(R, XO, XO + cl))
         if c == 0 and t < NV - 1:
             cp(ind(a("X", 4096), ox), a(R, XO, XO + cl))
@@ -653,7 +672,7 @@ def plan(all_ops, deps, rounds, seed, start):
         return x[0] / 2147483648.0
 
     def forward(key):
-        key = [-1e9 + i if ops[i].get("dma") else key[i] for i in range(n)]
+        key = [-1e9 + i if ops[i].get("dma") and not ops[i].get("late") else key[i] for i in range(n)]
         return place(ops, deps, in_order(deps, users, key), hop, False)
 
     def score(st):
@@ -662,7 +681,7 @@ def plan(all_ops, deps, rounds, seed, start):
         return r[0] + sum(r), order, r, [ops[i]["e"] for i in flex], st
 
     def flip(i):
-        e = "s" if ops[i]["e"] == "v" else "v"
+        e = [x for x in ops[i]["alt"] if x != ops[i]["e"]][0]
         for o, h in all_ops:
             put(o, i, e)
 
@@ -691,7 +710,148 @@ def plan(all_ops, deps, rounds, seed, start):
                 flip(i)
         if s[0] < best[0]:
             best = s
-    return deps, best[1], dict(zip(flex, best[3])), best[2], best[4]
+    for i, e in zip(flex, best[3]):
+        for o, h in all_ops:
+            put(o, i, e)
+    return refine(all_ops, deps, users, best[1], ROUNDS[2], rnd)
+
+
+def refine(all_ops, deps, users, order, rounds, rnd):
+    ops = all_ops[0][0]
+    n = len(ops)
+    QN = {"v": 0, "s": 1, "p": 2, "g": 3, "y": 4, "net": 5}
+    eng = [QN[o["e"]] for o in ops]
+    flex = [sum(QN[e] for e in o["alt"]) if "alt" in o else 0 for o in ops]
+    fixed = [bool(o.get("dma")) and not o.get("late") for o in ops]
+    ms = []
+    for mo, hop in all_ops:
+        dl = [[(j, 0.0 if ops[i]["e"] == "net" or ops[i]["e"] == "p" == ops[j]["e"] else hop) for j in deps[i]] for i in range(n)]
+        cost = [{QN[e]: o["alt"][e][1] for e in o["alt"]} if "alt" in o else [o["cost"]] * 6 for o in mo]
+        ms.append((dl, cost, [o.get("dq") for o in mo]))
+
+    def run(m, order, trace=False):
+        dl, cost, dq = m
+        free, fin, de = [0.0] * 6, [0.0] * n, 0.0
+        st, why, last, dlast = [0.0] * n, [None] * n, [None] * 6, None
+        for i in order:
+            e = eng[i]
+            t = free[e]
+            w = -1
+            for j, h in dl[i]:
+                x = fin[j] + h
+                if x > t:
+                    t = x
+                    w = j
+            f = t + cost[i][e]
+            if e < 5:
+                free[e] = f
+            if trace:
+                st[i], why[i] = t, (w, last[e])
+                last[e] = i
+            q = dq[i]
+            if q:
+                f += q[0]
+                if de > f:
+                    f = de
+                    if trace:
+                        why[i] = (dlast, None)
+                de = f = f + q[1]
+                dlast = i
+            fin[i] = f
+        return (max(fin), fin, st, why) if trace else max(fin)
+
+    def score(order, limit=1e18):
+        r = [run(ms[0], order)]
+        if r[0] > limit:
+            return 1e18, r
+        r += [run(m, order) for m in ms[1:]]
+        return r[0] + sum(r), r
+
+    def chain(order):
+        end, fin, st, why = run(ms[int(rnd() * len(ms))], order, True)
+        i, out = fin.index(end), []
+        while i is not None:
+            w, prev = why[i]
+            out.append((i, prev if w == -1 else None))
+            i = prev if w == -1 else w
+        return out
+
+    def ahead(order, pos, u, v):
+        a, b = pos[u], pos[v]
+        mark = {v}
+        for k in range(b - 1, a - 1, -1):
+            i = order[k]
+            if any(x in mark for x in users[i]):
+                if i == u:
+                    return None
+                mark.add(i)
+        mid = order[a:b + 1]
+        return order[:a] + [i for i in mid if i in mark] + [i for i in mid if i not in mark] + order[b + 1:]
+
+    def behind(order, pos, u, v):
+        a, b = pos[u], pos[v]
+        mark = {u}
+        for k in range(a + 1, b + 1):
+            i = order[k]
+            if any(x in mark for x in deps[i]):
+                if i == v:
+                    return None
+                mark.add(i)
+        mid = order[a:b + 1]
+        return order[:a] + [i for i in mid if i not in mark] + [i for i in mid if i in mark] + order[b + 1:]
+
+    def tidy(order):
+        st = run(ms[0], order, True)[2]
+        pos = {i: k for k, i in enumerate(order)}
+        order = sorted(order, key=lambda i: (st[i], pos[i]))
+        return order, {i: k for k, i in enumerate(order)}
+
+    order, pos = tidy(order)
+    cs, r = score(order)
+    best = (cs, order, list(eng), r)
+    ch = chain(order)
+    for k in range(rounds):
+        heat = HEAT[0] * (1.0 - k / rounds) * rnd() ** 2
+        v, u = ch[int(rnd() * len(ch))]
+        x, new, fl = rnd(), None, None
+        if x < 0.25:
+            fl = v if flex[v] else u if u is not None and flex[u] else None
+            if fl is None:
+                continue
+            eng[fl] = flex[fl] - eng[fl]
+            new = order
+        elif u is None or fixed[u] or fixed[v]:
+            continue
+        elif x < 0.65:
+            p = pos[u]
+            for _ in range(int(rnd() ** 2 * 4)):
+                p2 = p - 1
+                while p2 >= 0 and eng[order[p2]] != eng[v]:
+                    p2 -= 1
+                if p2 >= 0 and not fixed[order[p2]]:
+                    p = p2
+            new = ahead(order, pos, order[p], v)
+        else:
+            p = pos[v]
+            for _ in range(int(rnd() ** 2 * 4)):
+                p2 = p + 1
+                while p2 < n and eng[order[p2]] != eng[v]:
+                    p2 += 1
+                if p2 < n:
+                    p = p2
+            new = behind(order, pos, u, order[p])
+        if new is None:
+            continue
+        s, r2 = score(new, r[0] + heat)
+        if s <= cs + heat:
+            order, pos = tidy(new)
+            cs, r = score(order)
+            ch = chain(order)
+            if cs < best[0]:
+                best = (cs, order, list(eng), r)
+        elif fl is not None:
+            eng[fl] = flex[fl] - eng[fl]
+    return deps, best[1], {i: "vspg"[best[2][i]] for i in range(n) if flex[i]}, best[3]
 
 
 def rank_program(g, core, T, topo):
@@ -706,8 +866,9 @@ def rank_program(g, core, T, topo):
 
     def send(rec, i, out, k):
         sent[0] += n_out
-        j = rec("g", [lambda q: q.remote_dma(out[0], i[0], T.sem["ar%d" % k], T.sem.sent, pid, rid, mask)], [i], [], 300, remote=1)
-        rec("net", [], [], [out], 0, lat=M["rl"] + 128 * 2 * i[2] / M["rb"], after=[j], sem=("ar%d" % k, n_in))
+        j = rec("g", [lambda q: q.remote_dma(out[0], i[0], T.sem["ar%d" % k], T.sem.sent, pid, rid, mask)], [i], [], 300 if k else M["r1"], remote=1)
+        rec("net", [], [], [out], 0, lat=M["rl"] + 128 * 2 * i[2] / M["rb"], after=[j], sem=("ar%d" % k, n_in),
+            dq=(M["rl"], 128 * 2 * i[2] / M["rb"]))
 
     ops = build(g, T, send)
     if not _PLAN:

@@ -3,20 +3,15 @@ from concourse.mybir import dt, AluOpType, AxisListType, ActivationFunctionType
 A = AluOpType
 F = ActivationFunctionType
 NV, SHIFT, NC = 3, 3, 2
-CLS = [96, 96]
-PA = [3, 3]
-FUSE = [[1, 1, 1, 1], [1, 1, 1, 1]]
-LPE = [True, True]
-PPE = [True, True]
-L0S = [0, CLS[0]]
-EXT = 16 * CLS[0]
+Q, CL, NA, PA = 192, 96, 6, 3
+PW = 8 * PA
+EXT = 16 * CL
+FUSE = [((0, 0, 1, 1), (1, 1, 1, 1))] + [((1, 1, 1, 1), (1, 1, 1, 1))] * 2
+YCUT = ((0, 24), (24, 48), (48, 96))
+HINT = [1, 1, 0]
 BIG = 8192.0
-EV = 130
-
-
-def region(cl):
-    return 0, cl, 2 * cl, 2 * cl + 16, 3 * cl + 16, 4 * cl + 16, 4 * cl + 32, 5 * cl + 32, 6 * cl + 32
-
+EV = 98
+XO, ZO, NO, RO, LO, NI, RI, LI, RW = 0, 192, 384, 400, 592, 784, 800, 992, 1184
 
 SCRATCH = {}
 
@@ -26,45 +21,47 @@ def _buf(name, cols, dtype, where="sbuf"):
 
 
 for _n, _c, _d in (
-        ("X", 4096 + EXT, "bfloat16"), ("DL", 1024 + 4 * sum(CLS), "bfloat16"), ("Z0", 192, "bfloat16"), ("L0", 192, "bfloat16"),
-        ("WI", 1, "int32"), ("KI", 1, "int32"), ("CNI", 192, "int32"), ("LMI", 2, "int32"),
-        ("CNF", 192, "float32"), ("LMF", 2, "float32"), ("TH", 4, "float32"),
-        ("PI", 8, "int32"), ("PF", 32, "float32"), ("IC", 144, "bfloat16"), ("IB", 128, "bfloat16"),
-        ("ICO", 512, "bfloat16"), ("INN", 512, "bfloat16"), ("IPA", 512, "bfloat16"), ("KC", 128, "bfloat16"),
-        ("IS", 16, "float32"), ("Z8", 144, "float32"), ("E8", 128, "float32"), ("E", 1024, "bfloat16"),
+        ("X", 4096 + EXT, "bfloat16"), ("XO", EXT, "bfloat16"), ("DL", 1024 + 4 * Q, "bfloat16"), ("Z0", Q, "bfloat16"),
+        ("WI", 256, "int32"), ("WR", 272, "bfloat16"), ("CNI", Q, "int32"), ("LMI", 2, "int32"),
+        ("CNF", Q, "bfloat16"), ("LMF", 2, "float32"), ("TH", 4, "float32"),
+        ("PI", 8, "int32"), ("PF", 24, "float32"), ("IC", 144, "bfloat16"), ("IB", 128, "bfloat16"),
+        ("ICO", 512, "bfloat16"), ("INN", 512, "bfloat16"), ("KC", Q, "bfloat16"),
+        ("IS", 12, "float32"), ("Z8", 144, "bfloat16"), ("E8", 128, "float32"), ("E", 768, "bfloat16"),
         ("ID", 128, "bfloat16"), ("NID", 128, "bfloat16"), ("IDB", 128, "bfloat16"), ("ZS", 144, "bfloat16"), ("NZS", 144, "bfloat16"),
         ("WZ", 144, "float16"), ("WB", 128, "float16"), ("NH", 128, "float16"), ("IDH", 128, "float16"),
-        ("DGM", 128, "float16"), ("DGJ", 128, "float16"), ("CH", 640, "float16"), ("XO", EXT, "bfloat16"),
-        ("BLK", 128, "bfloat16"), ("ONE", 128, "bfloat16"), ("CT", 256, "bfloat16"),
-        ("DG", 32, "bfloat16"), ("KF", 16, "float32"), ("DS", 16, "float32"), ("DK", 128, "float32"), ("OF", 24, "float32"),
-        ("OFU", 24, "uint16"), ("TAB", 1024, "bfloat16"), ("LN", 8, "float32"),
-        ("NF", 16, "bfloat16"), ("AC", 2, "float32"), ("YN", 192, "float32")):
+        ("DGM", 128, "float16"), ("DGJ", 128, "float16"), ("CH", 480, "float16"),
+        ("BLK", 128, "bfloat16"), ("ONE", 128, "bfloat16"), ("CT", Q, "bfloat16"),
+        ("DG", 32, "bfloat16"), ("KF", 16, "float32"), ("DS", 16, "float32"), ("DK", Q, "float32"), ("OF", 32, "float32"),
+        ("OFU", 32, "uint16"), ("TAB", 1024, "bfloat16"), ("LN", 12, "float32"), ("OFF", Q, "float32"),
+        ("NF", 12, "bfloat16"), ("AC", 2, "float32"), ("YN", Q, "float32"),
+        ("CB", 48, "float32"), ("B", [6, 12], "float32"), ("DE", [3, 12], "float32"), ("NB", 112, "float32"), ("FO", 48, "float32"),
+        ("SC", 2 * Q, "float32"), ("XH", Q, "float32"), ("IL", 224, "int32"), ("OL", 96, "uint16"), ("BA", 1168, "bfloat16")):
     _buf(_n, _c, _d)
 for _c in range(NC):
-    _na, _w16 = CLS[_c] // 16, 16 * CLS[_c]
     for _n, _w, _d in (
-            ("CB", 32, "float32"), ("B", 48, "float32"), ("DE", 24, "float32"), ("NB", 32, "float32"), ("EB", 16, "float32"),
-            ("FA", 1024, "float32"), ("OFF", 256, "float32"), ("SC", 256, "float32"),
-            ("IA", 416, "int32"), ("IH", [_na, 16], "int32"), ("IY", [_na, 16], "int32"), ("OU", 448, "uint16"), ("BA", 1040, "bfloat16"),
-            ("ZT", 128, "bfloat16"), ("X2", 128, "float16"),
-            ("XC", _w16, "bfloat16"), ("H", _w16, "bfloat16"), ("Y", _w16 + 16, "bfloat16"),
-            ("AB", [2 * _na, 128], "bfloat16"), ("AM", [2 * _na, 128], "bfloat16"), ("AJ", [2 * _na, 128], "bfloat16")):
+            ("FA", 400, "float32"), ("IA", 2 * CL, "int32"), ("IH", [NA, 16], "int32"), ("IY", [NA, 16], "int32"), ("OU", 296, "uint16"),
+            ("ZT", 128, "bfloat16"), ("X2", CL, "float16"),
+            ("XC", 16 * CL, "bfloat16"), ("H", 16 * CL, "bfloat16"), ("Y", 16 * CL + 16, "bfloat16"),
+            ("AB", [2 * NA, 128], "bfloat16"), ("AM", [2 * NA, 128], "bfloat16"), ("AJ", [CL, 16], "bfloat16")):
         _buf(_n + str(_c), _w, _d)
     for _t in range(NV):
-        _buf("ST%d%d" % (_t, _c), region(CLS[_c])[8], "bfloat16")
-        _buf("ZI%d%d" % (_t, _c), [_na, 16], "float16")
-        _buf("ZN%d%d" % (_t, _c), CLS[_c], "float16")
+        _buf("ZI%d%d" % (_t, _c), [NA, 16], "float16")
+        _buf("ZN%d%d" % (_t, _c), CL, "float16")
+for _t in range(NV):
+    _buf("ST%d" % _t, RW, "bfloat16")
 for _b in ("D0", "D1", "D2", "D3", "K0", "K1", "U0", "U1"):
-    _buf("PS" + _b, 512, "float32", "psum")
+    _buf("PS" + _b, [32, 16] if _b[0] == "D" else 512, "float32", "psum")
 
-NSEM = {"v": 44, "s": 30, "p": 30, "g": 11}
-SEMAPHORES = [e + str(i) for e in NSEM for i in range(NSEM[e])] + ["ld%d" % i for i in range(13)] \
-    + ["ar%d" % i for i in range(8)] + ["sent", "st"]
-M = dict(cy=0.83, pcy=0.43, hop=202.0, ov=0.0, ga=1.56, sc=3.8, rl=1200.0, rb=17.0, r1=2600.0, ld=1840.0, lb=256.0)
-MODELS = [dict(M), dict(cy=0.9, pcy=0.5, hop=170.0, ov=0.0, ga=1.25, sc=2.5, rl=2000.0, rb=30.0, r1=3500.0, ld=1600.0, lb=200.0),
-          dict(cy=1.05, pcy=0.6, hop=260.0, ov=0.0, ga=1.85, sc=5.0, rl=1800.0, rb=22.0, r1=2000.0, ld=2000.0, lb=230.0)]
-ROUNDS = [600, 3, 60000]
-HEAT = [2500.0]
+NSEM = {"v": 46, "s": 30, "p": 30, "g": 11}
+SEMAPHORES = [e + str(i) for e in NSEM for i in range(NSEM[e])] + ["ld%d" % i for i in range(11)] \
+    + ["ar%d" % i for i in range(10)] + ["sent", "st"]
+M = dict(cy=0.83, pcy=0.43, hop=215.0, ga=1.56, sc=3.8, rl=700.0, rb=50.0, r1=2200.0, ld=1200.0, lb=280.0)
+MODELS = [dict(M), dict(cy=0.95, pcy=0.5, hop=200.0, ga=1.7, sc=4.5, rl=1400.0, rb=18.0, r1=3200.0, ld=2000.0, lb=150.0),
+          dict(cy=1.05, pcy=0.58, hop=320.0, ga=1.4, sc=3.8, rl=1000.0, rb=35.0, r1=2600.0, ld=1400.0, lb=230.0),
+          dict(cy=0.85, pcy=0.44, hop=200.0, ga=1.56, sc=3.8, rl=1400.0, rb=16.0, r1=2800.0, ld=1900.0, lb=240.0)]
+WEIGHTS = [1.0, 1.0, 1.0, 1.0]
+ROUNDS, STARTS = [300, 7, 11000], [1, 2]
+TRIES, REST, BACK, NOISE = 16, 14, 1000, 200.0
 _PLAN = {}
 
 
@@ -84,12 +81,13 @@ def build(g, T, send):
         ap = T[n][:, hi - 1:lo - 1:-1] if lo else T[n][:, hi - 1::-1]
         return (ap, ((n, lo, hi),), hi - lo, SCRATCH[n][2], None)
 
-    def a3(n, r0=0, r1=None, c0=0, c1=None):
+    def a3(n, r0=0, r1=None, c0=0, c1=None, st=1, p=128, p0=0):
         rows, w = SCRATCH[n][1][1:]
         r1 = rows if r1 is None else r1
         c1 = w if c1 is None else c1
-        rng = ((n, r0 * w, r1 * w),) if (c0, c1) == (0, w) else tuple((n, r * w + c0, r * w + c1) for r in range(r0, r1))
-        return (T[n][:, r0:r1, c0:c1], rng, (r1 - r0) * (c1 - c0), SCRATCH[n][2], None)
+        rng = ((n, r0 * w, r1 * w),) if 2 * (c1 - c0) > w else tuple((n, r * w + c0, r * w + c1) for r in range(r0, r1, st))
+        ap = T[n][p0:p0 + p, r0:r1:st, c0:c1] if st > 1 else T[n][p0:p0 + p, r0:r1, c0:c1]
+        return (ap, rng, len(range(r0, r1, st)) * (c1 - c0), SCRATCH[n][2], None)
 
     def ind(win, off):
         return (win[0].indirect(off[0]), win[1] + off[1], 16 * off[2], win[3], "ind")
@@ -101,7 +99,7 @@ def build(g, T, send):
                 r += list(x[1])
         for x in wr:
             w += list(x[1])
-        ops.append(dict(e=e, fns=fns, r=r, w=w, cost=cost + (M["ov"] if e in "vs" else 0), **kw))
+        ops.append(dict(e=e, fns=fns, r=r, w=w, cost=cost, **kw))
         return len(ops) - 1
 
     def u(x):
@@ -128,10 +126,9 @@ def build(g, T, send):
     def plain(*xs):
         return all(x[3] in ("float32", "bfloat16") and not x[1][0][0].startswith("PS") for x in xs if isinstance(x, tuple))
 
-    def also(e=None):
+    def also():
         o2, o1 = ops.pop(), ops[-1]
         o1["alt"] = {o1["e"]: (o1["fns"], o1["cost"]), o2["e"]: (o2["fns"], o2["cost"])}
-        put(ops, len(ops) - 1, e or o1["e"])
 
     def tt(out, i0, i1, op):
         sb = not (i0[1][0][0].startswith("PS") or i1[1][0][0].startswith("PS"))
@@ -145,9 +142,9 @@ def build(g, T, send):
             act(out, i)
             also()
 
-    def ms(out, val):
+    def ms(out, val, v=False):
         rec("v", [lambda q: q.memset(out[0], val)], [], [out], vc(out, [out]))
-        if val == int(val) and abs(val) <= 256 and plain(out):
+        if not v and val == int(val) and abs(val) <= 256 and plain(out):
             iota(out, [[0, out[2]]], int(val), 0)
             also()
 
@@ -179,53 +176,53 @@ def build(g, T, send):
 
     nld = [0]
 
-    def load(e, out, src, ns):
-        rec(e, [lambda q: q.dma_start(out[0], src)], [], [out], 60, lat=ns, sem=("ld%d" % nld[0], 16), dma=1, dq=local(out[2]))
-        nld[0] += 1
-
     def local(cols):
         return M["ld"], 160 + 128 * 2 * cols / M["lb"]
 
-    def store(dst, i):
-        rec("y", [lambda q: q.dma_start(dst, i[0])], [i], [], 60, lat=sum(local(i[2])), store=1, dq=local(i[2]))
+    def load(e, out, src, ns, cols=None, after=(), **kw):
+        rec(e, [lambda q: q.dma_start(out[0], u(src))], [src] + list(after), [out], 60, lat=ns, sem=("ld%d" % nld[0], 16), dma=1,
+            dq=local(out[2] if cols is None else cols), **kw)
+        nld[0] += 1
 
-    def either(e, out, i, scale=1.0, bias=0.0):
-        ts(out, i, scale, A.mult, bias, A.add)
-        put(ops, len(ops) - 1, e)
+    def store(dst, i, after=()):
+        cols = dst.shape[1]
+        rec("y", [lambda q: q.dma_start(dst, u(i))], [i] + list(after), [], 60, lat=sum(local(cols)), store=1, dq=local(cols))
 
-    D0 = 4 * CLS[0]
     load("y", a("Z0"), T.zed[:], 2200)
-    load("s", a("WI"), T.wt[:], 2200)
-    load("s", a("KI"), T.kap[:], 2300)
+    load("s", a("WI", 0, 128, p=1), T.wt[:], 2200, -60)
+    load("s", a("WI", 128, 256, p=1), T.kap[:], 2300, -60)
+    load("y", a("LMI", p=8), T.lim[:], 2600, -60)
+    load("s", a("CNI", p=8), T.cnt[:], 2600, -60)
     load("y", a("X", 0, 4096), T.stock[:], 7000)
-    for c in range(NC):
-        RI = region(CLS[c])[6]
-        load("s", a("ST0%d" % c, RI, RI + CLS[c]), T.rend[:, L0S[c]:L0S[c] + CLS[c]], 2500)
-    load("s", a("CNI", p=8), T.cnt[:], 2600)
-    load("s", a("LMI", p=8), T.lim[:], 2600)
-    load("y", a("DL", D0, D0 + 1024), T.donor[:], 8500)
+    load("s", a("ST0", RI, RI + Q), T.rend[:], 7500)
+    load("y", a("DL", 0, 1024), T.donor[:], 8500)
     load("y", a("X", 4096, 4096 + EXT), T.stock[:, 0:EXT], 10500)
-    load("y", a("L0"), T.lend[:], 11000)
+    load("y", a("ST0", LI, LI + Q), T.lend[:], 11000)
     iota(a("PI", 0, 1), [[0, 1]], 0, 1)
     iota(a("IB"), [[16, 8], [0, 16]])
     iota(a("IC"), [[1, 144]])
-    iota(a("IS", 0, 8), [[1, 8]])
-    iota(a("E", 0, 512), [[16, 4], [1, 8], [0, 16]])
-    iota(a("KC"), [[0, 8], [1, 16]])
+    iota(a("IS"), [[1, 12]])
+    iota(a("E", 0, 384), [[16, PA], [1, 8], [0, 16]])
+    iota(a("KC"), [[0, 12], [1, 16]])
     iota(a("Z8", p=8), [[1, 144]], -15, -16)
     iota(a("E8", p=8), [[16, 8], [0, 16]], 0, -16)
+    iota(a("OFF"), [[256, NA], [2, 16], [0, 2]])
     iota(a("ICO"), [[0, 16], [1, 32]])
     iota(a("INN"), [[1, 16], [0, 32]])
-    iota(a("IPA"), [[0, 256], [-1, 2]], 1)
     p0 = a("PI", 0, 1)
     for j, m in ((1, 15), (2, 112), (3, 63), (4, 7), (5, 8)):
         ts(a("PI", j, j + 1), p0, m, A.bitwise_and)
     cp(a("PF", 0, 6), a("PI", 0, 6))
     col = lambda j: a("PF", j, j + 1)
-    PP, PB, G16, P64, P7, P8, W32, W2, KP, K4, KQ, K53, K1, K2, K15, CW, C1024, C2047 = [col(j) for j in range(18)]
-    ts(W2, a("WI"), 0.5, A.mult)
-    cp(KP, a("KI"))
-    ts(K4, a("KI"), 2.0, A.mult, -4.0, A.add)
+    PP, PB, G16, P64, P7, P8, W2, KP, K4, KQ, K53, K1, K2, K15, CW, C1024, C2047, T0, T1, T2 = [col(j) for j in range(20)]
+    ms(a("WR", 256, 257, p=1), 1.0, True)
+    cp(a("WR", 0, 256, p=1), a("WI", p=1))
+    for j in range(2):
+        mm(a("PSK1", 440 + j, 441 + j), [(a("WR", 128 * j, 128 * j + 128, p=1), a("WR", 256, 257, p=1))])
+    ts(W2, a("PSK1", 440, 441), 0.5, A.mult)
+    cp(KP, a("PSK1", 441, 442))
+    cp(a("DG", 16, 17), a("PSK1", 440, 441))
+    ts(K4, KP, 2.0, A.mult, -4.0, A.add)
     ts(KQ, KP, KP, A.mult, -4.0, A.mult)
     ts(KQ, KQ, -0.25, A.add)
     ts(a("WB"), a("IB"), G16, A.is_equal, W2, A.mult)
@@ -233,141 +230,134 @@ def build(g, T, send):
     ts(a("NH"), a("ID"), -0.5, A.mult)
     ts(a("ZS"), a("IC"), G16, A.subtract, 15.0, A.is_equal)
     ts(a("WZ"), a("ZS"), W2, A.mult)
-    ts(a("E", 512, 1024), a("E", 0, 512), 8.0, A.add, P64, A.is_equal)
-    ts(a("E", 0, 512), a("E", 0, 512), P64, A.is_equal)
+    ts(a("E", 384, 768), a("E", 0, 384), 8.0, A.add, P64, A.is_equal)
+    ts(a("E", 0, 384), a("E", 0, 384), P64, A.is_equal)
     ms(a("ONE"), 1.0)
-    ms(a("CT", 0, 128, p=32), -64.0)
-    ms(a("CT", 0, 128, p=32, p0=32), 1.0 / 64)
-    ms(a("CT", 128, 256, p=64), 0.25)
-    ms(a("CH", 0, 256), -2048.0)
-    ms(a("CH", 256, 384), BIG)
-    ms(a("CH", 384, 640, 2), 2041.0)
-    ms(a("CH", 385, 640, 2), -2040.0)
-    ms(a("CH", 384, 640, 32), -60000.0)
+    ms(a("CT", 0, CL, p=32), -64.0)
+    ms(a("CT", 0, CL, p=32, p0=32), 1.0 / 64)
+    ms(a("CT", CL, Q, p=64), 0.25)
+    ms(a("CH", 0, 192), -2048.0)
+    ms(a("CH", 192, 288), BIG)
+    ms(a("CH", 288, 480, 2), 2041.0)
+    ms(a("CH", 289, 480, 2), -2040.0)
+    ms(a("CH", 288, 480, 32), -60000.0)
     ms(C1024, 1024.0)
     ms(C2047, 2047.5)
     ts(a("BLK"), a("IB"), G16, A.is_equal)
     ts(a("DG", 0, 16), a("KC", 0, 16), PB, A.is_equal, KP, A.mult)
-    cp(a("DG", 16, 17), a("WI"))
-    mm(a("PSD2", 0, 17), [(a("BLK"), a("DG", 0, 17))])
-    cp(a("KF"), a("PSD2", 0, 16))
-    ts(CW, a("PSD2", 16, 17), -1024.0, A.mult)
+    mm(a("PSK1", 416, 433), [(a("BLK"), a("DG", 0, 17))])
+    cp(a("KF"), a("PSK1", 416, 432))
+    ts(CW, a("PSK1", 432, 433), -1024.0, A.mult)
     ts(K53, PB, 53.0, A.mult)
     ts(K1, PB, 2.0, A.mult, 1.0, A.add)
     ts(K2, PB, 2.0, A.mult)
-    ts(a("OF", 0, 8), a("IS", 0, 8), 0.0, A.mult, PB, A.add)
-    for c in range(NC):
-        lo = 8 + 4 * c
-        ts(a("OF", lo, lo + 2), a("IS", 0, 2), 0.0, A.mult, P7, A.add)
-        ts(a("OF", lo, lo + 2), a("OF", lo, lo + 2), CLS[c] // 16 - 1.0, A.min)
-        ts(a("OF", lo + 2, lo + 4), a("OF", lo, lo + 2), 32.0, A.mult)
-    cp(a("OF", 16, 24), a("IS", 0, 8))
+    LN, EB = a("LN"), a("CB", 24, 36)
+    ts(LN, a("IS"), 16.0, A.mult, PB, A.add)
+    ts(a("OF", 0, 6), a("IS", 0, 6), 0.0, A.mult, PB, A.add)
+    ts(a("PI", 5, 8), a("LN", 0, 3), -5.5, A.add, 1.0 / 12, A.mult)
+    ms(a("OF", 6, 16), 0.0)
+    ts(a("OF", 12, 15), a("PI", 5, 8), -12.0, A.mult)
+    tt(a("OF", 8, 11), a("OF", 12, 15), a("LN", 0, 3), A.add)
+    ts(a("OF", 12, 15), a("OF", 8, 11), 32.0, A.mult)
+    ts(a("OF", 30, 32), a("OF", 8, 10), 6.0, A.is_ge, -192.0, A.mult)
+    tt(a("OF", 28, 30), a("OF", 12, 14), a("OF", 30, 32), A.add)
+    cp(a("OF", 16, 28), a("IS"))
     cp(a("OFU"), a("OF"))
     ms(a("DS", 0, 1), 33554432.0)
     tt(a("DS", 1, 16), a("KF", 0, 15), a("KF", 1, 16), A.subtract)
     ts(a("DS", 1, 16), a("DS", 1, 16), -256.0, A.add)
-    act(a("DK"), ind(a("DS"), a("OFU", 0, 8)))
-    ts(K15, a("KF", 15, 16), 3840.0, A.add)
+    act(a("DK", 0, CL), ind(a("DS"), a("OFU", 0, 6)))
+    ms(a("DK", CL, Q), -256.0)
+    ms(a("DK", CL, Q, 16), 33554432.0)
+    ts(K15, a("KF", 15, 16), 16.0, A.mult)
     ts(a("NID"), a("ID"), -1.0, A.mult)
     ts(a("IDB"), a("ID"), 134217728.0, A.mult)
     ts(a("IDH"), a("ID"), BIG, A.mult)
     ts(a("NZS"), a("ZS"), -1.0, A.mult)
-    LN = a("LN")
-    ts(LN, a("IS", 0, 8), 16.0, A.mult, PB, A.add)
+    ts(T0, P8, 16.0 * NA, A.mult)
+    ts(T1, P7, 16.0, A.mult, T0, A.add)
+    ts(T2, T1, 2.0, A.mult)
     for c in range(NC):
-        s, na, cl = str(c), CLS[c] // 16, CLS[c]
-        XO, ZO, NO, RO, LO, NI, RI, LI, RW = region(cl)
-        EB, T0, T1, OFF = a("EB" + s, 0, 8), col(20 + 2 * c), col(21 + 2 * c), "OFF" + s
-        ts(T0, P8, 16.0 * na, A.mult)
-        ts(T1, P7, 16.0, A.mult, T0, A.add)
-        ts(EB, a("IS", 0, 8), 128.0, A.mult, T1, A.add)
-        ts(a("B" + s, 0, 8), EB, -2.0, A.mult)
-        ts(T0, T1, 2.0, A.mult)
-        iota(a(OFF, 0, 32 * na), [[256, na], [2, 16], [0, 2]])
-        ts(a(OFF, 0, 32 * na), a(OFF, 0, 32 * na), T0, A.add)
-        ts(a(OFF, 1, 32 * na, 2), a(OFF, 1, 32 * na, 2), 0.75, A.add)
-        ts(a(OFF, 31, 32 * na, 32), a(OFF, 31, 32 * na, 32), -0.125, A.add)
-        ms(a("CB" + s, 0, 8), 1.0)
-        ts(a("CB" + s, 8, 16), LN, 4.0, A.mult, float(D0) if c == 0 else 0.0, A.add)
-        cp(a("CB" + s, 16, 24), EB)
-        ts(a("CB" + s, 24, 32), LN, 16.0, A.mult)
-        cp(a("B" + s, 8, 16), LN)
-        ms(a("DE" + s, 0, 8), float(RI - LO))
-        ms(a("DE" + s, 8, 16), 0.0)
-        ms(a("DE" + s, 16, 24), -float(D0) if c == 0 else 1024.0 - D0)
-        ms(a("NB" + s, 0, 8), 0.0)
-        ms(a("NB" + s, 8, 32), -0.2)
-        ms(a("IA" + s, 0, 8), 0)
+        ts(a("CB", 24 + NA * c, 30 + NA * c), a("IS", 0, NA), 128.0, A.mult, T1, A.add)
+    ts(a("OFF"), a("OFF"), T2, A.add)
+    ts(a("OFF", 1, Q, 2), a("OFF", 1, Q, 2), 0.75, A.add)
+    ts(a("OFF", 31, Q, 32), a("OFF", 31, Q, 32), -0.125, A.add)
+    ms(a("CB", 0, 12), 1.0)
+    ts(a("CB", 12, 24), LN, 4.0, A.mult)
+    ts(a("CB", 36, 48), LN, 16.0, A.mult)
+    ts(a3("B", 0, 1), EB, -2.0, A.mult)
+    cp(a3("B", 1, 2), LN)
+    ms(a3("DE", 0, 1), float(RI - LO))
+    ms(a3("DE", 2, 3), 1024.0)
+    ms(a("NB", 12), -0.2)
+    ms(a("ST%d" % (NV - 1), LO + CL, NI), 0.0)
+    ms(a("BA", 0, 16), 0.0)
+    ms(a("ST0", NI + 8, RI), 0.0)
+    for t in range(NV - 1):
+        ms(a("ST%d" % t, NO + 8, RO), 0.0)
+    for c in range(NC):
+        s = str(c)
         ms(a("Y" + s, 0, 16), 0.0)
-        ms(a("BA" + s, 0, 16), 0.0)
-        ms(a("ST0" + s, NI, RI), 0.0)
-        ms(a("PSK" + s, EV + 32 * na - 1, EV + 32 * na), -1e6)
-        ms(a("PSD%d" % (2 * c + 1), 0, 128), 0.0)
-        for t in range(NV - 1):
-            ms(a("ST%d%d" % (t, c), NO + 8, RO), 0.0)
-        ts(a3("ZI0" + s), a("Z0", L0S[c], L0S[c] + cl), 2.0, A.mult, 2048.0, A.add)
-    ms(a("DL", 0, D0), 0.0)
-    ms(a("DL", D0 + 1024), 0.0)
+        ms(a("PSK" + s, EV + Q - 1, EV + Q), -1e6)
+        ms(a3("PSD%d" % (2 * c + 1), 0, 8), 0.0)
+        ms(a3("AJ" + s, 0, CL, 0, 2), 0.0, True)
+        ts(a3("ZI0" + s), a("Z0", CL * c, CL * c + CL), 2.0, A.mult, 2048.0, A.add)
+    ms(a("DL", 1024), 0.0)
     ts(a("Z8", p=8), a("Z8", p=8), 0.0, A.is_equal)
     ts(a("E8", p=8), a("E8", p=8), 0.0, A.is_equal)
     cp(a("CNF", p=8), a("CNI", p=8))
     cp(a("LMF", p=8), a("LMI", p=8))
-    mm(a("PSD2", 32, 44), [(a("Z8", 15 - b, 143 - b, p=8), a("CNF", b, 192, 16, p=8)) for b in range(16)])
-    mm(a("PSD2", 48, 50), [(a("E8", p=8), a("LMF", p=8))])
-    for c in range(NC):
-        NI = region(CLS[c])[5]
-        act(a("ST0%d" % c, NI, NI + CLS[c] // 16), a("PSD2", 32 + L0S[c] // 16, 32 + (L0S[c] + CLS[c]) // 16))
-    act(a("TH", 0, 2), a("PSD2", 48, 50))
+    mm(a("PSK1", 448, 460), [(a("Z8", 15 - b, 143 - b, p=8), a("CNF", b, Q, 16, p=8)) for b in range(16)])
+    mm(a("PSK1", 464, 466), [(a("E8", p=8), a("LMF", p=8))])
+    act(a("ST0", NI, NI + 12), a("PSK1", 448, 460))
+    act(a("TH", 0, 2), a("PSK1", 464, 466))
     ts(a("TH", 2, 3), a("TH", 0, 1), -1.0, A.mult, 2040.0, A.add)
     ts(a("TH", 3, 4), a("TH", 1, 2), -2040.0, A.add)
     ts(a("DGM"), a("ID"), a("TH", 2, 3), A.mult)
     ts(a("DGJ"), a("ID"), a("TH", 3, 4), A.mult)
-    ts(a("TAB", 512, 1024), a("ICO"), K2, A.is_le)
-    tt(a("TAB", 512, 1024), a("TAB", 512, 1024), a("IPA"), A.mult)
+    ts(a("TAB", 512, 1024, 2), a("ICO", 0, 512, 2), K2, A.is_le)
+    ms(a("TAB", 513, 1024, 2), 0.0, True)
     ts(a("ICO"), a("ICO"), K1, A.is_ge)
     ts(a("INN"), a("INN"), PB, A.is_le)
     tt(a("TAB", 0, 512), a("ICO"), a("INN"), A.mult)
-    store(T.yx[:, 3072:4096], a("X", 3072, 4096))
-    rec("y", [lambda q: q.dma_start(T.yd[:, 768:1024], T.donor[:, 768:1024])], [a("L0")], [], 60, lat=2500, store=1, dq=local(256))
+    store(T.yx[:, 16 * Q:4096], a("X", 16 * Q, 4096))
+    store(T.yd[:, 4 * Q:1024], T.donor[:, 4 * Q:1024], [a("ST0", LI, LI + Q)])
 
-    XW, XE, DW = a("X", 0, 4096), a("X"), a("DL", D0, D0 + 1024)
+    XW, XE, DW = a("X", 0, 4096), a("X"), a("DL", 0, 1024)
     sel = [a("ZS", 15 - b, 143 - b) for b in range(16)]
     nsel = [a("NZS", 15 - b, 143 - b) for b in range(16)]
     ID, NID = a("ID"), a("NID")
-    APS = a("PSD0", 511, 512)
-
-    def pieces(c):
-        w = 8 * PA[c]
-        return [(w * i, w) for i in range(CLS[c] // w)]
+    APS = (T.PSD0[:, 31, 15:16], (("PSD0", 511, 512),), 1, "float32", None)
+    PEN, DD, DF, M1, M2 = 16, 208, 400, 784, 976
+    il = lambda k, c=None: a("IL", k, k + 12) if c is None else a("IL", k + NA * c, k + NA * c + NA)
+    ol = lambda k, c=None: a("OL", k, k + 12) if c is None else a("OL", k + NA * c, k + NA * c + NA)
+    pieces = range(0, CL, PW)
 
     def listing(c, I, lo, add):
-        na = CLS[c] // 16
         for h in range(2):
-            o = a("OU%d" % c, lo + 8 * na * h, lo + 8 * na * (h + 1))
+            o, i = a("OU%d" % c, lo + 8 * NA * h, lo + 8 * NA * (h + 1)), a3(I, 0, NA, 8 * h, 8 * h + 8)
             if add is None:
-                cp(o, a3(I, 0, na, 8 * h, 8 * h + 8))
+                cp(o, i)
             else:
-                ts(o, a3(I, 0, na, 8 * h, 8 * h + 8), add, A.add)
+                ts(o, i, add, A.add)
 
-    def sums(c, out, w, nm, h, first, last, whole=None):
-        na = CLS[c] // 16
-        mm(out, [(w[8 * h + b], a3(nm, h * na, h * na + na, 16 * b, 16 * b + 16)) for b in range(8)], first, last, whole)
+    def sums(out, w, nm, h, first, last, whole=None):
+        lanes = lambda b: a3(nm, 8 * NA * h + b, 8 * NA * (h + 1), st=8) if nm[1] == "J" else a3(nm, h * NA, h * NA + NA, 16 * b, 16 * b + 16)
+        mm(out, [(w[8 * h + b], lanes(b)) for b in range(8)], first, last, whole)
 
     def first(t, c):
-        s, cl, na, pa = str(c), CLS[c], CLS[c] // 16, PA[c]
-        XO, ZO, NO, RO, LO, NI, RI, LI, RW = region(cl)
-        R, Z = "ST%d%d" % (t, c), "ZI%d%d" % (t, c)
-        PU, PK, FA, IA, OU, BA, B = "PSU" + s, "PSK" + s, "FA" + s, "IA" + s, "OU" + s, "BA" + s, "B" + s
+        s = str(c)
+        R, Z = "ST%d" % t, "ZI%d%d" % (t, c)
+        PU, PK, FA, IA, OU = "PSU" + s, "PSK" + s, "FA" + s, "IA" + s, "OU" + s
         PD = ["PSD%d" % (2 * c), "PSD%d" % (2 * c + 1)]
-        fa = lambda k: a(FA, 128 * k, 128 * k + cl)
-        one, z2 = a("ONE", p=64), a3(Z)
-        pu = a(PU, 0, 256)
-        mm(pu, [(a("WB"), a("CH", 0, 256)), (one, a("CT", p=64))], True, False)
+        fa = lambda k: a(FA, CL * k, CL * k + CL)
+        z2, pu = a3(Z), a(PU, 0, Q)
+        mm(pu, [(a("WB"), a("CH", 0, Q)), (a("ONE", p=64), a("CT", p=64))], True, False)
         for k in range(2):
-            mm(a(PU, 128 * k, 128 * k + cl), [(a("WB"), z2)], False, k == 1, pu)
+            mm(a(PU, CL * k, CL * k + CL), [(a("WB"), z2)], False, k == 1, pu)
         v = fa(1)
-        ts(fa(0), a(PU, 0, cl), 51539607552.0, A.add, 51539607552.0, A.subtract)
-        tt(v, a(PU, 128, 128 + cl), fa(0), A.subtract)
+        ts(fa(0), a(PU, 0, CL), 51539607552.0, A.add, 51539607552.0, A.subtract)
+        tt(v, a(PU, CL, Q), fa(0), A.subtract)
         act(fa(2), v, F.Square, 0.25, K4)
         ts(a3("IY" + s), fa(2), KQ, A.add)
         ts(a3("IY" + s), a3("IY" + s), 4095, A.bitwise_and)
@@ -375,173 +365,178 @@ def build(g, T, send):
         if t and c == 0:
             ts(a("AC", 0, 1), APS, 0.0, A.add)
             ts(a("AC", 1, 2), APS, -0.25, A.add)
-        for r in range(na // pa):
-            mm(a(PD[1], 0, 128, p=16 * pa, p0=64 * r), [(a3(Z, r * pa, r * pa + pa), a("NH"))])
-        act(a("ZT" + s), a(PD[1], 0, 128), bias=C1024)
-        mm(a(PK, 400, 400 + na), [(a("WZ", 15 - b, 143 - b), a3(Z, 0, na, b, b + 1)) for b in range(16)])
-        ts(a(IA, 0, na), a(PK, 400, 400 + na), CW, A.add)
-        uu, ba = a(IA, 8, 8 + na), a(IA, 16, 16 + na)
-        ts(uu, a(IA, 0, na), 4095, A.bitwise_and)
-        tt(a(FA, 896, 896 + na), uu, uu, A.mult)
-        ts(ba, a(FA, 896, 896 + na), 1.0 / 16, A.mult, -0.25 if t == 0 else a("AC", 1, 2), A.add)
-        tt(a(IA, 160, 160 + cl), a(R, RI, RI + cl), v, A.mult)
-        ts(a3("IH" + s), a(IA, 160, 160 + cl), 4, A.logical_shift_right, 4095, A.bitwise_and)
-        listing(c, "IH" + s, 128, K53)
-        for i, (lo, w) in enumerate(pieces(c)):
-            xc, d = a("XC" + s, 16 * lo, 16 * (lo + w)), a((PD[0], PD[1], PU, PD[0])[i], 0, 16 * w)
-            either("sv"[i % 2], xc, ind(XW if t == 0 else XE, a(OU, lo, lo + w)))
-            h, r = divmod(i, na // pa)
-            mm(d, [(ID, xc), (a("ZT" + s, p=2 * w, p0=64 * r), a("E", 512 * h, 512 * h + 16 * w, p=2 * w, p0=64 * r))])
-            act(a3("AB" + s, lo // 8, (lo + w) // 8), d, F.Abs, 4096.0)
-        for i, (lo, w) in enumerate(pieces(c)):
-            if not FUSE[c][i]:
-                either("s", a("H" + s, 16 * lo, 16 * (lo + w)), ind(XE, a(OU, 128 + lo, 128 + lo + w)))
+        for r in range(2):
+            mm(a3(PD[1], 0, 8, p=16 * PA, p0=64 * r), [(a3(Z, r * PA, r * PA + PA), a("NH"))])
+        act(a("ZT" + s), a3(PD[1], 0, 8), bias=C1024)
+        mm(a(PK, 496, 496 + NA), [(a("WZ", 15 - b, 143 - b), a3(Z, 0, NA, b, b + 1)) for b in range(16)])
+        uu, ba, k = il(12, c), il(24, c), il(36, c)
+        ts(il(0, c), a(PK, 496, 496 + NA), CW, A.add)
+        ts(uu, il(0, c), 4095, A.bitwise_and)
+        ts(a(FA, 384, 384 + NA), uu, K15, A.add)
+        tt(a(FA, 384, 384 + NA), a(FA, 384, 384 + NA), uu, A.mult)
+        ts(ba, a(FA, 384, 384 + NA), 1.0 / 16, A.mult, -0.25 if t == 0 else a("AC", 1, 2), A.add)
+        for i, lo in enumerate(pieces):
+            xc, d = a("XC" + s, 16 * lo, 16 * (lo + PW)), a(PU, 0, 16 * PW) if i == 2 else a3(PD[i == 1], 0, PW)
+            cp(xc, ind(XW if t == 0 else XE, a(OU, lo, lo + PW)))
+            h, r = divmod(i, 2)
+            mm(d, [(ID, xc), (a("ZT" + s, p=2 * PW, p0=64 * r), a("E", 384 * h, 384 * h + 384, p=2 * PW, p0=64 * r))])
+            act(a3("AB" + s, lo // 8, (lo + PW) // 8), d, F.Abs, 4096.0)
+        mm(a(PU, 384, 384 + CL), [(ID, a(R, RI + CL * c, RI + CL * c + CL))])
+        tt(a(IA, 0, CL), a(PU, 384, 384 + CL), v, A.mult)
+        ts(a3("IH" + s), a(IA, 0, CL), 4, A.logical_shift_right, 4095, A.bitwise_and)
+        listing(c, "IH" + s, CL, K53)
         for h in range(2):
-            sums(c, a(PK, 0, cl), sel, "AB" + s, h, h == 0, h == 1)
-        scan(fa(2), a("DK", 0, cl), a(PK, 0, cl), A.add, A.min)
-        k = a(IA, 24, 24 + na)
-        ts(k, a(FA, 256 + 15, 256 + cl, 16), K15, A.add)
-        ts(k, k, 255, A.bitwise_and)
+            sums(a(PK, 0, CL), sel, "AB" + s, h, h == 0, h == 1)
+        scan(fa(2), a("DK", 0, CL), a(PK, 0, CL), A.add, A.min)
+        scan(fa(0), a("DK", CL, Q), a(PK, 0, CL), A.add, A.min)
+        tt(k, a(FA, 2 * CL + 15, 3 * CL, 16), a(FA, 15, CL, 16), A.subtract)
         tt(k, k, uu, A.mult)
         tt(k, k, ba, A.add)
-        ts(a(IA, 32, 32 + na), k, 1023, A.bitwise_and)
-        od, oc = a(OU, 384, 384 + na), a(OU, 392, 392 + na)
-        cp(od, a(IA, 32, 32 + na))
-        tt(a(IA, 288, 288 + cl), ind(DW, od), v, A.mult)
-        ts(a3("IY" + s), a(IA, 288, 288 + cl), 4, A.logical_shift_right, 4095, A.bitwise_and)
-        listing(c, "IY" + s, 256, K53)
-        for i, (lo, w) in enumerate(pieces(c)):
-            y = a("Y" + s, 16 + 16 * lo, 16 + 16 * (lo + w))
-            either("s", y, ind(XE, a(OU, 256 + lo, 256 + lo + w)))
-            if FUSE[c][i]:
-                tt(a("H" + s, 16 * lo, 16 * (lo + w)), ind(XE, a(OU, 128 + lo, 128 + lo + w)), y, A.subtract)
-        ts(a(IA, 40, 40 + na), k, 4095, A.bitwise_and)
-        cp(oc, a(IA, 40, 40 + na))
-        either("s", a(BA, 144, 144 + cl), ind(DW, od))
-        either("s", fa(3), ind(XW, oc), 1.0, C2047)
-        ts(fa(4), z2, 0.5, A.mult, 1023.5, A.add)
-        ts(a(IA, 48, 80), ind(a(IA, 0, 8), a("OFU", 8 + 4 * c, 10 + 4 * c)), 1.0, A.mult)
-        ts(a(IA, 48, 72), a(IA, 48, 72), 3, A.bitwise_and)
-        ts(a(IA, 72, 80), a(IA, 72, 80), 15, A.bitwise_and)
-        tt(a(B, 16, 48), a(IA, 48, 80), a("CB" + s), A.add)
-        cp(a(OU, 400, 408), a(B, 40, 48))
-        either("s", a("NB" + s, 0, na), a(R, NI, NI + na), 32.0)
-        L = a("L0", L0S[c], L0S[c] + cl) if t == 0 else a(R, LI, LI + cl)
-        nw, on = a(R, NI, NI + 16), a("OFU", 16, 16 + na)
-        if PPE[c]:
-            pn = a(PU, 256, 256 + cl)
-            either("s", a(BA, 272, 272 + cl), ind(nw, on))
-            mm(pn, [(ID, a(BA, 272, 272 + cl)), (NID, a("KC", 0, cl))])
-            act(a(BA, 16, 16 + cl), pn, F.Relu)
+        ts(il(48, c), k, 1023, A.bitwise_and)
+        cp(ol(0, c), il(48, c))
+        tt(a(IA, CL, Q), ind(DW, ol(0, c)), v, A.mult)
+        ts(a3("IY" + s), a(IA, CL, Q), 4, A.logical_shift_right, 4095, A.bitwise_and)
+        listing(c, "IY" + s, Q, K53)
+        for lo, hi in YCUT:
+            cp(a("Y" + s, 16 + 16 * lo, 16 + 16 * hi), ind(XE, a(OU, Q + lo, Q + hi)))
+        for i, lo in enumerate(pieces):
+            h, hs = a("H" + s, 16 * lo, 16 * (lo + PW)), ind(XE, a(OU, CL + lo, CL + lo + PW))
+            if FUSE[t][c][i]:
+                tt(h, hs, a("Y" + s, 16 + 16 * lo, 16 + 16 * (lo + PW)), A.subtract)
+            else:
+                cp(h, hs)
+        ts(fa(3), z2, 0.5, A.mult, 1023.5, A.add)
+
+    def middle(t, c):
+        R = "ST%d" % t
+        ts(il(60), il(36), 4095, A.bitwise_and)
+        cp(ol(12), il(60))
+        ts(a("XH"), ind(XW, ol(12)), 1.0, A.mult, C2047, A.add)
+        ts(a("IL", 72, 120), ind(a("IL", 0, 12), a("OFU", 8, 11)), 1.0, A.mult)
+        ts(a("IL", 72, 108), a("IL", 72, 108), 3, A.bitwise_and)
+        ts(il(108), il(108), 15, A.bitwise_and)
+        tt(a3("B", 2, 6), a("IL", 72, 120), a("CB"), A.add)
+        cp(ol(24), a3("B", 5, 6))
+        if t < NV - 1:
+            ts(a("NB", 0, 12), a(R, NI, NI + 12), 32.0, A.mult)
         else:
-            tt(a(BA, 16, 16 + cl), ind(nw, on), a("KC", 0, cl), A.is_gt)
-        mm(a(PU, cl, 2 * cl), [(ID, a(R, RI, RI + cl)), (NID, L)])
-        mm(a(PU, 0, cl), [(ID, a(BA, 144, 144 + cl)), (NID, L)])
-        act(a(BA, 400, 400 + 2 * cl), a(PU, 0, 2 * cl))
+            for c in range(NC):
+                ts(a("NB", 48 + 32 * c, 48 + 32 * c + NA), a(R, NI + NA * c, NI + NA * c + NA), 32.0, A.mult)
+        pn = a("PSU0", 0, Q)
+        nn = a(R, NI, NI + 12)
+        mm(pn, [(NID, a("KC"))], True, False)
+        rec("p", [(lambda q, k=k: q.matmul(T.PSU0[:, k:Q:16], ID[0], nn[0], False, k == 15)) for k in range(16)], [ID, nn], [pn],
+            16 * 64 * M["pcy"], grp=groups[None])
+        act(a("BA", PEN, PEN + Q), pn, F.Relu)
+        L = a(R, LI, LI + Q)
+        tt(a("BA", DF, DF + Q), ind(DW, ol(0)), L, A.subtract)
+        mm(a("PSU1", 0, Q), [(ID, a(R, RI, RI + Q)), (NID, L)])
+        act(a("BA", DF + Q, DF + 2 * Q), a("PSU1", 0, Q))
 
     def second(t, c):
-        s, cl, na = str(c), CLS[c], CLS[c] // 16
-        XO, ZO, NO, RO, LO, NI, RI, LI, RW = region(cl)
-        R = "ST%d%d" % (t, c)
-        PU, PK, FA, IA, OU, BA, B, Y, SC = "PSU" + s, "PSK" + s, "FA" + s, "IA" + s, "OU" + s, "BA" + s, "B" + s, "Y" + s, "SC" + s
-        fa = lambda k: a(FA, 128 * k, 128 * k + cl)
-        L = a("L0", L0S[c], L0S[c] + cl) if t == 0 else a(R, LI, LI + cl)
-        k = 0
-        for i, (lo, w) in enumerate(pieces(c)):
-            y = a(Y, 16 + 16 * lo, 16 + 16 * (lo + w))
-            for j, (nm, o) in enumerate((("AJ" + s, a(Y, 15 + 16 * lo, 15 + 16 * (lo + w))), ("AM" + s, a("H" + s, 16 * lo, 16 * (lo + w))))):
-                out = a3(nm, lo // 8, (lo + w) // 8)
-                if j and FUSE[c][i]:
-                    act(out, o, F.Abs, BIG)
-                    continue
-                d = a("PSD%d" % (2 * c + k % 2), 0, 16 * w)
-                k += 1
-                mm(d, [(ID, y), (NID, o)])
-                act(out, d, F.Abs, BIG)
-        ev, pj, pm = a(PK, EV - 1, EV - 1 + 32 * na), a(PK, EV - 1, EV - 1 + 32 * na, 2), a(PK, EV, EV + 32 * na, 2)
-        mm(ev, [(a("IDH"), a("CH", 384, 384 + 2 * cl))], True, False)
-        for out, dg, pen in ((pj, "DGJ", 15), (pm, "DGM", 16)):
-            mm(out, [(a(dg), a("CH", 256, 256 + cl)), (a("IDB"), a(BA, pen, pen + cl))], False, False, ev)
+        s = str(c)
+        R, PK, OU, Y = "ST%d" % t, "PSK" + s, "OU" + s, "Y" + s
+        for i, lo in enumerate(pieces):
+            d = "PSD%d" % (2 * c + i % 2)
+            mm(a3(d, 0, PW), [(ID, a(Y, 16 + 16 * lo, 16 + 16 * (lo + PW))), (NID, a(Y, 15 + 16 * lo, 15 + 16 * (lo + PW)))])
+            act(a3("AJ" + s, lo, lo + PW, 2, 16), a3(d, 0, PW, 2, 16), F.Abs, BIG)
+            h = a("H" + s, 16 * lo, 16 * (lo + PW))
+            if not FUSE[t][c][i]:
+                d = a3("PSD%d" % (3 - 2 * c), 0, PW) if i % 2 else a("PSU" + s, 0, 16 * PW)
+                mm(d, [(ID, a(Y, 16 + 16 * lo, 16 + 16 * (lo + PW))), (NID, h)])
+                h = d
+            act(a3("AM" + s, lo // 8, (lo + PW) // 8), h, F.Abs, BIG)
+        ev, pj, pm = a(PK, EV - 1, EV - 1 + Q), a(PK, EV - 1, EV - 1 + Q, 2), a(PK, EV, EV + Q, 2)
+        mm(ev, [(a("IDH"), a("CH", 288, 480))], True, False)
+        for out, dg, pen in ((pj, "DGJ", PEN - 1 + CL * c), (pm, "DGM", PEN + CL * c)):
+            mm(out, [(a(dg), a("CH", 192, 288)), (a("IDB"), a("BA", pen, pen + CL))], False, False, ev)
         for h in range(2):
-            sums(c, pj, nsel, "AJ" + s, h, False, False, ev)
-            sums(c, pm, sel, "AM" + s, h, False, h == 1, ev)
-        scan(rev(SC, 0, 32 * na), rev(PK, EV, EV + 32 * na), rev("OFF" + s, 0, 32 * na), A.min, A.max)
-        sc, oe = a(SC, 0, 32 * na, 32), a(OU, 408, 408 + na)
-        ts(oe, sc, 0.5, A.mult)
+            sums(pj, nsel, "AJ" + s, h, False, False, ev)
+            sums(pm, sel, "AM" + s, h, False, h == 1, ev)
+        scan(rev("SC", Q * c, Q * c + Q), rev(PK, EV, EV + Q), rev("OFF", 0, Q), A.min, A.max)
+        oe = a(OU, 288, 288 + NA)
+        ts(oe, a("SC", Q * c, Q * c + Q, 32), 0.5, A.mult)
         yw, zn = a(Y, 16), a("ZN%d%d" % (t, c))
-        tt(zn, ind(yw, oe), fa(4), A.add)
+        tt(zn, ind(yw, oe), a("FA" + s, 3 * CL, 4 * CL), A.add)
         if t < NV - 1:
-            send(rec, zn, a3("ZI%d%d" % (t + 1, c)), 4 * t + 2 * c)
-        tt(a("X2" + s, 0, cl), ind(yw, oe), fa(3), A.add)
-        ts(a(R, XO, XO + cl), a("X2" + s, 0, cl), 0.5, A.mult, -1024.0, A.add)
-        tt(a(IA, 80, 112), ind(a(SC, 0, 32 * na), a("OFU", 10 + 4 * c, 12 + 4 * c)), a("NB" + s), A.add)
-        if t < NV - 1:
-            tt(a("NF", 8 * c, 8 * c + na), sc, a(IA, 88, 88 + na), A.is_equal)
-            mm(APS, [(a("ONE"), a("NF", 8 * c + j, 8 * c + j + 1)) for j in range(na)], c == 0, c == NC - 1)
-        ts(a(IA, 136, 136 + na), sc, 0.5, A.mult)
-        ts(a(IA, 112, 136), a(IA, 88, 112), 1, A.bitwise_and)
-        tt(a("DE" + s, 8, 8 + na), a(IA, 136, 136 + na), a(B, 32, 32 + na), A.subtract)
-        tt(a(IA, 88, 112), a(IA, 112, 136), a("DE" + s), A.mult)
-        tt(a(FA, 912, 944), a(IA, 80, 112), a(B, 0, 32), A.add)
-        cp(a(OU, 416, 448), a(FA, 912, 944))
-        either("s", a(R, NO, NO + 8), a(FA, 928, 936))
-        if t == NV - 1:
-            ts(a(R, ZO, ZO + cl), zn, 0.5, A.mult, -1024.0, A.add)
-            store(T.yz[:, L0S[c]:L0S[c] + cl], a(R, ZO, ZO + cl))
-            nn = a(R, NO, NO + na)
-            fns = [(lambda q, b=b: q.matmul(T[PU][0:8, 384 + b:384 + cl:16], T.ID[:, b:128:16], nn[0], True, True)) for b in range(16)]
-            rec("p", fns, [ID, nn], [a(PU, 384, 384 + cl)], 16 * 64 * M["pcy"], each=1, grp=-1 - c)
-            act(a("YN", L0S[c], L0S[c] + cl, p=8), a(PU, 384, 384 + cl, p=8))
-            if c == NC - 1:
-                store(T.yn[:], a("YN", p=8))
-        oi = a(OU, 416, 416 + na)
-        m1, m2 = a(BA, 656, 656 + cl), a(BA, 784, 784 + cl)
-        tt(m1, ind(a("TAB", 0, 512), oi), a(BA, 400, 400 + cl), A.mult)
-        tt(m2, ind(a("TAB", 512, 1024), oi), a(BA, 400 + cl, 400 + 2 * cl), A.mult)
-        if LPE[c]:
-            pl = a(PK, 0, cl)
-            mm(pl, [(ID, L), (ID, m1), (ID, m2)])
-            act(a(R, LO, LO + cl), pl)
+            send(rec, zn, a3("ZI%d%d" % (t + 1, c)), 5 * t + c)
         else:
-            tt(m1, m1, L, A.add)
-            tt(a(R, LO, LO + cl), m1, m2, A.add)
-        either("s", a(R, RO, RO + cl), ind(a(R, LO, RI + cl), a(OU, 424, 424 + na)))
-        if t < NV - 1:
-            send(rec, a(R, NO, LO + cl), a("ST%d%d" % (t + 1, c), NI, LI + cl), 4 * t + 2 * c + 1)
+            ts(a(R, ZO + CL * c, ZO + CL * c + CL), zn, 0.5, A.mult, -1024.0, A.add)
+        tt(a("X2" + s), ind(yw, oe), a("XH", CL * c, CL * c + CL), A.add)
+        ts(a(R, XO + CL * c, XO + CL * c + CL), a("X2" + s), 0.5, A.mult, -1024.0, A.add)
+
+    def third(t, c):
+        R, both = "ST%d" % t, t < NV - 1
+        w, lo, l0, ln = (12, 0, 0, Q) if both else (NA, NA * c, CL * c, CL)
+        lanes = lambda n, k: a(n, k + l0, k + l0 + ln)
+        for c in range(NC) if both else (c,):
+            xw, x = a("X", 0, EXT * (c + 1)), a(R, XO + CL * c, XO + CL * c + CL)
+            if c == 0 and not both:
+                load("y", a("XO"), xw, 3500, None, [a(R, NI)], late=1)
+                xw = a("XO")
+            cp(ind(xw, ol(24, c)), x)
+            if c == 0 and both:
+                cp(ind(a("X", 4096), ol(24, c)), x)
+            if not both:
+                store(T.yx[:, EXT * c:EXT * c + EXT], a("X", EXT, 2 * EXT) if c else xw)
+        sw, sc = a("SC", 2 * l0, 2 * (l0 + ln)), a("SC", 2 * l0, 2 * (l0 + ln), 32)
+        rows = lambda n, r0, r1: a3(n, r0, r1, lo, lo + w)
+        if both:
+            tt(a("IL", 120, 168), ind(sw, a("OFU", 12, 15)), a("NB", 0, 48), A.add)
+            tt(a("NF"), sc, il(132), A.is_equal)
+            mm(APS, [(a("ONE"), a("NF", j, j + 1)) for j in range(12)])
         else:
-            store(T.yl[:, L0S[c]:L0S[c] + cl], a(R, LO, LO + cl))
-            store(T.yr[:, L0S[c]:L0S[c] + cl], a(R, RO, RO + cl))
-
-    def writes(t, c):
-        s, cl, na = str(c), CLS[c], CLS[c] // 16
-        XO, ZO, NO, RO, LO, NI, RI, LI, RW = region(cl)
-        R = "ST%d%d" % (t, c)
-        xw, ox = a("X", 16 * L0S[c], 16 * (L0S[c] + cl)), a("OU" + s, 400, 400 + na)
-        if c == 0 and t == NV - 1:
-            rec("y", [lambda q, x=xw: q.dma_start(T.XO[:], x[0])], [xw, a("ST%d1" % t, region(CLS[1])[5])], [a("XO")], 60,
-                lat=3500, sem=("ld%d" % nld[0], 16), dma=1, late=1, dq=local(EXT))
-            xw = a("XO")
-        cp(ind(xw, ox), a(R, XO, XO + cl))
-        if c == 0 and t < NV - 1:
-            cp(ind(a("X", 4096), ox), a(R, XO, XO + cl))
-        dw = a("DL", 0, 2 * D0) if c == 0 else a("DL", 2 * D0)
-        cp(ind(dw, a("OU" + s, 440, 440 + na)), a(R, LO, LO + cl))
-        if t == NV - 1:
-            store(T.yx[:, 16 * L0S[c]:16 * (L0S[c] + cl)], xw)
-            store(T.yd[:, 4 * L0S[c]:4 * (L0S[c] + cl)], a("DL", D0 + 4 * L0S[c], D0 + 4 * (L0S[c] + cl)))
-
-    def part(f, t, c):
-        k = len(ops)
-        f(t, c)
-        for j in range(k, len(ops)):
-            ops[j]["key"] = ((first, second, writes).index(f), c, (j - k) / (len(ops) - k), t)
+            tt(a("IL", 120, 152), ind(sw, a("OFU", 28, 30)), a("NB", 48 + 32 * c, 80 + 32 * c), A.add)
+        flags, e, o0 = a("IL", 168, 168 + 3 * w), a("IL", 204, 204 + w), 48 + 4 * lo
+        ts(e, sc, 0.5, A.mult)
+        ts(flags, a("IL", 120 + w, 120 + 4 * w), 1, A.bitwise_and)
+        tt(rows("DE", 1, 2), e, rows("B", 4, 5), A.subtract)
+        tt(a("IL", 120 + w, 120 + 4 * w), flags, rows("DE", 0, 3), A.mult)
+        tt(a("FO", 0, 4 * w), a("IL", 120, 120 + 4 * w), rows("B", 0, 4), A.add)
+        lst = lambda k: a("OL", o0 + k * w, o0 + k * w + w)
+        cp(a("OL", o0, o0 + 4 * w), a("FO", 0, 4 * w))
+        if l0:
+            ts(lst(3), a("FO", 3 * w, 4 * w), -4.0 * l0, A.add)
+        cp(a(R, NO + lo, NO + lo + w), a("FO", 2 * w, 3 * w))
+        m1, m2, pl = lanes("BA", M1), lanes("BA", M2), a("PSK%d" % c, 304, 304 + ln)
+        tt(m1, ind(a("TAB", 0, 512), lst(0)), lanes("BA", DF), A.mult)
+        tt(m2, ind(a("TAB", 512, 1024), lst(0)), lanes("BA", DF + Q), A.mult)
+        mm(pl, [(ID, lanes(R, LI)), (ID, m1), (ID, m2)])
+        act(lanes(R, LO), pl)
+        for k in range(0, w, NA):
+            cp(a(R, RO + l0 + 16 * k, RO + l0 + 16 * k + CL), ind(a(R, LO, RI + Q), a("OL", o0 + w + k, o0 + w + k + NA)))
+        cp(ind(a("DL", 4 * l0), lst(3)), lanes(R, LO))
+        if both:
+            j = []
+            for k, (c0, c1) in enumerate(((NO, RO + CL), (RO + CL, NI))):
+                j = [send(rec, a(R, c0, c1), a("ST%d" % (t + 1), c0 + NI - NO, c1 + NI - NO), 5 * t + 2 + k, j)]
+            return
+        for out, k in ((T.yz, ZO), (T.yl, LO), (T.yr, RO)):
+            store(out[:, l0:l0 + ln], lanes(R, k))
+        store(T.yd[:, 4 * l0:4 * (l0 + ln)], a("DL", 4 * l0, 4 * (l0 + ln)))
+        if c:
+            nn = a(R, NO, NO + 12)
+            fns = [(lambda q, b=b: q.matmul(T.PSU1[0:8, b:Q:16], T.ID[:, b:128:16], nn[0], True, True)) for b in range(16)]
+            rec("p", fns, [ID, nn], [a("PSU1", 0, Q)], 16 * 64 * M["pcy"], each=1, grp=-1)
+            act(a("YN", p=8), a("PSU1", 0, Q, p=8))
+            store(T.yn[:], a("YN", p=8))
 
     for t in range(NV):
-        for c in range(NC):
-            part(first, t, c)
-        for c in range(NC):
-            part(second, t, c)
-            part(writes, t, c)
+        ends = ((second, 1, 12, 5), (third, 0, 17, 3)) if t < NV - 1 else ((third, 0, 13, 3), (second, 1, 12, 5), (third, 1, 17, 3))
+        for f, c, at, span in ((first, 0, -3, 11), (first, 1, 1, 11), (middle, 0, 8, 2), (second, 0, 8, 5)) + ends:
+            k = len(ops)
+            f(t, c)
+            for j in range(k, len(ops)):
+                ops[j]["key"] = 1000.0 * (18 * t + at + span * (j - k) / (len(ops) - k))
+    writer = lambda n, lo: [i for i, o in enumerate(ops) if "key" in o and o["w"] and o["w"][0][:2] == (n, lo)]
+    for t in range(NV - 1):
+        for lo in list(pieces)[HINT[0]:]:
+            ops[writer("H1", 16 * lo)[t]]["behind"] = writer("ZN%d0" % t, 0)
+        if HINT[1]:
+            ops[writer("OU1", 0)[t + 1]]["behind"] = [writer("BA", M1)[t], writer("BA", M2)[t]]
+        if HINT[2] and t == 0:
+            ops[writer("FA0", 0)[2]]["behind"] = [writer("BA", M1)[t], writer("BA", M2)[t]]
+            ops[writer("FA0", 2 * CL)[2]]["behind"] = writer("ST%d" % t, LO)
     return ops
 
 
@@ -575,10 +570,16 @@ def depend(ops):
         done.append(1 << i if ops[i]["e"] == "net" else m | 1 << i)
         issued.append(q | 1 << i)
         deps[i] = keep
+    for i, o in enumerate(ops):
+        deps[i] |= set(o.get("behind", ()))
     return deps
 
 
-def place(ops, before, seq, hop, back):
+def queued(ops, i, j):
+    return ops[i]["e"] == "p" == ops[j]["e"] or j in ops[i].get("behind", ())
+
+
+def place(ops, before, seq, hop, back, choose=None, bias=0.0):
     busy = {}
     end = [0.0] * len(ops)
     st = [0.0] * len(ops)
@@ -588,24 +589,31 @@ def place(ops, before, seq, hop, back):
         t = 0.0
         e = o["e"]
         for j in before[i]:
-            x = end[j] if e == "p" == ops[j]["e"] else end[j] + hop
+            x = end[j] if queued(ops, i, j) or queued(ops, j, i) else end[j] + hop
             if x > t:
                 t = x
         if back:
             t += lat
-        if o["e"] != "net":
-            iv = busy.setdefault(o["e"], [])
-            lo, hi = 0, len(iv)
-            while lo < hi:
-                mid = (lo + hi) // 2
-                if iv[mid][1] <= t:
-                    lo = mid + 1
-                else:
-                    hi = mid
-            while lo < len(iv) and iv[lo][0] < t + c:
-                t = max(t, iv[lo][1])
-                lo += 1
-            iv.insert(lo, (t, t + c))
+        if e != "net":
+            found = []
+            for e2 in o["alt"] if choose and "alt" in o else (e,):
+                iv, t2 = busy.setdefault(e2, []), t
+                c2 = o["alt"][e2][1] if "alt" in o else c
+                lo, hi = 0, len(iv)
+                while lo < hi:
+                    mid = (lo + hi) // 2
+                    if iv[mid][1] <= t2:
+                        lo = mid + 1
+                    else:
+                        hi = mid
+                while lo < len(iv) and iv[lo][0] < t2 + c2:
+                    t2 = max(t2, iv[lo][1])
+                    lo += 1
+                found.append((t2 + c2 + (bias * c2 if e2 == "v" else 0), e2, t2, c2, lo))
+            x, e2, t, c, lo = min(found)
+            if e2 != e:
+                choose(i, e2)
+            busy[e2].insert(lo, (t, t + c))
         st[i] = t
         end[i] = t + c + (0 if back else lat)
     return st, end
@@ -629,35 +637,12 @@ def in_order(before, users, key):
     return seq
 
 
-def replay(ops, deps, order, hop):
-    free, fin = {}, [0.0] * len(ops)
-    for i in order:
-        o = ops[i]
-        e = o["e"]
-        t = free.get(e, 0.0)
-        for j in deps[i]:
-            x = fin[j] if e == "p" == ops[j]["e"] else fin[j] + hop
-            if x > t:
-                t = x
-        if o["e"] != "net":
-            free[o["e"]] = t + o["cost"]
-        fin[i] = t + o["cost"] + o.get("lat", 0)
-    return fin
-
-
-def guess(o, i):
-    if "key" not in o:
-        return -1e6 + i
-    ph, c, x, t = o["key"]
-    return 1000.0 * (18 * t + 4 * c + (-3 + 11 * x, 8 + 5 * x, 13)[ph])
-
-
 def put(ops, i, e):
     ops[i]["e"] = e
     ops[i]["fns"], ops[i]["cost"] = ops[i]["alt"][e]
 
 
-def plan(all_ops, deps, rounds, seed, start):
+def plan(all_ops, deps, rounds, seed):
     ops, hop = all_ops[0]
     n = len(ops)
     users = [[] for _ in ops]
@@ -671,49 +656,136 @@ def plan(all_ops, deps, rounds, seed, start):
         x[0] = (x[0] * 1103515245 + 12345) % 2147483648
         return x[0] / 2147483648.0
 
-    def forward(key):
-        key = [-1e9 + i if ops[i].get("dma") and not ops[i].get("late") else key[i] for i in range(n)]
-        return place(ops, deps, in_order(deps, users, key), hop, False)
+    def choose(i, e):
+        put(ops, i, e)
 
-    def score(st):
-        order = in_order(deps, users, st)
-        r = [max(replay(o, deps, order, h)) for o, h in all_ops]
-        return r[0] + sum(r), order, r, [ops[i]["e"] for i in flex], st
+    def forward(key, bias):
+        key = [key[i] - (1e5 if lists[i] else 0) if "key" in ops[i] else -1e6 + i if early[i] else 6000.0 + i for i in range(n)]
+        return place(ops, deps, in_order(deps, users, key), hop, False, choose, bias)
 
-    def flip(i):
-        e = [x for x in ops[i]["alt"] if x != ops[i]["e"]][0]
-        for o, h in all_ops:
-            put(o, i, e)
-
-    st, end = forward(start)
-    best = score(st)
-    cur, cs = st, best[0]
-    for r in range(rounds):
-        key = list(cur)
-        fl = []
-        if r:
-            a = rnd() * max(key)
+    early = ["key" not in o and (bool(o.get("dma")) or o["e"] == "g") or bool(o["w"]) and o["w"][0][0] in ("AB0", "AB1") and o["key"] < 12000 for o in ops]
+    for i in range(n - 1, -1, -1):
+        if early[i]:
+            for j in deps[i]:
+                early[j] = True
+    lists = [early[i] and not any(x[0][:2] in ("XC", "AB") for x in o["r"] + o["w"]) for i, o in enumerate(ops)]
+    starts = []
+    for _ in range(STARTS[0]):
+        cur, cs, best = [o.get("key", 0.0) for o in ops], 1e18, (1e18,)
+        for r in range(rounds):
+            a, bias = rnd() * max(cur), 2.0 * rnd()
             w, amp = 2000 + 5000 * rnd(), 500 + 5000 * rnd() ** 2
-            key = [k + amp * (rnd() - 0.5) if a <= k <= a + w else k for k in key]
-            if rnd() < 0.4:
-                fl = [i for i in flex if a <= cur[i] <= a + w and rnd() < 0.25]
-        for i in fl:
-            flip(i)
-        st, end = forward(key)
-        bs, be = place(ops, users, in_order(users, deps, [-e for e in end]), hop, True)
-        st, end = forward([-e for e in be])
-        s = score(st)
-        if s[0] <= cs + 300:
-            cur, cs = st, s[0]
-        else:
-            for i in fl:
-                flip(i)
-        if s[0] < best[0]:
-            best = s
-    for i, e in zip(flex, best[3]):
-        for o, h in all_ops:
-            put(o, i, e)
+            st, end = forward([k + amp * (rnd() - 0.5) if a <= k <= a + w else k for k in cur], bias)
+            bs, be = place(ops, users, in_order(users, deps, [-e for e in end]), hop, True)
+            st, end = forward([-e for e in be], bias)
+            s = max(end)
+            if s <= cs + 100:
+                cur, cs = st, s
+            if s < best[0]:
+                best = (s, st, [ops[i]["e"] for i in flex])
+        for i, e in zip(flex, best[2]):
+            put(ops, i, e)
+        starts.append(refine(all_ops, deps, users, in_order(deps, users, best[1]), STARTS[1], rnd))
+    best = min(starts, key=lambda x: x[4])
+    for i in flex:
+        put(ops, i, best[2][i])
     return refine(all_ops, deps, users, best[1], ROUNDS[2], rnd)
+
+
+def dispatch(ops, hop, deps, users, tail, look, idle):
+    n = len(ops)
+    left, rel, fin = [len(d) for d in deps], [0.0] * n, [0.0] * n
+    can = [list(o["alt"]) if "alt" in o else [o["e"]] for o in ops]
+    free, ready, order, eng, de = {e: 0.0 for e in "vspgy"}, {e: [] for e in "vspgy"}, [], {}, [0.0]
+
+    def issue(i, e, t):
+        o = ops[i]
+        f = t + (o["alt"][e][1] if "alt" in o else o["cost"])
+        if e != "net":
+            free[e] = f
+            for e2 in can[i]:
+                ready[e2].remove(i)
+        if "dq" in o:
+            de[0] = f = max(f + o["dq"][0], de[0]) + o["dq"][1]
+        order.append(i)
+        eng[i] = e
+        for j in users[i]:
+            rel[j] = max(rel[j], f if ops[j]["e"] == "net" or e == "p" == ops[j]["e"] else f + hop)
+            left[j] -= 1
+            if not left[j]:
+                if ops[j]["e"] == "net":
+                    issue(j, "net", rel[j])
+                else:
+                    for e2 in can[j]:
+                        ready[e2].append(j)
+        fin[i] = f
+
+    for i in range(n):
+        if not left[i]:
+            for e in can[i]:
+                ready[e].append(i)
+    while len(order) < n:
+        t, e = min((max(free[e], min(rel[i] for i in ready[e])), e) for e in ready if ready[e])
+        near = sorted((i for i in ready[e] if rel[i] <= t + look), key=lambda i: -tail[i])[:6]
+        best = None
+        for i in near:
+            s = max(t, rel[i])
+            f = s + (ops[i]["alt"][e][1] if "alt" in ops[i] else ops[i]["cost"])
+            worst = max([s + tail[i]] + [max(f, rel[j]) + tail[j] for j in near if j != i and len(can[j]) == 1])
+            worst += idle * (s - t) - 1e-3 * tail[i]
+            if best is None or worst < best[0]:
+                best = (worst, i, s)
+        issue(best[1], e, best[2])
+    return max(fin), order, eng
+
+
+def plan2(all_ops, deps, rounds, seed):
+    n = len(deps)
+    users = [[] for _ in deps]
+    for i in range(n):
+        for j in deps[i]:
+            users[j].append(i)
+    x = [seed]
+
+    def rnd():
+        x[0] = (x[0] * 1103515245 + 12345) % 2147483648
+        return x[0] / 2147483648.0
+
+    def tails(ops, hop, order=None, eng=None):
+        tail, nxt = [0.0] * n, {}
+        for i in reversed(order or range(n)):
+            o = ops[i]
+            e = eng[i] if eng else o["e"]
+            t = max([0.0] + [tail[j] + (0 if ops[j]["e"] == "net" or e == "p" == ops[j]["e"] else hop) for j in users[i]]) + sum(o.get("dq", ()))
+            if order and e != "net":
+                t = max(t, nxt.get(e, 0.0) - SLACK[0])
+            tail[i] = nxt[e] = t + (o["alt"][e][1] if "alt" in o else o["cost"])
+        return [t + (1e6 - i if ops[i].get("dma") and not ops[i].get("late") else 0) for i, t in enumerate(tail)]
+
+    found = []
+    for s in range(STARTS[0]):
+        ops, hop = all_ops[0 if s % 2 else 2]
+        base = tails(ops, hop)
+        cur, cs, best = base, 1e18, (1e18,)
+        for r in range(rounds):
+            amp, mix = 600 * rnd(), rnd()
+            tail = [mix * a + (1 - mix) * b + amp * rnd() for a, b in zip(base, cur)]
+            got = dispatch(ops, hop, deps, users, tail, 300 + 500 * rnd(), 2 * rnd())
+            if got[0] <= cs + 500:
+                cur, cs = tails(ops, hop, got[1], got[2]), got[0]
+            if got[0] < best[0]:
+                best = got
+        for i in range(n):
+            if "alt" in ops[i]:
+                put(all_ops[0][0], i, best[2][i])
+        found.append(refine(all_ops, deps, users, best[1], STARTS[1], rnd))
+    best = min(found, key=lambda x: x[4])
+    for i in best[2]:
+        put(all_ops[0][0], i, best[2][i])
+    return refine(all_ops, deps, users, best[1], ROUNDS[2], rnd)
+
+
+SLACK = [0.0]
 
 
 def refine(all_ops, deps, users, order, rounds, rnd):
@@ -724,16 +796,25 @@ def refine(all_ops, deps, users, order, rounds, rnd):
     flex = [sum(QN[e] for e in o["alt"]) if "alt" in o else 0 for o in ops]
     fixed = [bool(o.get("dma")) and not o.get("late") for o in ops]
     ms = []
-    for mo, hop in all_ops:
-        dl = [[(j, 0.0 if ops[i]["e"] == "net" or ops[i]["e"] == "p" == ops[j]["e"] else hop) for j in deps[i]] for i in range(n)]
+    for (mo, hop), weight in zip(all_ops, WEIGHTS):
+        gap = lambda i, j: 0.0 if ops[i]["e"] == "net" or queued(ops, i, j) else hop
         cost = [{QN[e]: o["alt"][e][1] for e in o["alt"]} if "alt" in o else [o["cost"]] * 6 for o in mo]
-        ms.append((dl, cost, [o.get("dq") for o in mo]))
+        ms.append(([[(j, gap(i, j)) for j in deps[i]] for i in range(n)], cost, [o.get("dq") for o in mo],
+                   [[(j, gap(j, i)) for j in users[i]] for i in range(n)], weight))
 
-    def run(m, order, trace=False):
-        dl, cost, dq = m
-        free, fin, de = [0.0] * 6, [0.0] * n, 0.0
-        st, why, last, dlast = [0.0] * n, [None] * n, [None] * 6, None
-        for i in order:
+    def trace(m, order, old=None, a=0, b=n - 1):
+        dl, cost, dq, ul, weight = m
+        if old:
+            fin, st, marks, tail, rest, why = old[1], old[2], old[3][:a], old[5], old[6][:b:-1], old[8]
+            free, de, last, dlast = old[3][a]
+            nxt, dn = old[6][b]
+            free, last, nxt = free[:], last[:], nxt[:]
+        else:
+            free, fin, de = [0.0] * 6, [0.0] * n, 0.0
+            st, why, last, dlast, marks = [0.0] * n, [None] * n, [None] * 6, None, []
+            tail, nxt, dn, rest = [0.0] * n, [0.0] * 6, 0.0, []
+        for i in order[a:]:
+            marks.append((free[:], de, last[:], dlast))
             e = eng[i]
             t = free[e]
             w = -1
@@ -745,113 +826,172 @@ def refine(all_ops, deps, users, order, rounds, rnd):
             f = t + cost[i][e]
             if e < 5:
                 free[e] = f
-            if trace:
-                st[i], why[i] = t, (w, last[e])
-                last[e] = i
+            st[i], why[i] = t, (w, last[e])
+            last[e] = i
             q = dq[i]
             if q:
                 f += q[0]
                 if de > f:
                     f = de
-                    if trace:
-                        why[i] = (dlast, None)
+                    why[i] = (dlast, None)
                 de = f = f + q[1]
                 dlast = i
             fin[i] = f
-        return (max(fin), fin, st, why) if trace else max(fin)
-
-    def score(order, limit=1e18):
-        r = [run(ms[0], order)]
-        if r[0] > limit:
-            return 1e18, r
-        r += [run(m, order) for m in ms[1:]]
-        return r[0] + sum(r), r
-
-    def chain(order):
-        end, fin, st, why = run(ms[int(rnd() * len(ms))], order, True)
+        for i in order[b::-1]:
+            rest.append((nxt[:], dn))
+            e = eng[i]
+            t = 0.0
+            for j, h in ul[i]:
+                x = tail[j] + h
+                if x > t:
+                    t = x
+            q = dq[i]
+            if q:
+                dn = q[1] + (t if t > dn else dn)
+                t = q[0] + dn
+            if nxt[e] > t:
+                t = nxt[e]
+            tail[i] = t = t + cost[i][e]
+            if e < 5:
+                nxt[e] = t
+        rest.reverse()
+        end = max(fin)
         i, out = fin.index(end), []
         while i is not None:
             w, prev = why[i]
-            out.append((i, prev if w == -1 else None))
+            if w == -1 and prev is not None or flex[i]:
+                out.append((i, prev if w == -1 else None))
             i = prev if w == -1 else w
-        return out
+        near = [(fin[i] + h + tail[j], i, j) for i in order if st[i] + tail[i] > end - 800 for j, h in ul[i] if fin[i] + h + tail[j] > end - 800]
+        near.sort(reverse=True)
+        return end, fin, st, marks, out, tail, rest, near, why
 
-    def ahead(order, pos, u, v):
-        a, b = pos[u], pos[v]
-        mark = {v}
-        for k in range(b - 1, a - 1, -1):
+    def run(m, tr, mid, a, b, pos):
+        dl, cost, dq, ul, weight = m
+        free, de = tr[3][a][:2]
+        free, old, tail, fin, end = free[:], tr[1], tr[5], {}, 0.0
+        by = 0.0
+        for x, i, j in tr[7]:
+            if pos[i] < a and pos[j] > b:
+                by = x
+                break
+        for i in mid:
+            e = eng[i]
+            t = free[e]
+            for j, h in dl[i]:
+                x = (fin[j] if j in fin else old[j]) + h
+                if x > t:
+                    t = x
+            f = t + cost[i][e]
+            if e < 5:
+                free[e] = f
+            q = dq[i]
+            if q:
+                f += q[0]
+                if de > f:
+                    f = de
+                de = f = f + q[1]
+            fin[i] = f
+            if f > end:
+                end = f
+            for j, h in ul[i]:
+                if pos[j] > b:
+                    x = f + h + tail[j]
+                    if x > end:
+                        end = x
+        nxt, dn = tr[6][b]
+        for e in range(5):
+            if free[e] + nxt[e] > end:
+                end = free[e] + nxt[e]
+        end = max(end, de + dn)
+        return weight * (max(end, by) + 0.1 * (end - tr[0]))
+
+    def move(order, a, b, ahead):
+        mark = {order[b if ahead else a]}
+        for k in range(b - 1, a - 1, -1) if ahead else range(a + 1, b + 1):
             i = order[k]
-            if any(x in mark for x in users[i]):
-                if i == u:
-                    return None
-                mark.add(i)
+            for x in users[i] if ahead else deps[i]:
+                if x in mark:
+                    if k == (a if ahead else b):
+                        return None
+                    mark.add(i)
+                    break
         mid = order[a:b + 1]
-        return order[:a] + [i for i in mid if i in mark] + [i for i in mid if i not in mark] + order[b + 1:]
+        return [i for i in mid if (i in mark) == ahead] + [i for i in mid if (i in mark) != ahead]
 
-    def behind(order, pos, u, v):
-        a, b = pos[u], pos[v]
-        mark = {u}
-        for k in range(a + 1, b + 1):
-            i = order[k]
-            if any(x in mark for x in deps[i]):
-                if i == v:
-                    return None
-                mark.add(i)
-        mid = order[a:b + 1]
-        return order[:a] + [i for i in mid if i not in mark] + [i for i in mid if i in mark] + order[b + 1:]
+    def take(order, tidy, a=None, b=None):
+        if not tidy and a is not None:
+            for k in range(a, b + 1):
+                pos[order[k]] = k
+            new = [trace(m, order, t, a, b) for m, t in zip(ms, trs)]
+            return order, pos, new, sum(m[4] * t[0] for m, t in zip(ms, new))
+        return take_all(order, tidy)
 
-    def tidy(order):
-        st = run(ms[0], order, True)[2]
-        pos = {i: k for k, i in enumerate(order)}
-        order = sorted(order, key=lambda i: (st[i], pos[i]))
-        return order, {i: k for k, i in enumerate(order)}
+    def take_all(order, tidy):
+        if tidy:
+            st = trace(ms[0], order)[2]
+            pos = {i: k for k, i in enumerate(order)}
+            order = sorted(order, key=lambda i: (st[i], pos[i]))
+        trs = [trace(m, order) for m in ms]
+        pos = [0] * n
+        for k, i in enumerate(order):
+            pos[i] = k
+        return order, pos, trs, sum(m[4] * t[0] for m, t in zip(ms, trs))
 
-    order, pos = tidy(order)
-    cs, r = score(order)
-    best = (cs, order, list(eng), r)
-    ch = chain(order)
-    for k in range(rounds):
-        heat = HEAT[0] * (1.0 - k / rounds) * rnd() ** 2
-        v, u = ch[int(rnd() * len(ch))]
-        x, new, fl = rnd(), None, None
-        if x < 0.25:
-            fl = v if flex[v] else u if u is not None and flex[u] else None
-            if fl is None:
+    order, pos, trs, cs = take(order, True)
+    best = (cs, order, list(eng), [t[0] for t in trs])
+    rests, since = [0] * n, 0
+    for k in range(1, rounds):
+        pick, floor = None, cs - 400.0 * sum(WEIGHTS)
+        for _ in range(TRIES):
+            ch = trs[int(rnd() * len(ms))][4]
+            v, u = ch[int(rnd() * len(ch))]
+            x, fl = rnd(), None
+            if x < 0.2 or u is None:
+                who = fl = v if flex[v] else u if flex[u] else None
+                if fl is None:
+                    continue
+                a = b = pos[fl]
+                mid = [fl]
+                eng[fl] = flex[fl] - eng[fl]
+            elif fixed[u] or fixed[v]:
                 continue
-            eng[fl] = flex[fl] - eng[fl]
-            new = order
-        elif u is None or fixed[u] or fixed[v]:
+            else:
+                a, b = pos[u], pos[v]
+                who = v if x < 0.6 else u
+                for _ in range(int(rnd() ** 3 * 12)):
+                    p, d = (a - 1, -1) if x < 0.6 else (b + 1, 1)
+                    while 0 <= p < n and eng[order[p]] != eng[v]:
+                        p += d
+                    if 0 <= p < n and not fixed[order[p]]:
+                        a, b = (p, b) if x < 0.6 else (a, p)
+                mid = move(order, a, b, x < 0.6)
+                if mid is None:
+                    continue
+            s = NOISE * rnd() + floor
+            for m, t in zip(ms, trs):
+                s += run(m, t, mid, a, b, pos) - m[4] * (t[0] - 400.0)
+                if pick and s > pick[0]:
+                    break
+            if fl is not None:
+                eng[fl] = flex[fl] - eng[fl]
+            if (rests[who] < k or s < best[0]) and (pick is None or s < pick[0]):
+                pick = (s, who, fl, a, b, mid)
+        if pick is None:
             continue
-        elif x < 0.65:
-            p = pos[u]
-            for _ in range(int(rnd() ** 2 * 4)):
-                p2 = p - 1
-                while p2 >= 0 and eng[order[p2]] != eng[v]:
-                    p2 -= 1
-                if p2 >= 0 and not fixed[order[p2]]:
-                    p = p2
-            new = ahead(order, pos, order[p], v)
-        else:
-            p = pos[v]
-            for _ in range(int(rnd() ** 2 * 4)):
-                p2 = p + 1
-                while p2 < n and eng[order[p2]] != eng[v]:
-                    p2 += 1
-                if p2 < n:
-                    p = p2
-            new = behind(order, pos, u, order[p])
-        if new is None:
-            continue
-        s, r2 = score(new, r[0] + heat)
-        if s <= cs + heat:
-            order, pos = tidy(new)
-            cs, r = score(order)
-            ch = chain(order)
-            if cs < best[0]:
-                best = (cs, order, list(eng), r)
-        elif fl is not None:
+        s, who, fl, a, b, mid = pick
+        if fl is not None:
             eng[fl] = flex[fl] - eng[fl]
-    return deps, best[1], {i: "vspg"[best[2][i]] for i in range(n) if flex[i]}, best[3]
+        rests[who] = k + REST + int(REST * rnd())
+        order, pos, trs, cs = take(order[:a] + mid + order[b + 1:], not k & 15, a, b)
+        since += 1
+        if cs < best[0]:
+            best, since = (cs, order, list(eng), [t[0] for t in trs]), 0
+        elif since > BACK:
+            eng[:] = best[2]
+            order, pos, trs, cs = take(best[1], False)
+            since = 0
+    return deps, best[1], {i: "vspg"[best[2][i]] for i in range(n) if flex[i]}, best[3], best[0]
 
 
 def rank_program(g, core, T, topo):
@@ -861,14 +1001,17 @@ def rank_program(g, core, T, topo):
     n = len(T.cores)
     dst, src = T.cores[(rank + SHIFT) % n], T.cores[(rank - SHIFT) % n]
     rid, pid = topo.addr(dst)[:2]
-    mask, n_out, n_in = topo.mask(core, dst), len(topo.engines(core, dst)), len(topo.engines(src, core))
+    n_out = n_in = min(len(topo.engines(c, T.cores[(r + SHIFT) % n])) for r, c in enumerate(T.cores))
+    mask = sum(1 << e for e in topo.engines(core, dst)[:n_out])
     sent = [0]
 
-    def send(rec, i, out, k):
+    def send(rec, i, out, k, behind=()):
         sent[0] += n_out
-        j = rec("g", [lambda q: q.remote_dma(out[0], i[0], T.sem["ar%d" % k], T.sem.sent, pid, rid, mask)], [i], [], 300 if k else M["r1"], remote=1)
+        j = rec("g", [lambda q: q.remote_dma(out[0], i[0], T.sem["ar%d" % k], T.sem.sent, pid, rid, mask)], [i], [], 300 if k else M["r1"],
+                behind=behind)
         rec("net", [], [], [out], 0, lat=M["rl"] + 128 * 2 * i[2] / M["rb"], after=[j], sem=("ar%d" % k, n_in),
             dq=(M["rl"], 128 * 2 * i[2] / M["rb"]))
+        return j
 
     ops = build(g, T, send)
     if not _PLAN:
@@ -877,17 +1020,16 @@ def rank_program(g, core, T, topo):
             M.update(m)
             all_ops.append((build(g, T, send), m["hop"]))
         sent[0] = mine
-        _PLAN["o"] = all_ops
-        _PLAN["p"] = plan(all_ops, depend(ops), ROUNDS[0], ROUNDS[1], [guess(o, i) for i, o in enumerate(ops)])
+        _PLAN["p"] = plan(all_ops, depend(ops), ROUNDS[0], ROUNDS[1])
     deps, order, eng = _PLAN["p"][:3]
     for i in eng:
         put(ops, i, eng[i])
-    Q = {"v": g.vector, "s": g.scalar, "p": g.tensor, "g": g, "y": g.sync}
+    QU = {"v": g.vector, "s": g.scalar, "p": g.tensor, "g": g, "y": g.sync}
     pos = {i: k for k, i in enumerate(order)}
     need = set()
     for final in (False, True):
-        known = {e: 0 for e in Q}
-        clos, sig, last, cnt, val, waited, group = {}, {}, {}, {e: 0 for e in Q}, {}, {}, {}
+        known = {e: 0 for e in QU}
+        clos, sig, last, cnt, val, waited, group = {}, {}, {}, {e: 0 for e in QU}, {}, {}, {}
         stores = 0
         for i in order:
             o = ops[i]
@@ -896,7 +1038,7 @@ def rank_program(g, core, T, topo):
                 clos[i], sig[i] = 1 << i, o["sem"]
                 val[o["sem"][0]] = o["sem"][1]
                 continue
-            want = sorted((j for j in deps[i] if not e == "p" == ops[j]["e"]), key=lambda j: -pos[j])
+            want = sorted((j for j in deps[i] if not queued(ops, i, j)), key=lambda j: -pos[j])
             if "sem" in o:
                 sig[i] = o["sem"]
             elif final and i in need:
@@ -911,7 +1053,7 @@ def rank_program(g, core, T, topo):
                     need.add(j)
                     known[e] |= clos[j]
                     if final:
-                        Q[e].wait_ge(T.sem[sig[j][0]], sig[j][1])
+                        QU[e].wait_ge(T.sem[sig[j][0]], sig[j][1])
                         waited[sig[j][0]] = max(waited.get(sig[j][0], 0), sig[j][1])
             clos[i] = known[e] | 1 << i
             if e == "p":
@@ -921,7 +1063,7 @@ def rank_program(g, core, T, topo):
                 val[sig[i][0]] = sig[i][1]
             if final:
                 for k, f in enumerate(o["fns"]):
-                    ins = f(Q[e])
+                    ins = f(QU[e])
                     if o.get("store"):
                         ins.then_inc(T.sem.st, 16)
                         stores += 16

from concourse.mybir import dt, AluOpType, AxisListType, ActivationFunctionType

A = AluOpType
F = ActivationFunctionType
NV, SHIFT, NC = 3, 3, 2
Q, CL, NA, PA = 192, 96, 6, 3
PW = 8 * PA
EXT = 16 * CL
FUSE = [((0, 0, 1, 1), (1, 1, 1, 1))] + [((1, 1, 1, 1), (1, 1, 1, 1))] * 2
YCUT = ((0, 24), (24, 48), (48, 96))
HINT = [1, 1, 0]
BIG = 8192.0
EV = 98
XO, ZO, NO, RO, LO, NI, RI, LI, RW = 0, 192, 384, 400, 592, 784, 800, 992, 1184

SCRATCH = {}


def _buf(name, cols, dtype, where="sbuf"):
    SCRATCH[name] = (where, [128] + (cols if isinstance(cols, list) else [cols]), dtype)


for _n, _c, _d in (
        ("X", 4096 + EXT, "bfloat16"), ("XO", EXT, "bfloat16"), ("DL", 1024 + 4 * Q, "bfloat16"), ("Z0", Q, "bfloat16"),
        ("WI", 256, "int32"), ("WR", 272, "bfloat16"), ("CNI", Q, "int32"), ("LMI", 2, "int32"),
        ("CNF", Q, "bfloat16"), ("LMF", 2, "float32"), ("TH", 4, "float32"),
        ("PI", 8, "int32"), ("PF", 24, "float32"), ("IC", 144, "bfloat16"), ("IB", 128, "bfloat16"),
        ("ICO", 512, "bfloat16"), ("INN", 512, "bfloat16"), ("KC", Q, "bfloat16"),
        ("IS", 12, "float32"), ("Z8", 144, "bfloat16"), ("E8", 128, "float32"), ("E", 768, "bfloat16"),
        ("ID", 128, "bfloat16"), ("NID", 128, "bfloat16"), ("IDB", 128, "bfloat16"), ("ZS", 144, "bfloat16"), ("NZS", 144, "bfloat16"),
        ("WZ", 144, "float16"), ("WB", 128, "float16"), ("NH", 128, "float16"), ("IDH", 128, "float16"),
        ("DGM", 128, "float16"), ("DGJ", 128, "float16"), ("CH", 480, "float16"),
        ("BLK", 128, "bfloat16"), ("ONE", 128, "bfloat16"), ("CT", Q, "bfloat16"),
        ("DG", 32, "bfloat16"), ("KF", 16, "float32"), ("DS", 16, "float32"), ("DK", Q, "float32"), ("OF", 32, "float32"),
        ("OFU", 32, "uint16"), ("TAB", 1024, "bfloat16"), ("LN", 12, "float32"), ("OFF", Q, "float32"),
        ("NF", 12, "bfloat16"), ("AC", 2, "float32"), ("YN", Q, "float32"),
        ("CB", 48, "float32"), ("B", [6, 12], "float32"), ("DE", [3, 12], "float32"), ("NB", 112, "float32"), ("FO", 48, "float32"),
        ("SC", 2 * Q, "float32"), ("XH", Q, "float32"), ("IL", 224, "int32"), ("OL", 96, "uint16"), ("BA", 1168, "bfloat16")):
    _buf(_n, _c, _d)
for _c in range(NC):
    for _n, _w, _d in (
            ("FA", 400, "float32"), ("IA", 2 * CL, "int32"), ("IH", [NA, 16], "int32"), ("IY", [NA, 16], "int32"), ("OU", 296, "uint16"),
            ("ZT", 128, "bfloat16"), ("X2", CL, "float16"),
            ("XC", 16 * CL, "bfloat16"), ("H", 16 * CL, "bfloat16"), ("Y", 16 * CL + 16, "bfloat16"),
            ("AB", [2 * NA, 128], "bfloat16"), ("AM", [2 * NA, 128], "bfloat16"), ("AJ", [CL, 16], "bfloat16")):
        _buf(_n + str(_c), _w, _d)
    for _t in range(NV):
        _buf("ZI%d%d" % (_t, _c), [NA, 16], "float16")
        _buf("ZN%d%d" % (_t, _c), CL, "float16")
for _t in range(NV):
    _buf("ST%d" % _t, RW, "bfloat16")
for _b in ("D0", "D1", "D2", "D3", "K0", "K1", "U0", "U1"):
    _buf("PS" + _b, [32, 16] if _b[0] == "D" else 512, "float32", "psum")

NSEM = {"v": 46, "s": 30, "p": 30, "g": 11}
SEMAPHORES = [e + str(i) for e in NSEM for i in range(NSEM[e])] + ["ld%d" % i for i in range(11)] \
    + ["ar%d" % i for i in range(10)] + ["sent", "st"]
M = dict(cy=0.83, pcy=0.43, hop=215.0, ga=1.56, sc=3.8, rl=700.0, rb=50.0, r1=2200.0, ld=1200.0, lb=280.0)
MODELS = [dict(M), dict(cy=0.95, pcy=0.5, hop=200.0, ga=1.7, sc=4.5, rl=1400.0, rb=18.0, r1=3200.0, ld=2000.0, lb=150.0),
          dict(cy=1.05, pcy=0.58, hop=320.0, ga=1.4, sc=3.8, rl=1000.0, rb=35.0, r1=2600.0, ld=1400.0, lb=230.0),
          dict(cy=0.85, pcy=0.44, hop=200.0, ga=1.56, sc=3.8, rl=1400.0, rb=16.0, r1=2800.0, ld=1900.0, lb=240.0)]
WEIGHTS = [1.0, 1.0, 1.0, 1.0]
ROUNDS, STARTS = [300, 7, 11000], [1, 2]
TRIES, REST, BACK, NOISE = 16, 14, 1000, 200.0
_PLAN = {}


def build(g, T, send):
    ops = []
    CY = M["cy"]

    def a(n, lo=None, hi=None, st=1, p=None, p0=0):
        w = SCRATCH[n][1][1]
        lo = 0 if lo is None else lo
        hi = w if hi is None else hi
        ps = slice(p0, p0 + (p or 128))
        ap = T[n][ps, lo:hi:st] if st > 1 else T[n][ps, lo:hi]
        return (ap, ((n, lo, hi),), len(range(lo, hi, st)), SCRATCH[n][2], None)

    def rev(n, lo, hi):
        ap = T[n][:, hi - 1:lo - 1:-1] if lo else T[n][:, hi - 1::-1]
        return (ap, ((n, lo, hi),), hi - lo, SCRATCH[n][2], None)

    def a3(n, r0=0, r1=None, c0=0, c1=None, st=1, p=128, p0=0):
        rows, w = SCRATCH[n][1][1:]
        r1 = rows if r1 is None else r1
        c1 = w if c1 is None else c1
        rng = ((n, r0 * w, r1 * w),) if 2 * (c1 - c0) > w else tuple((n, r * w + c0, r * w + c1) for r in range(r0, r1, st))
        ap = T[n][p0:p0 + p, r0:r1:st, c0:c1] if st > 1 else T[n][p0:p0 + p, r0:r1, c0:c1]
        return (ap, rng, len(range(r0, r1, st)) * (c1 - c0), SCRATCH[n][2], None)

    def ind(win, off):
        return (win[0].indirect(off[0]), win[1] + off[1], 16 * off[2], win[3], "ind")

    def rec(e, fns, rd, wr, cost, **kw):
        r, w = [], []
        for x in rd:
            if isinstance(x, tuple):
                r += list(x[1])
        for x in wr:
            w += list(x[1])
        ops.append(dict(e=e, fns=fns, r=r, w=w, cost=cost, **kw))
        return len(ops) - 1

    def u(x):
        return x[0] if isinstance(x, tuple) else x

    def vc(out, ins, two=False):
        if ins[0][4] == "ind":
            return (60 + M["ga"] * out[2]) * CY
        if out[4] == "ind":
            return (60 + M["sc"] * out[2]) * CY
        half = all(x[3] in ("bfloat16", "uint16", "float16") for x in [out] + ins)
        return max(64, out[2] * (0.5 if half else 1) * (2 if two else 1)) * CY

    def ts(out, i, s1, o0, s2=None, o1=None):
        if o1 is None:
            f = lambda q: q.tensor_scalar(out[0], i[0], u(s1), None, o0)
        else:
            f = lambda q: q.tensor_scalar(out[0], i[0], u(s1), u(s2), o0, o1)
        rec("v", [f], [i, s1, s2], [out], vc(out, [i]))
        if plain(out, i, s1, s2) and (o0, o1) in ((A.mult, None), (A.add, None), (A.mult, A.add)):
            act(out, i, scale=s1 if o0 == A.mult else 1.0, bias=s1 if o0 == A.add else s2 if o1 else 0.0)
            also()

    def plain(*xs):
        return all(x[3] in ("float32", "bfloat16") and not x[1][0][0].startswith("PS") for x in xs if isinstance(x, tuple))

    def also():
        o2, o1 = ops.pop(), ops[-1]
        o1["alt"] = {o1["e"]: (o1["fns"], o1["cost"]), o2["e"]: (o2["fns"], o2["cost"])}

    def tt(out, i0, i1, op):
        sb = not (i0[1][0][0].startswith("PS") or i1[1][0][0].startswith("PS"))
        rec("v", [lambda q: q.tensor_tensor(out[0], i0[0], i1[0], op)], [i0, i1], [out], vc(out, [i0, i1], sb))

    def cp(out, i):
        w = (out[0], out[1][:1]) if out[4] else out
        rd = [i] + ([(0, out[1][1:])] if out[4] else [])
        rec("v", [lambda q: q.tensor_copy(out[0], i[0])], rd, [w], vc(out, [i]))
        if plain(out, i) and not out[4]:
            act(out, i)
            also()

    def ms(out, val, v=False):
        rec("v", [lambda q: q.memset(out[0], val)], [], [out], vc(out, [out]))
        if not v and val == int(val) and abs(val) <= 256 and plain(out):
            iota(out, [[0, out[2]]], int(val), 0)
            also()

    def scan(out, d0, d1, o0, o1):
        rec("v", [lambda q: q.tensor_tensor_scan(out[0], d0[0], d1[0], 0.0, o0, o1)], [d0, d1], [out], vc(out, [d0, d1]))

    def act(out, i, fn=F.Identity, scale=1.0, bias=0.0):
        c = (78 + M["ga"] * out[2]) * CY if i[4] else max(64, out[2] + 8) * CY
        rec("s", [lambda q: q.activation(out[0], i[0], fn, bias=u(bias), scale=u(scale))], [i, bias, scale], [out], c)

    groups = {None: 0}

    def mm(out, pairs, first=True, last=True, whole=None):
        k = len(pairs)
        key = (whole or out)[1][0]
        if first:
            groups[None] += 1
            groups[key] = groups[None]
        fns = [(lambda q, j=j: q.matmul(out[0], pairs[j][0][0], pairs[j][1][0], first and j == 0, last and j == k - 1)) for j in range(k)]
        c = sum(max(64, r[2]) * (4 if r[3] == "float32" else 1) for l, r in pairs) * M["pcy"] + 30
        rec("p", fns, [x for pr in pairs for x in pr], [out], c, grp=groups[key])

    def iota(out, pat, base=0, cm=0):
        if out[3] == "int32":
            f = lambda q: q.iota(out[0], pat, base, cm)
        else:
            f = lambda q: q.iota(out[0], pat, base, cm, allow_small_or_imprecise_dtypes=True)
        rec("g", [f], [], [out], 130 + 2 * out[2] * CY)

    nld = [0]

    def local(cols):
        return M["ld"], 160 + 128 * 2 * cols / M["lb"]

    def load(e, out, src, ns, cols=None, after=(), **kw):
        rec(e, [lambda q: q.dma_start(out[0], u(src))], [src] + list(after), [out], 60, lat=ns, sem=("ld%d" % nld[0], 16), dma=1,
            dq=local(out[2] if cols is None else cols), **kw)
        nld[0] += 1

    def store(dst, i, after=()):
        cols = dst.shape[1]
        rec("y", [lambda q: q.dma_start(dst, u(i))], [i] + list(after), [], 60, lat=sum(local(cols)), store=1, dq=local(cols))

    load("y", a("Z0"), T.zed[:], 2200)
    load("s", a("WI", 0, 128, p=1), T.wt[:], 2200, -60)
    load("s", a("WI", 128, 256, p=1), T.kap[:], 2300, -60)
    load("y", a("LMI", p=8), T.lim[:], 2600, -60)
    load("s", a("CNI", p=8), T.cnt[:], 2600, -60)
    load("y", a("X", 0, 4096), T.stock[:], 7000)
    load("s", a("ST0", RI, RI + Q), T.rend[:], 7500)
    load("y", a("DL", 0, 1024), T.donor[:], 8500)
    load("y", a("X", 4096, 4096 + EXT), T.stock[:, 0:EXT], 10500)
    load("y", a("ST0", LI, LI + Q), T.lend[:], 11000)
    iota(a("PI", 0, 1), [[0, 1]], 0, 1)
    iota(a("IB"), [[16, 8], [0, 16]])
    iota(a("IC"), [[1, 144]])
    iota(a("IS"), [[1, 12]])
    iota(a("E", 0, 384), [[16, PA], [1, 8], [0, 16]])
    iota(a("KC"), [[0, 12], [1, 16]])
    iota(a("Z8", p=8), [[1, 144]], -15, -16)
    iota(a("E8", p=8), [[16, 8], [0, 16]], 0, -16)
    iota(a("OFF"), [[256, NA], [2, 16], [0, 2]])
    iota(a("ICO"), [[0, 16], [1, 32]])
    iota(a("INN"), [[1, 16], [0, 32]])
    p0 = a("PI", 0, 1)
    for j, m in ((1, 15), (2, 112), (3, 63), (4, 7), (5, 8)):
        ts(a("PI", j, j + 1), p0, m, A.bitwise_and)
    cp(a("PF", 0, 6), a("PI", 0, 6))
    col = lambda j: a("PF", j, j + 1)
    PP, PB, G16, P64, P7, P8, W2, KP, K4, KQ, K53, K1, K2, K15, CW, C1024, C2047, T0, T1, T2 = [col(j) for j in range(20)]
    ms(a("WR", 256, 257, p=1), 1.0, True)
    cp(a("WR", 0, 256, p=1), a("WI", p=1))
    for j in range(2):
        mm(a("PSK1", 440 + j, 441 + j), [(a("WR", 128 * j, 128 * j + 128, p=1), a("WR", 256, 257, p=1))])
    ts(W2, a("PSK1", 440, 441), 0.5, A.mult)
    cp(KP, a("PSK1", 441, 442))
    cp(a("DG", 16, 17), a("PSK1", 440, 441))
    ts(K4, KP, 2.0, A.mult, -4.0, A.add)
    ts(KQ, KP, KP, A.mult, -4.0, A.mult)
    ts(KQ, KQ, -0.25, A.add)
    ts(a("WB"), a("IB"), G16, A.is_equal, W2, A.mult)
    ts(a("ID"), a("IC", 0, 128), PP, A.is_equal)
    ts(a("NH"), a("ID"), -0.5, A.mult)
    ts(a("ZS"), a("IC"), G16, A.subtract, 15.0, A.is_equal)
    ts(a("WZ"), a("ZS"), W2, A.mult)
    ts(a("E", 384, 768), a("E", 0, 384), 8.0, A.add, P64, A.is_equal)
    ts(a("E", 0, 384), a("E", 0, 384), P64, A.is_equal)
    ms(a("ONE"), 1.0)
    ms(a("CT", 0, CL, p=32), -64.0)
    ms(a("CT", 0, CL, p=32, p0=32), 1.0 / 64)
    ms(a("CT", CL, Q, p=64), 0.25)
    ms(a("CH", 0, 192), -2048.0)
    ms(a("CH", 192, 288), BIG)
    ms(a("CH", 288, 480, 2), 2041.0)
    ms(a("CH", 289, 480, 2), -2040.0)
    ms(a("CH", 288, 480, 32), -60000.0)
    ms(C1024, 1024.0)
    ms(C2047, 2047.5)
    ts(a("BLK"), a("IB"), G16, A.is_equal)
    ts(a("DG", 0, 16), a("KC", 0, 16), PB, A.is_equal, KP, A.mult)
    mm(a("PSK1", 416, 433), [(a("BLK"), a("DG", 0, 17))])
    cp(a("KF"), a("PSK1", 416, 432))
    ts(CW, a("PSK1", 432, 433), -1024.0, A.mult)
    ts(K53, PB, 53.0, A.mult)
    ts(K1, PB, 2.0, A.mult, 1.0, A.add)
    ts(K2, PB, 2.0, A.mult)
    LN, EB = a("LN"), a("CB", 24, 36)
    ts(LN, a("IS"), 16.0, A.mult, PB, A.add)
    ts(a("OF", 0, 6), a("IS", 0, 6), 0.0, A.mult, PB, A.add)
    ts(a("PI", 5, 8), a("LN", 0, 3), -5.5, A.add, 1.0 / 12, A.mult)
    ms(a("OF", 6, 16), 0.0)
    ts(a("OF", 12, 15), a("PI", 5, 8), -12.0, A.mult)
    tt(a("OF", 8, 11), a("OF", 12, 15), a("LN", 0, 3), A.add)
    ts(a("OF", 12, 15), a("OF", 8, 11), 32.0, A.mult)
    ts(a("OF", 30, 32), a("OF", 8, 10), 6.0, A.is_ge, -192.0, A.mult)
    tt(a("OF", 28, 30), a("OF", 12, 14), a("OF", 30, 32), A.add)
    cp(a("OF", 16, 28), a("IS"))
    cp(a("OFU"), a("OF"))
    ms(a("DS", 0, 1), 33554432.0)
    tt(a("DS", 1, 16), a("KF", 0, 15), a("KF", 1, 16), A.subtract)
    ts(a("DS", 1, 16), a("DS", 1, 16), -256.0, A.add)
    act(a("DK", 0, CL), ind(a("DS"), a("OFU", 0, 6)))
    ms(a("DK", CL, Q), -256.0)
    ms(a("DK", CL, Q, 16), 33554432.0)
    ts(K15, a("KF", 15, 16), 16.0, A.mult)
    ts(a("NID"), a("ID"), -1.0, A.mult)
    ts(a("IDB"), a("ID"), 134217728.0, A.mult)
    ts(a("IDH"), a("ID"), BIG, A.mult)
    ts(a("NZS"), a("ZS"), -1.0, A.mult)
    ts(T0, P8, 16.0 * NA, A.mult)
    ts(T1, P7, 16.0, A.mult, T0, A.add)
    ts(T2, T1, 2.0, A.mult)
    for c in range(NC):
        ts(a("CB", 24 + NA * c, 30 + NA * c), a("IS", 0, NA), 128.0, A.mult, T1, A.add)
    ts(a("OFF"), a("OFF"), T2, A.add)
    ts(a("OFF", 1, Q, 2), a("OFF", 1, Q, 2), 0.75, A.add)
    ts(a("OFF", 31, Q, 32), a("OFF", 31, Q, 32), -0.125, A.add)
    ms(a("CB", 0, 12), 1.0)
    ts(a("CB", 12, 24), LN, 4.0, A.mult)
    ts(a("CB", 36, 48), LN, 16.0, A.mult)
    ts(a3("B", 0, 1), EB, -2.0, A.mult)
    cp(a3("B", 1, 2), LN)
    ms(a3("DE", 0, 1), float(RI - LO))
    ms(a3("DE", 2, 3), 1024.0)
    ms(a("NB", 12), -0.2)
    ms(a("ST%d" % (NV - 1), LO + CL, NI), 0.0)
    ms(a("BA", 0, 16), 0.0)
    ms(a("ST0", NI + 8, RI), 0.0)
    for t in range(NV - 1):
        ms(a("ST%d" % t, NO + 8, RO), 0.0)
    for c in range(NC):
        s = str(c)
        ms(a("Y" + s, 0, 16), 0.0)
        ms(a("PSK" + s, EV + Q - 1, EV + Q), -1e6)
        ms(a3("PSD%d" % (2 * c + 1), 0, 8), 0.0)
        ms(a3("AJ" + s, 0, CL, 0, 2), 0.0, True)
        ts(a3("ZI0" + s), a("Z0", CL * c, CL * c + CL), 2.0, A.mult, 2048.0, A.add)
    ms(a("DL", 1024), 0.0)
    ts(a("Z8", p=8), a("Z8", p=8), 0.0, A.is_equal)
    ts(a("E8", p=8), a("E8", p=8), 0.0, A.is_equal)
    cp(a("CNF", p=8), a("CNI", p=8))
    cp(a("LMF", p=8), a("LMI", p=8))
    mm(a("PSK1", 448, 460), [(a("Z8", 15 - b, 143 - b, p=8), a("CNF", b, Q, 16, p=8)) for b in range(16)])
    mm(a("PSK1", 464, 466), [(a("E8", p=8), a("LMF", p=8))])
    act(a("ST0", NI, NI + 12), a("PSK1", 448, 460))
    act(a("TH", 0, 2), a("PSK1", 464, 466))
    ts(a("TH", 2, 3), a("TH", 0, 1), -1.0, A.mult, 2040.0, A.add)
    ts(a("TH", 3, 4), a("TH", 1, 2), -2040.0, A.add)
    ts(a("DGM"), a("ID"), a("TH", 2, 3), A.mult)
    ts(a("DGJ"), a("ID"), a("TH", 3, 4), A.mult)
    ts(a("TAB", 512, 1024, 2), a("ICO", 0, 512, 2), K2, A.is_le)
    ms(a("TAB", 513, 1024, 2), 0.0, True)
    ts(a("ICO"), a("ICO"), K1, A.is_ge)
    ts(a("INN"), a("INN"), PB, A.is_le)
    tt(a("TAB", 0, 512), a("ICO"), a("INN"), A.mult)
    store(T.yx[:, 16 * Q:4096], a("X", 16 * Q, 4096))
    store(T.yd[:, 4 * Q:1024], T.donor[:, 4 * Q:1024], [a("ST0", LI, LI + Q)])

    XW, XE, DW = a("X", 0, 4096), a("X"), a("DL", 0, 1024)
    sel = [a("ZS", 15 - b, 143 - b) for b in range(16)]
    nsel = [a("NZS", 15 - b, 143 - b) for b in range(16)]
    ID, NID = a("ID"), a("NID")
    APS = (T.PSD0[:, 31, 15:16], (("PSD0", 511, 512),), 1, "float32", None)
    PEN, DD, DF, M1, M2 = 16, 208, 400, 784, 976
    il = lambda k, c=None: a("IL", k, k + 12) if c is None else a("IL", k + NA * c, k + NA * c + NA)
    ol = lambda k, c=None: a("OL", k, k + 12) if c is None else a("OL", k + NA * c, k + NA * c + NA)
    pieces = range(0, CL, PW)

    def listing(c, I, lo, add):
        for h in range(2):
            o, i = a("OU%d" % c, lo + 8 * NA * h, lo + 8 * NA * (h + 1)), a3(I, 0, NA, 8 * h, 8 * h + 8)
            if add is None:
                cp(o, i)
            else:
                ts(o, i, add, A.add)

    def sums(out, w, nm, h, first, last, whole=None):
        lanes = lambda b: a3(nm, 8 * NA * h + b, 8 * NA * (h + 1), st=8) if nm[1] == "J" else a3(nm, h * NA, h * NA + NA, 16 * b, 16 * b + 16)
        mm(out, [(w[8 * h + b], lanes(b)) for b in range(8)], first, last, whole)

    def first(t, c):
        s = str(c)
        R, Z = "ST%d" % t, "ZI%d%d" % (t, c)
        PU, PK, FA, IA, OU = "PSU" + s, "PSK" + s, "FA" + s, "IA" + s, "OU" + s
        PD = ["PSD%d" % (2 * c), "PSD%d" % (2 * c + 1)]
        fa = lambda k: a(FA, CL * k, CL * k + CL)
        z2, pu = a3(Z), a(PU, 0, Q)
        mm(pu, [(a("WB"), a("CH", 0, Q)), (a("ONE", p=64), a("CT", p=64))], True, False)
        for k in range(2):
            mm(a(PU, CL * k, CL * k + CL), [(a("WB"), z2)], False, k == 1, pu)
        v = fa(1)
        ts(fa(0), a(PU, 0, CL), 51539607552.0, A.add, 51539607552.0, A.subtract)
        tt(v, a(PU, CL, Q), fa(0), A.subtract)
        act(fa(2), v, F.Square, 0.25, K4)
        ts(a3("IY" + s), fa(2), KQ, A.add)
        ts(a3("IY" + s), a3("IY" + s), 4095, A.bitwise_and)
        listing(c, "IY" + s, 0, None if t == 0 else APS if c == 0 else a("AC", 0, 1))
        if t and c == 0:
            ts(a("AC", 0, 1), APS, 0.0, A.add)
            ts(a("AC", 1, 2), APS, -0.25, A.add)
        for r in range(2):
            mm(a3(PD[1], 0, 8, p=16 * PA, p0=64 * r), [(a3(Z, r * PA, r * PA + PA), a("NH"))])
        act(a("ZT" + s), a3(PD[1], 0, 8), bias=C1024)
        mm(a(PK, 496, 496 + NA), [(a("WZ", 15 - b, 143 - b), a3(Z, 0, NA, b, b + 1)) for b in range(16)])
        uu, ba, k = il(12, c), il(24, c), il(36, c)
        ts(il(0, c), a(PK, 496, 496 + NA), CW, A.add)
        ts(uu, il(0, c), 4095, A.bitwise_and)
        ts(a(FA, 384, 384 + NA), uu, K15, A.add)
        tt(a(FA, 384, 384 + NA), a(FA, 384, 384 + NA), uu, A.mult)
        ts(ba, a(FA, 384, 384 + NA), 1.0 / 16, A.mult, -0.25 if t == 0 else a("AC", 1, 2), A.add)
        for i, lo in enumerate(pieces):
            xc, d = a("XC" + s, 16 * lo, 16 * (lo + PW)), a(PU, 0, 16 * PW) if i == 2 else a3(PD[i == 1], 0, PW)
            cp(xc, ind(XW if t == 0 else XE, a(OU, lo, lo + PW)))
            h, r = divmod(i, 2)
            mm(d, [(ID, xc), (a("ZT" + s, p=2 * PW, p0=64 * r), a("E", 384 * h, 384 * h + 384, p=2 * PW, p0=64 * r))])
            act(a3("AB" + s, lo // 8, (lo + PW) // 8), d, F.Abs, 4096.0)
        mm(a(PU, 384, 384 + CL), [(ID, a(R, RI + CL * c, RI + CL * c + CL))])
        tt(a(IA, 0, CL), a(PU, 384, 384 + CL), v, A.mult)
        ts(a3("IH" + s), a(IA, 0, CL), 4, A.logical_shift_right, 4095, A.bitwise_and)
        listing(c, "IH" + s, CL, K53)
        for h in range(2):
            sums(a(PK, 0, CL), sel, "AB" + s, h, h == 0, h == 1)
        scan(fa(2), a("DK", 0, CL), a(PK, 0, CL), A.add, A.min)
        scan(fa(0), a("DK", CL, Q), a(PK, 0, CL), A.add, A.min)
        tt(k, a(FA, 2 * CL + 15, 3 * CL, 16), a(FA, 15, CL, 16), A.subtract)
        tt(k, k, uu, A.mult)
        tt(k, k, ba, A.add)
        ts(il(48, c), k, 1023, A.bitwise_and)
        cp(ol(0, c), il(48, c))
        tt(a(IA, CL, Q), ind(DW, ol(0, c)), v, A.mult)
        ts(a3("IY" + s), a(IA, CL, Q), 4, A.logical_shift_right, 4095, A.bitwise_and)
        listing(c, "IY" + s, Q, K53)
        for lo, hi in YCUT:
            cp(a("Y" + s, 16 + 16 * lo, 16 + 16 * hi), ind(XE, a(OU, Q + lo, Q + hi)))
        for i, lo in enumerate(pieces):
            h, hs = a("H" + s, 16 * lo, 16 * (lo + PW)), ind(XE, a(OU, CL + lo, CL + lo + PW))
            if FUSE[t][c][i]:
                tt(h, hs, a("Y" + s, 16 + 16 * lo, 16 + 16 * (lo + PW)), A.subtract)
            else:
                cp(h, hs)
        ts(fa(3), z2, 0.5, A.mult, 1023.5, A.add)

    def middle(t, c):
        R = "ST%d" % t
        ts(il(60), il(36), 4095, A.bitwise_and)
        cp(ol(12), il(60))
        ts(a("XH"), ind(XW, ol(12)), 1.0, A.mult, C2047, A.add)
        ts(a("IL", 72, 120), ind(a("IL", 0, 12), a("OFU", 8, 11)), 1.0, A.mult)
        ts(a("IL", 72, 108), a("IL", 72, 108), 3, A.bitwise_and)
        ts(il(108), il(108), 15, A.bitwise_and)
        tt(a3("B", 2, 6), a("IL", 72, 120), a("CB"), A.add)
        cp(ol(24), a3("B", 5, 6))
        if t < NV - 1:
            ts(a("NB", 0, 12), a(R, NI, NI + 12), 32.0, A.mult)
        else:
            for c in range(NC):
                ts(a("NB", 48 + 32 * c, 48 + 32 * c + NA), a(R, NI + NA * c, NI + NA * c + NA), 32.0, A.mult)
        pn = a("PSU0", 0, Q)
        nn = a(R, NI, NI + 12)
        mm(pn, [(NID, a("KC"))], True, False)
        rec("p", [(lambda q, k=k: q.matmul(T.PSU0[:, k:Q:16], ID[0], nn[0], False, k == 15)) for k in range(16)], [ID, nn], [pn],
            16 * 64 * M["pcy"], grp=groups[None])
        act(a("BA", PEN, PEN + Q), pn, F.Relu)
        L = a(R, LI, LI + Q)
        tt(a("BA", DF, DF + Q), ind(DW, ol(0)), L, A.subtract)
        mm(a("PSU1", 0, Q), [(ID, a(R, RI, RI + Q)), (NID, L)])
        act(a("BA", DF + Q, DF + 2 * Q), a("PSU1", 0, Q))

    def second(t, c):
        s = str(c)
        R, PK, OU, Y = "ST%d" % t, "PSK" + s, "OU" + s, "Y" + s
        for i, lo in enumerate(pieces):
            d = "PSD%d" % (2 * c + i % 2)
            mm(a3(d, 0, PW), [(ID, a(Y, 16 + 16 * lo, 16 + 16 * (lo + PW))), (NID, a(Y, 15 + 16 * lo, 15 + 16 * (lo + PW)))])
            act(a3("AJ" + s, lo, lo + PW, 2, 16), a3(d, 0, PW, 2, 16), F.Abs, BIG)
            h = a("H" + s, 16 * lo, 16 * (lo + PW))
            if not FUSE[t][c][i]:
                d = a3("PSD%d" % (3 - 2 * c), 0, PW) if i % 2 else a("PSU" + s, 0, 16 * PW)
                mm(d, [(ID, a(Y, 16 + 16 * lo, 16 + 16 * (lo + PW))), (NID, h)])
                h = d
            act(a3("AM" + s, lo // 8, (lo + PW) // 8), h, F.Abs, BIG)
        ev, pj, pm = a(PK, EV - 1, EV - 1 + Q), a(PK, EV - 1, EV - 1 + Q, 2), a(PK, EV, EV + Q, 2)
        mm(ev, [(a("IDH"), a("CH", 288, 480))], True, False)
        for out, dg, pen in ((pj, "DGJ", PEN - 1 + CL * c), (pm, "DGM", PEN + CL * c)):
            mm(out, [(a(dg), a("CH", 192, 288)), (a("IDB"), a("BA", pen, pen + CL))], False, False, ev)
        for h in range(2):
            sums(pj, nsel, "AJ" + s, h, False, False, ev)
            sums(pm, sel, "AM" + s, h, False, h == 1, ev)
        scan(rev("SC", Q * c, Q * c + Q), rev(PK, EV, EV + Q), rev("OFF", 0, Q), A.min, A.max)
        oe = a(OU, 288, 288 + NA)
        ts(oe, a("SC", Q * c, Q * c + Q, 32), 0.5, A.mult)
        yw, zn = a(Y, 16), a("ZN%d%d" % (t, c))
        tt(zn, ind(yw, oe), a("FA" + s, 3 * CL, 4 * CL), A.add)
        if t < NV - 1:
            send(rec, zn, a3("ZI%d%d" % (t + 1, c)), 5 * t + c)
        else:
            ts(a(R, ZO + CL * c, ZO + CL * c + CL), zn, 0.5, A.mult, -1024.0, A.add)
        tt(a("X2" + s), ind(yw, oe), a("XH", CL * c, CL * c + CL), A.add)
        ts(a(R, XO + CL * c, XO + CL * c + CL), a("X2" + s), 0.5, A.mult, -1024.0, A.add)

    def third(t, c):
        R, both = "ST%d" % t, t < NV - 1
        w, lo, l0, ln = (12, 0, 0, Q) if both else (NA, NA * c, CL * c, CL)
        lanes = lambda n, k: a(n, k + l0, k + l0 + ln)
        for c in range(NC) if both else (c,):
            xw, x = a("X", 0, EXT * (c + 1)), a(R, XO + CL * c, XO + CL * c + CL)
            if c == 0 and not both:
                load("y", a("XO"), xw, 3500, None, [a(R, NI)], late=1)
                xw = a("XO")
            cp(ind(xw, ol(24, c)), x)
            if c == 0 and both:
                cp(ind(a("X", 4096), ol(24, c)), x)
            if not both:
                store(T.yx[:, EXT * c:EXT * c + EXT], a("X", EXT, 2 * EXT) if c else xw)
        sw, sc = a("SC", 2 * l0, 2 * (l0 + ln)), a("SC", 2 * l0, 2 * (l0 + ln), 32)
        rows = lambda n, r0, r1: a3(n, r0, r1, lo, lo + w)
        if both:
            tt(a("IL", 120, 168), ind(sw, a("OFU", 12, 15)), a("NB", 0, 48), A.add)
            tt(a("NF"), sc, il(132), A.is_equal)
            mm(APS, [(a("ONE"), a("NF", j, j + 1)) for j in range(12)])
        else:
            tt(a("IL", 120, 152), ind(sw, a("OFU", 28, 30)), a("NB", 48 + 32 * c, 80 + 32 * c), A.add)
        flags, e, o0 = a("IL", 168, 168 + 3 * w), a("IL", 204, 204 + w), 48 + 4 * lo
        ts(e, sc, 0.5, A.mult)
        ts(flags, a("IL", 120 + w, 120 + 4 * w), 1, A.bitwise_and)
        tt(rows("DE", 1, 2), e, rows("B", 4, 5), A.subtract)
        tt(a("IL", 120 + w, 120 + 4 * w), flags, rows("DE", 0, 3), A.mult)
        tt(a("FO", 0, 4 * w), a("IL", 120, 120 + 4 * w), rows("B", 0, 4), A.add)
        lst = lambda k: a("OL", o0 + k * w, o0 + k * w + w)
        cp(a("OL", o0, o0 + 4 * w), a("FO", 0, 4 * w))
        if l0:
            ts(lst(3), a("FO", 3 * w, 4 * w), -4.0 * l0, A.add)
        cp(a(R, NO + lo, NO + lo + w), a("FO", 2 * w, 3 * w))
        m1, m2, pl = lanes("BA", M1), lanes("BA", M2), a("PSK%d" % c, 304, 304 + ln)
        tt(m1, ind(a("TAB", 0, 512), lst(0)), lanes("BA", DF), A.mult)
        tt(m2, ind(a("TAB", 512, 1024), lst(0)), lanes("BA", DF + Q), A.mult)
        mm(pl, [(ID, lanes(R, LI)), (ID, m1), (ID, m2)])
        act(lanes(R, LO), pl)
        for k in range(0, w, NA):
            cp(a(R, RO + l0 + 16 * k, RO + l0 + 16 * k + CL), ind(a(R, LO, RI + Q), a("OL", o0 + w + k, o0 + w + k + NA)))
        cp(ind(a("DL", 4 * l0), lst(3)), lanes(R, LO))
        if both:
            j = []
            for k, (c0, c1) in enumerate(((NO, RO + CL), (RO + CL, NI))):
                j = [send(rec, a(R, c0, c1), a("ST%d" % (t + 1), c0 + NI - NO, c1 + NI - NO), 5 * t + 2 + k, j)]
            return
        for out, k in ((T.yz, ZO), (T.yl, LO), (T.yr, RO)):
            store(out[:, l0:l0 + ln], lanes(R, k))
        store(T.yd[:, 4 * l0:4 * (l0 + ln)], a("DL", 4 * l0, 4 * (l0 + ln)))
        if c:
            nn = a(R, NO, NO + 12)
            fns = [(lambda q, b=b: q.matmul(T.PSU1[0:8, b:Q:16], T.ID[:, b:128:16], nn[0], True, True)) for b in range(16)]
            rec("p", fns, [ID, nn], [a("PSU1", 0, Q)], 16 * 64 * M["pcy"], each=1, grp=-1)
            act(a("YN", p=8), a("PSU1", 0, Q, p=8))
            store(T.yn[:], a("YN", p=8))

    for t in range(NV):
        ends = ((second, 1, 12, 5), (third, 0, 17, 3)) if t < NV - 1 else ((third, 0, 13, 3), (second, 1, 12, 5), (third, 1, 17, 3))
        for f, c, at, span in ((first, 0, -3, 11), (first, 1, 1, 11), (middle, 0, 8, 2), (second, 0, 8, 5)) + ends:
            k = len(ops)
            f(t, c)
            for j in range(k, len(ops)):
                ops[j]["key"] = 1000.0 * (18 * t + at + span * (j - k) / (len(ops) - k))
    writer = lambda n, lo: [i for i, o in enumerate(ops) if "key" in o and o["w"] and o["w"][0][:2] == (n, lo)]
    for t in range(NV - 1):
        for lo in list(pieces)[HINT[0]:]:
            ops[writer("H1", 16 * lo)[t]]["behind"] = writer("ZN%d0" % t, 0)
        if HINT[1]:
            ops[writer("OU1", 0)[t + 1]]["behind"] = [writer("BA", M1)[t], writer("BA", M2)[t]]
        if HINT[2] and t == 0:
            ops[writer("FA0", 0)[2]]["behind"] = [writer("BA", M1)[t], writer("BA", M2)[t]]
            ops[writer("FA0", 2 * CL)[2]]["behind"] = writer("ST%d" % t, LO)
    return ops


def depend(ops):
    acc = {}
    deps = []
    for i, o in enumerate(ops):
        d = set(o.get("after", ()))
        for kind, lst in ((0, o["r"]), (1, o["w"])):
            for n, lo, hi in lst:
                for j, k2, l2, h2 in acc.get(n, ()):
                    if j == i:
                        continue
                    if (kind or k2) and lo < h2 and l2 < hi:
                        d.add(j)
                    elif n.startswith("PS") and (ops[j]["e"] != o["e"] or o["e"] == "p"):
                        d.add(j)
        for kind, lst in ((0, o["r"]), (1, o["w"])):
            for n, lo, hi in lst:
                acc.setdefault(n, []).append((i, kind, lo, hi))
        deps.append(d)
    done, issued = [], []
    for i, d in enumerate(deps):
        m, q, keep = 0, 0, set()
        for j in sorted(d, reverse=True):
            soft = ops[i]["e"] == "p" == ops[j]["e"]
            if not (m | q if soft else m) >> j & 1:
                keep.add(j)
                m |= done[j] & ~(1 << j) if soft and ops[i]["grp"] != ops[j]["grp"] else done[j]
                q |= issued[j] if soft else 0
        done.append(1 << i if ops[i]["e"] == "net" else m | 1 << i)
        issued.append(q | 1 << i)
        deps[i] = keep
    for i, o in enumerate(ops):
        deps[i] |= set(o.get("behind", ()))
    return deps


def queued(ops, i, j):
    return ops[i]["e"] == "p" == ops[j]["e"] or j in ops[i].get("behind", ())


def place(ops, before, seq, hop, back, choose=None, bias=0.0):
    busy = {}
    end = [0.0] * len(ops)
    st = [0.0] * len(ops)
    for i in seq:
        o = ops[i]
        c, lat = o["cost"], o.get("lat", 0)
        t = 0.0
        e = o["e"]
        for j in before[i]:
            x = end[j] if queued(ops, i, j) or queued(ops, j, i) else end[j] + hop
            if x > t:
                t = x
        if back:
            t += lat
        if e != "net":
            found = []
            for e2 in o["alt"] if choose and "alt" in o else (e,):
                iv, t2 = busy.setdefault(e2, []), t
                c2 = o["alt"][e2][1] if "alt" in o else c
                lo, hi = 0, len(iv)
                while lo < hi:
                    mid = (lo + hi) // 2
                    if iv[mid][1] <= t2:
                        lo = mid + 1
                    else:
                        hi = mid
                while lo < len(iv) and iv[lo][0] < t2 + c2:
                    t2 = max(t2, iv[lo][1])
                    lo += 1
                found.append((t2 + c2 + (bias * c2 if e2 == "v" else 0), e2, t2, c2, lo))
            x, e2, t, c, lo = min(found)
            if e2 != e:
                choose(i, e2)
            busy[e2].insert(lo, (t, t + c))
        st[i] = t
        end[i] = t + c + (0 if back else lat)
    return st, end


def in_order(before, users, key):
    left = [len(b) for b in before]
    ready = sorted(((key[i], i) for i in range(len(before)) if not left[i]), reverse=True)
    seq = []
    while ready:
        i = ready.pop()[1]
        seq.append(i)
        new = False
        for k in users[i]:
            left[k] -= 1
            if not left[k]:
                ready.append((key[k], k))
                new = True
        if new:
            ready.sort(reverse=True)
    return seq


def put(ops, i, e):
    ops[i]["e"] = e
    ops[i]["fns"], ops[i]["cost"] = ops[i]["alt"][e]


def plan(all_ops, deps, rounds, seed):
    ops, hop = all_ops[0]
    n = len(ops)
    users = [[] for _ in ops]
    for i in range(n):
        for j in deps[i]:
            users[j].append(i)
    flex = [i for i in range(n) if "alt" in ops[i]]
    x = [seed]

    def rnd():
        x[0] = (x[0] * 1103515245 + 12345) % 2147483648
        return x[0] / 2147483648.0

    def choose(i, e):
        put(ops, i, e)

    def forward(key, bias):
        key = [key[i] - (1e5 if lists[i] else 0) if "key" in ops[i] else -1e6 + i if early[i] else 6000.0 + i for i in range(n)]
        return place(ops, deps, in_order(deps, users, key), hop, False, choose, bias)

    early = ["key" not in o and (bool(o.get("dma")) or o["e"] == "g") or bool(o["w"]) and o["w"][0][0] in ("AB0", "AB1") and o["key"] < 12000 for o in ops]
    for i in range(n - 1, -1, -1):
        if early[i]:
            for j in deps[i]:
                early[j] = True
    lists = [early[i] and not any(x[0][:2] in ("XC", "AB") for x in o["r"] + o["w"]) for i, o in enumerate(ops)]
    starts = []
    for _ in range(STARTS[0]):
        cur, cs, best = [o.get("key", 0.0) for o in ops], 1e18, (1e18,)
        for r in range(rounds):
            a, bias = rnd() * max(cur), 2.0 * rnd()
            w, amp = 2000 + 5000 * rnd(), 500 + 5000 * rnd() ** 2
            st, end = forward([k + amp * (rnd() - 0.5) if a <= k <= a + w else k for k in cur], bias)
            bs, be = place(ops, users, in_order(users, deps, [-e for e in end]), hop, True)
            st, end = forward([-e for e in be], bias)
            s = max(end)
            if s <= cs + 100:
                cur, cs = st, s
            if s < best[0]:
                best = (s, st, [ops[i]["e"] for i in flex])
        for i, e in zip(flex, best[2]):
            put(ops, i, e)
        starts.append(refine(all_ops, deps, users, in_order(deps, users, best[1]), STARTS[1], rnd))
    best = min(starts, key=lambda x: x[4])
    for i in flex:
        put(ops, i, best[2][i])
    return refine(all_ops, deps, users, best[1], ROUNDS[2], rnd)


def dispatch(ops, hop, deps, users, tail, look, idle):
    n = len(ops)
    left, rel, fin = [len(d) for d in deps], [0.0] * n, [0.0] * n
    can = [list(o["alt"]) if "alt" in o else [o["e"]] for o in ops]
    free, ready, order, eng, de = {e: 0.0 for e in "vspgy"}, {e: [] for e in "vspgy"}, [], {}, [0.0]

    def issue(i, e, t):
        o = ops[i]
        f = t + (o["alt"][e][1] if "alt" in o else o["cost"])
        if e != "net":
            free[e] = f
            for e2 in can[i]:
                ready[e2].remove(i)
        if "dq" in o:
            de[0] = f = max(f + o["dq"][0], de[0]) + o["dq"][1]
        order.append(i)
        eng[i] = e
        for j in users[i]:
            rel[j] = max(rel[j], f if ops[j]["e"] == "net" or e == "p" == ops[j]["e"] else f + hop)
            left[j] -= 1
            if not left[j]:
                if ops[j]["e"] == "net":
                    issue(j, "net", rel[j])
                else:
                    for e2 in can[j]:
                        ready[e2].append(j)
        fin[i] = f

    for i in range(n):
        if not left[i]:
            for e in can[i]:
                ready[e].append(i)
    while len(order) < n:
        t, e = min((max(free[e], min(rel[i] for i in ready[e])), e) for e in ready if ready[e])
        near = sorted((i for i in ready[e] if rel[i] <= t + look), key=lambda i: -tail[i])[:6]
        best = None
        for i in near:
            s = max(t, rel[i])
            f = s + (ops[i]["alt"][e][1] if "alt" in ops[i] else ops[i]["cost"])
            worst = max([s + tail[i]] + [max(f, rel[j]) + tail[j] for j in near if j != i and len(can[j]) == 1])
            worst += idle * (s - t) - 1e-3 * tail[i]
            if best is None or worst < best[0]:
                best = (worst, i, s)
        issue(best[1], e, best[2])
    return max(fin), order, eng


def plan2(all_ops, deps, rounds, seed):
    n = len(deps)
    users = [[] for _ in deps]
    for i in range(n):
        for j in deps[i]:
            users[j].append(i)
    x = [seed]

    def rnd():
        x[0] = (x[0] * 1103515245 + 12345) % 2147483648
        return x[0] / 2147483648.0

    def tails(ops, hop, order=None, eng=None):
        tail, nxt = [0.0] * n, {}
        for i in reversed(order or range(n)):
            o = ops[i]
            e = eng[i] if eng else o["e"]
            t = max([0.0] + [tail[j] + (0 if ops[j]["e"] == "net" or e == "p" == ops[j]["e"] else hop) for j in users[i]]) + sum(o.get("dq", ()))
            if order and e != "net":
                t = max(t, nxt.get(e, 0.0) - SLACK[0])
            tail[i] = nxt[e] = t + (o["alt"][e][1] if "alt" in o else o["cost"])
        return [t + (1e6 - i if ops[i].get("dma") and not ops[i].get("late") else 0) for i, t in enumerate(tail)]

    found = []
    for s in range(STARTS[0]):
        ops, hop = all_ops[0 if s % 2 else 2]
        base = tails(ops, hop)
        cur, cs, best = base, 1e18, (1e18,)
        for r in range(rounds):
            amp, mix = 600 * rnd(), rnd()
            tail = [mix * a + (1 - mix) * b + amp * rnd() for a, b in zip(base, cur)]
            got = dispatch(ops, hop, deps, users, tail, 300 + 500 * rnd(), 2 * rnd())
            if got[0] <= cs + 500:
                cur, cs = tails(ops, hop, got[1], got[2]), got[0]
            if got[0] < best[0]:
                best = got
        for i in range(n):
            if "alt" in ops[i]:
                put(all_ops[0][0], i, best[2][i])
        found.append(refine(all_ops, deps, users, best[1], STARTS[1], rnd))
    best = min(found, key=lambda x: x[4])
    for i in best[2]:
        put(all_ops[0][0], i, best[2][i])
    return refine(all_ops, deps, users, best[1], ROUNDS[2], rnd)


SLACK = [0.0]


def refine(all_ops, deps, users, order, rounds, rnd):
    ops = all_ops[0][0]
    n = len(ops)
    QN = {"v": 0, "s": 1, "p": 2, "g": 3, "y": 4, "net": 5}
    eng = [QN[o["e"]] for o in ops]
    flex = [sum(QN[e] for e in o["alt"]) if "alt" in o else 0 for o in ops]
    fixed = [bool(o.get("dma")) and not o.get("late") for o in ops]
    ms = []
    for (mo, hop), weight in zip(all_ops, WEIGHTS):
        gap = lambda i, j: 0.0 if ops[i]["e"] == "net" or queued(ops, i, j) else hop
        cost = [{QN[e]: o["alt"][e][1] for e in o["alt"]} if "alt" in o else [o["cost"]] * 6 for o in mo]
        ms.append(([[(j, gap(i, j)) for j in deps[i]] for i in range(n)], cost, [o.get("dq") for o in mo],
                   [[(j, gap(j, i)) for j in users[i]] for i in range(n)], weight))

    def trace(m, order, old=None, a=0, b=n - 1):
        dl, cost, dq, ul, weight = m
        if old:
            fin, st, marks, tail, rest, why = old[1], old[2], old[3][:a], old[5], old[6][:b:-1], old[8]
            free, de, last, dlast = old[3][a]
            nxt, dn = old[6][b]
            free, last, nxt = free[:], last[:], nxt[:]
        else:
            free, fin, de = [0.0] * 6, [0.0] * n, 0.0
            st, why, last, dlast, marks = [0.0] * n, [None] * n, [None] * 6, None, []
            tail, nxt, dn, rest = [0.0] * n, [0.0] * 6, 0.0, []
        for i in order[a:]:
            marks.append((free[:], de, last[:], dlast))
            e = eng[i]
            t = free[e]
            w = -1
            for j, h in dl[i]:
                x = fin[j] + h
                if x > t:
                    t = x
                    w = j
            f = t + cost[i][e]
            if e < 5:
                free[e] = f
            st[i], why[i] = t, (w, last[e])
            last[e] = i
            q = dq[i]
            if q:
                f += q[0]
                if de > f:
                    f = de
                    why[i] = (dlast, None)
                de = f = f + q[1]
                dlast = i
            fin[i] = f
        for i in order[b::-1]:
            rest.append((nxt[:], dn))
            e = eng[i]
            t = 0.0
            for j, h in ul[i]:
                x = tail[j] + h
                if x > t:
                    t = x
            q = dq[i]
            if q:
                dn = q[1] + (t if t > dn else dn)
                t = q[0] + dn
            if nxt[e] > t:
                t = nxt[e]
            tail[i] = t = t + cost[i][e]
            if e < 5:
                nxt[e] = t
        rest.reverse()
        end = max(fin)
        i, out = fin.index(end), []
        while i is not None:
            w, prev = why[i]
            if w == -1 and prev is not None or flex[i]:
                out.append((i, prev if w == -1 else None))
            i = prev if w == -1 else w
        near = [(fin[i] + h + tail[j], i, j) for i in order if st[i] + tail[i] > end - 800 for j, h in ul[i] if fin[i] + h + tail[j] > end - 800]
        near.sort(reverse=True)
        return end, fin, st, marks, out, tail, rest, near, why

    def run(m, tr, mid, a, b, pos):
        dl, cost, dq, ul, weight = m
        free, de = tr[3][a][:2]
        free, old, tail, fin, end = free[:], tr[1], tr[5], {}, 0.0
        by = 0.0
        for x, i, j in tr[7]:
            if pos[i] < a and pos[j] > b:
                by = x
                break
        for i in mid:
            e = eng[i]
            t = free[e]
            for j, h in dl[i]:
                x = (fin[j] if j in fin else old[j]) + h
                if x > t:
                    t = x
            f = t + cost[i][e]
            if e < 5:
                free[e] = f
            q = dq[i]
            if q:
                f += q[0]
                if de > f:
                    f = de
                de = f = f + q[1]
            fin[i] = f
            if f > end:
                end = f
            for j, h in ul[i]:
                if pos[j] > b:
                    x = f + h + tail[j]
                    if x > end:
                        end = x
        nxt, dn = tr[6][b]
        for e in range(5):
            if free[e] + nxt[e] > end:
                end = free[e] + nxt[e]
        end = max(end, de + dn)
        return weight * (max(end, by) + 0.1 * (end - tr[0]))

    def move(order, a, b, ahead):
        mark = {order[b if ahead else a]}
        for k in range(b - 1, a - 1, -1) if ahead else range(a + 1, b + 1):
            i = order[k]
            for x in users[i] if ahead else deps[i]:
                if x in mark:
                    if k == (a if ahead else b):
                        return None
                    mark.add(i)
                    break
        mid = order[a:b + 1]
        return [i for i in mid if (i in mark) == ahead] + [i for i in mid if (i in mark) != ahead]

    def take(order, tidy, a=None, b=None):
        if not tidy and a is not None:
            for k in range(a, b + 1):
                pos[order[k]] = k
            new = [trace(m, order, t, a, b) for m, t in zip(ms, trs)]
            return order, pos, new, sum(m[4] * t[0] for m, t in zip(ms, new))
        return take_all(order, tidy)

    def take_all(order, tidy):
        if tidy:
            st = trace(ms[0], order)[2]
            pos = {i: k for k, i in enumerate(order)}
            order = sorted(order, key=lambda i: (st[i], pos[i]))
        trs = [trace(m, order) for m in ms]
        pos = [0] * n
        for k, i in enumerate(order):
            pos[i] = k
        return order, pos, trs, sum(m[4] * t[0] for m, t in zip(ms, trs))

    order, pos, trs, cs = take(order, True)
    best = (cs, order, list(eng), [t[0] for t in trs])
    rests, since = [0] * n, 0
    for k in range(1, rounds):
        pick, floor = None, cs - 400.0 * sum(WEIGHTS)
        for _ in range(TRIES):
            ch = trs[int(rnd() * len(ms))][4]
            v, u = ch[int(rnd() * len(ch))]
            x, fl = rnd(), None
            if x < 0.2 or u is None:
                who = fl = v if flex[v] else u if flex[u] else None
                if fl is None:
                    continue
                a = b = pos[fl]
                mid = [fl]
                eng[fl] = flex[fl] - eng[fl]
            elif fixed[u] or fixed[v]:
                continue
            else:
                a, b = pos[u], pos[v]
                who = v if x < 0.6 else u
                for _ in range(int(rnd() ** 3 * 12)):
                    p, d = (a - 1, -1) if x < 0.6 else (b + 1, 1)
                    while 0 <= p < n and eng[order[p]] != eng[v]:
                        p += d
                    if 0 <= p < n and not fixed[order[p]]:
                        a, b = (p, b) if x < 0.6 else (a, p)
                mid = move(order, a, b, x < 0.6)
                if mid is None:
                    continue
            s = NOISE * rnd() + floor
            for m, t in zip(ms, trs):
                s += run(m, t, mid, a, b, pos) - m[4] * (t[0] - 400.0)
                if pick and s > pick[0]:
                    break
            if fl is not None:
                eng[fl] = flex[fl] - eng[fl]
            if (rests[who] < k or s < best[0]) and (pick is None or s < pick[0]):
                pick = (s, who, fl, a, b, mid)
        if pick is None:
            continue
        s, who, fl, a, b, mid = pick
        if fl is not None:
            eng[fl] = flex[fl] - eng[fl]
        rests[who] = k + REST + int(REST * rnd())
        order, pos, trs, cs = take(order[:a] + mid + order[b + 1:], not k & 15, a, b)
        since += 1
        if cs < best[0]:
            best, since = (cs, order, list(eng), [t[0] for t in trs]), 0
        elif since > BACK:
            eng[:] = best[2]
            order, pos, trs, cs = take(best[1], False)
            since = 0
    return deps, best[1], {i: "vspg"[best[2][i]] for i in range(n) if flex[i]}, best[3], best[0]


def rank_program(g, core, T, topo):
    rank = T.rank_of(core)
    if rank is None:
        return
    n = len(T.cores)
    dst, src = T.cores[(rank + SHIFT) % n], T.cores[(rank - SHIFT) % n]
    rid, pid = topo.addr(dst)[:2]
    n_out = n_in = min(len(topo.engines(c, T.cores[(r + SHIFT) % n])) for r, c in enumerate(T.cores))
    mask = sum(1 << e for e in topo.engines(core, dst)[:n_out])
    sent = [0]

    def send(rec, i, out, k, behind=()):
        sent[0] += n_out
        j = rec("g", [lambda q: q.remote_dma(out[0], i[0], T.sem["ar%d" % k], T.sem.sent, pid, rid, mask)], [i], [], 300 if k else M["r1"],
                behind=behind)
        rec("net", [], [], [out], 0, lat=M["rl"] + 128 * 2 * i[2] / M["rb"], after=[j], sem=("ar%d" % k, n_in),
            dq=(M["rl"], 128 * 2 * i[2] / M["rb"]))
        return j

    ops = build(g, T, send)
    if not _PLAN:
        all_ops, mine = [], sent[0]
        for m in MODELS:
            M.update(m)
            all_ops.append((build(g, T, send), m["hop"]))
        sent[0] = mine
        _PLAN["p"] = plan(all_ops, depend(ops), ROUNDS[0], ROUNDS[1])
    deps, order, eng = _PLAN["p"][:3]
    for i in eng:
        put(ops, i, eng[i])
    QU = {"v": g.vector, "s": g.scalar, "p": g.tensor, "g": g, "y": g.sync}
    pos = {i: k for k, i in enumerate(order)}
    need = set()
    for final in (False, True):
        known = {e: 0 for e in QU}
        clos, sig, last, cnt, val, waited, group = {}, {}, {}, {e: 0 for e in QU}, {}, {}, {}
        stores = 0
        for i in order:
            o = ops[i]
            e = o["e"]
            if e == "net":
                clos[i], sig[i] = 1 << i, o["sem"]
                val[o["sem"][0]] = o["sem"][1]
                continue
            want = sorted((j for j in deps[i] if not queued(ops, i, j)), key=lambda j: -pos[j])
            if "sem" in o:
                sig[i] = o["sem"]
            elif final and i in need:
                s = e + str(cnt[e] % NSEM[e])
                cnt[e] += 1
                if s in last:
                    want.append(last[s])
                last[s] = i
                sig[i] = (s, val.get(s, 0) + (len(o["fns"]) if o.get("each") else 1))
            for j in want:
                if not known[e] >> j & 1:
                    need.add(j)
                    known[e] |= clos[j]
                    if final:
                        QU[e].wait_ge(T.sem[sig[j][0]], sig[j][1])
                        waited[sig[j][0]] = max(waited.get(sig[j][0], 0), sig[j][1])
            clos[i] = known[e] | 1 << i
            if e == "p":
                group[o["grp"]] = group.get(o["grp"], 0) | 1 << i
                clos[i] |= group[o["grp"]]
            if i in sig:
                val[sig[i][0]] = sig[i][1]
            if final:
                for k, f in enumerate(o["fns"]):
                    ins = f(QU[e])
                    if o.get("store"):
                        ins.then_inc(T.sem.st, 16)
                        stores += 16
                    elif i in sig and (o.get("each") or k == len(o["fns"]) - 1):
                        ins.then_inc(T.sem[sig[i][0]], 16 if o.get("dma") else 1)
    for s in val:
        if waited.get(s, 0) < val[s]:
            g.wait_ge(T.sem[s], val[s])
    g.wait_ge(T.sem.sent, sent[0])
    g.sync.wait_ge(T.sem.st, stores)
